import numpy as np, ml_dtypes
CORES = [9,25,41,57]
N = 4
import mx_ref
BF = ml_dtypes.bfloat16
def gentries(a):
    return np.ascontiguousarray(a.reshape(8, 16, -1).transpose(0, 2, 1)).reshape(8, -1)
def gtable(e):
    e = np.asarray(e); return np.ascontiguousarray(e.reshape(8, -1, 16).transpose(0, 2, 1)).reshape(128, -1).astype(np.int32)
def gcols(t, e):
    v = np.concatenate([t.reshape(8, 16, -1, 4), np.zeros((8, 16, 1, 4), BF)], axis=2)
    return np.ascontiguousarray(np.stack([v[g][:, e[g]] for g in range(8)])).reshape(128, -1)
def gpick(z, e):
    return np.concatenate([z[16 * g:16 * g + 16][:, e[g]] for g in range(8)])
def tile(rs):
    return np.stack(rs, axis=2).reshape(128, -1).astype(BF)
def pick(q, e):
    c = np.concatenate([q[0].reshape(128, -1, 4), np.zeros((128, 1, 4), np.uint8)], axis=1); s = np.concatenate([q[1], np.ones((16, 1), np.uint8)], axis=1)
    return (np.ascontiguousarray(c[:, e].reshape(128, -1)), np.ascontiguousarray(s[:, e]))
def join(*qs):
    return (np.concatenate([q[0] for q in qs], axis=1), np.concatenate([q[1] for q in qs], axis=1))
def put(q, e, v):
    c, s = q[0].reshape(128, -1, 4).copy(), q[1].copy(); c[:, e] = v[0].reshape(128, -1, 4); s[:, e] = v[1]
    return (c.reshape(128, -1), s)
def pk(c, s):
    return (np.ascontiguousarray(c), mx_ref.live(s))
def emit(q):
    return q[0], q[1]
def packed(v, rng):
    q = [mx_ref.quantize(np.ascontiguousarray(v[r])) for r in range(N)]
    return np.stack([a for a, b in q]), np.stack([mx_ref.plane(b, rng) for a, b in q])
def values_of_codes():
    e, c = np.zeros((128, 128, 4), np.float32), np.zeros((128, 2, 4), np.uint8)
    e[np.arange(128), np.arange(128), 0] = 1
    c[:127, :, 0] = np.arange(256).reshape(2, 128).T[:127]
    return mx_ref.matmul(mx_ref.quantize(e.reshape(128, 512).astype(BF)), (c.reshape(128, 8), np.full((16, 2), 127, np.uint8))).T.reshape(-1).astype(np.float64)
CODE_VALUE, SCALE_VALUE = values_of_codes(), 2.0 ** (np.arange(256) - 127.0)
def decode(q):
    return (CODE_VALUE[q[0]].reshape(16, 8, -1, 4) * SCALE_VALUE[q[1]][:, None, :, None] + 0.0).reshape(128, -1).astype(np.float32)
def f(rng, *shape):
    return mx_ref.flush((rng.standard_normal(shape, dtype=np.float32) * np.exp2(rng.integers(-2, 3, shape[:-1] + (1,)))).astype(BF))
def wide(rng, *shape, cols=0):
    v = rng.standard_normal(shape, dtype=np.float32) * np.exp2(rng.integers(-12, 13, shape)).astype(np.float32)
    if cols: v *= np.repeat(np.exp2(rng.integers(-cols, cols + 1, shape[:-2] + (1, shape[-1] // 4))) * (rng.random(shape[:-2] + (1, shape[-1] // 4)) > 0.0625), 4, axis=-1).astype(np.float32)
    return mx_ref.flush(v.astype(BF))
C = 384
STEP = [1, 2, 3]
GROUP, PLACE = np.arange(8)[:, None], np.arange(C)
def numbers_of(rng):
    return {"x": np.array(f(rng, N, 128, 4 * C)), "u": np.array(f(rng, N, 128, 512)), "v": np.array(f(rng, N, 128, 512))}
def orders(rng):
    return rng.permuted(np.tile(np.arange(C), (N, 8, 1)), axis=2)
def paired(e):
    k = np.zeros_like(e)
    np.put_along_axis(k, e[:, :, 0::2], e[:, :, 1::2], 2)
    np.put_along_axis(k, e[:, :, 1::2], e[:, :, 0::2], 2)
    return k
def stored(p, q, mu):
    return {a: np.stack([gtable(k[r]) for r in range(N)]) for a, k in (("pl", p), ("ql", q), ("ml", mu))}
def lists(rng):
    return stored(paired(orders(rng)), paired(orders(rng)), paired(orders(rng)))
def layers(rng, still=[]):
    w = np.array(f(rng, N, 128, 2048)).reshape(N, 8, 16, 4, 8, 16, 4)
    for i in still:
        w[:, :, i] = 0
        w[:, :, :, :, :, i] = 0
    return w
def weights(rng, w):
    c, s = packed(np.ascontiguousarray(w).reshape(N, 128, 2048), rng)
    return {"wc": c, "ws": s}
def setup_inputs(rng):
    return {**numbers_of(rng), **lists(rng), **weights(rng, layers(rng))}
def setup_inputs_ties(rng):
    d = numbers_of(rng)
    e = orders(rng)
    mu = paired(orders(rng))
    k = np.zeros((N, 8, C))
    for r in range(N):
        h = rng.permutation(8)
        c = rng.integers(0, C, 2)
        k[r, h[1], min(c[0], mu[r, h[1], c[0]])] = -1
        k[r, h[2], max(c[1], mu[r, h[2], c[1]])] = -1
        k[r, h[3], e[r, h[3], :2]] = -1
        k[r, h[4]] = rng.integers(-4, 0, C)
        k[r, h[5]] = rng.integers(-1, 3, C)
        k[r, h[6]] = rng.integers(1, 4, C)
        k[r, h[7]] = rng.integers(0, 2, C)
        k[r, h[7], e[r, h[7], 0]] = -1
        k[r, h[7], e[r, h[7], 2 * rng.integers(1, C // 2)]] = -1
    x = d["x"].reshape(N, 8, 16, C, 4)
    x[:, :, 0] = 0
    x[:, :, 0, :, 0] = k.astype(np.float32).astype(BF)
    u = d["u"].reshape(N, 128, 128, 4)
    u[:, :, ::16] = 0
    for h in range(0, 128, 16): u[:, h, h, 0] = 1
    return {"x": x.reshape(N, 128, 4 * C), "u": u.reshape(N, 128, 512), "v": d["v"], **stored(paired(e), paired(np.roll(e, -1, axis=2)), mu), **weights(rng, layers(rng, [0]))}
def setup_inputs_near(rng):
    d = numbers_of(rng)
    x = d["x"].astype(np.float32).reshape(N, 8, 16, C, 4)
    x[:, :, :2] = 0
    x[:, :, 8:] = 0
    x[:, :, 1, :, 0] = rng.choice([-1.0, 1.0], (N, 8, C)) * (1.0 + 0.125 * rng.integers(0, 8, (N, 8, C))) * 2.0 ** -7
    u = d["u"].reshape(N, 128, 128, 4)
    u[:, :, ::16] = 0
    w = layers(rng, [0, 1, 8, 9, 10, 11, 12, 13, 14, 15])
    o = rng.permutation(N) % 4
    for r in range(N):
        c = rng.choice([-1.0, 1.0], (8, 1))
        s = rng.integers(0, 16, (8, C))
        digits = ((s[:, :, None] >> np.arange(4)) & 1) * np.exp2(np.arange(4) - 23.0)
        if o[r] < 2:
            x[r, :, 0, :, 0] = c
            x[r, :, 8] = digits
            x[r, :, 11, :, 0] = 2.0 ** -10
        elif o[r] == 2: x[r, :, 8] = digits * rng.choice([-1.0, 1.0], (8, C, 1))
        else:
            x[r, :, 8, :, 0] = np.where(s < 8, 1.25, 0.0) * 2.0 ** -29 * c
            x[r, :, 9, :, 0] = np.where(s < 8, 0.0, 1.125) * 2.0 ** -29 * c
            x[r, :, 12, :, 0] = 2.0 ** -28
            for g in range(8): w[r, g, 1, 0, g, 10, 0] = 2.0 ** -30
            for i, g in enumerate(rng.permutation(8)[:4]):
                if i < 2:
                    e = rng.choice([-1.0, 1.0], C) * 2.0 ** -29
                    x[r, g, 8, :, 0] = 1.25 * e
                    x[r, g, 9, :, 0] = -1.125 * e
                else:
                    x[r, g, 8:] = 0
                    x[r, g, 12, :, 0] = 2.0 ** -30
                    w[r, g, 1, 0, g, 10, 0] = -2.0 ** -30
                    w[r, g, 1, 0, g, 11, 0] = 2.0 ** -30
        at = [0, C - 1, int(rng.integers(C)), int(rng.integers(C))]
        for g, j in zip(rng.permutation(8)[:4], at): x[r, g, 0, j, 0] = 2.0 ** 29 * rng.choice([-1.0, 1.0])
        k = 1.0 if o[r] == 0 else 2.0 ** -30
        for h in range(0, 128, 16):
            u[r, h, h, 0] = k if o[r] < 2 else 1.0
            if o[r] < 2: u[r, h + 11, h, 0] = k
            if o[r] < 3: u[r, h + 8, h] = k
            else:
                u[r, h + 8, h, 0] = k
                u[r, h + 9, h, 0] = 1.125 * k
                u[r, h + 10, h, 0] = k
                u[r, h + 11, h, 0] = 1.125 * k
    return {"x": x.reshape(N, 128, 4 * C).astype(BF), "u": u.reshape(N, 128, 512), "v": d["v"], **lists(rng), **weights(rng, w)}
def setup_inputs_odd(rng):
    d = numbers_of(rng)
    x = (1.0 + (2 * rng.integers(0, 64, (N, 16, 8, C, 4)) + 1) * 2.0 ** -7) * np.exp2(-rng.integers(0, 7, (N, 16, 8, C, 4)).astype(np.float64)) * rng.choice([-1.0, 1.0], (N, 16, 8, C, 4))
    x[:, :, 0, :, 0] = 1.96875 * 2.0 ** 8 * rng.choice([-1.0, 1.0], (N, 16, C))
    x[:, 1::2, 0, :, 0] *= np.where(rng.random((N, 8, C)) < 0.5, 2.0 ** -6, 1.0)
    u = d["u"].reshape(N, 16, 8, 128, 4)
    u[:, :, 0, ::16] = 0
    for r in range(N):
        for i, g in enumerate(rng.permutation(8)[:4]):
            x[r, 2 * g, 1, :, 0] = (8 + rng.integers(0, 2, C)) * 2.0 ** (i - 8)
            u[r, :, :, 16 * g] = 0
            u[r, 2 * g, 1, 16 * g, 0] = 1.0
    return {"x": x.astype(np.float32).reshape(N, 128, 4 * C).astype(BF), "u": u.reshape(N, 128, 512), "v": d["v"], **lists(rng), **weights(rng, layers(rng, [0, 8]))}
def setup_inputs_ends(rng):
    d = numbers_of(rng)
    o, e = rng.permutation(N) % 2, rng.permutation(N) % 4
    sign = rng.choice([-1.0, 1.0], (128, 1, 4))
    half = np.repeat(rng.choice([0.5, 1.0], (N, 1, C, 2)), 2, axis=3)
    small = sign * (1.0 + 0.125 * rng.integers(0, 8, (N, 128, C, 4))) * 2.0 ** -30
    x = sign * half * (14 + rng.integers(0, 3, (N, 128, C, 4))) * 2.0 ** 26
    x[o == 1] = small[o == 1]
    x[:, 112:120] = sign[112:120]
    x[:, 120:] = small[:, 120:]
    size = np.where(o == 0, 2.0 ** 30, 2.0 ** -30)
    kinds = np.array([[1, 1, 1, 1]] * 2 + [[-1, -1, -1, -1]] * 3 + [[1, 1, -1, -1]] * 2 + [[0, 0, 0, 0]])
    u = d["u"].astype(np.float32).reshape(N, 128, 128, 4)
    for r in range(N): u[r, :, ::16] = sign * kinds[rng.permutation(8)][None] * size[r]
    u[:, 112:, ::16] = 0
    v = rng.choice([-1.0, 1.0], (N, 128, 512)) * size[:, None, None]
    a = orders(rng)
    p, q, mu = paired(a), paired(np.roll(a, -1, axis=2)), paired(orders(rng))
    q[e == 1] = p[e == 1]
    mu[e == 1] = p[e == 1]
    p[e == 2] = C - 1 - np.arange(C)
    q[e == 2] = np.arange(C) ^ 1
    q[e == 3] = paired(orders(rng))[e == 3]
    w = np.zeros((N, 128, 4, 128, 4), np.float32)
    i, n = np.arange(112), np.arange(8)
    for b in range(4):
        for r in range(N):
            if o[r] == 0: w[r, i, b, i, b] = -4.0
            w[r, (120 if b < 2 else 96) + n, b, 112 + n, b] = 2.0 ** 30 if b < 2 else 2.0 ** -30
    return {"x": x.astype(np.float32).reshape(N, 128, 4 * C).astype(BF), "u": u.reshape(N, 128, 512).astype(BF), "v": v.astype(np.float32).astype(BF), **stored(p, q, mu), **weights(rng, w.astype(BF))}
def setup_inputs_spread(rng):
    d = setup_inputs(rng)
    d["x"] = wide(rng, N, 128, 4 * C, cols=6)
    return d
def check_inputs(d):
    b = []
    for k in ("x", "u", "v"):
        a = np.abs(d[k].astype(np.float32))
        if not (np.isfinite(a).all() and ((a == 0) | (a >= 2.0 ** -30) & (a <= 2.0 ** 30)).all()): b.append("a value of " + k)
    for k in ("pl", "ql", "ml"):
        for r in range(N):
            e = gentries(d[k][r])
            if not ((e >= 0) & (e < C)).all(): b.append("an entry of " + k)
            elif (e == PLACE).any() or (e[GROUP, e] != PLACE).any(): b.append(k + ": no involution without fixed points")
    none, least, most = [emit(mx_ref.quantize(np.full((128, 16), k, np.float32).astype(BF)))[1][0, 0] for k in (0.0, 2.0 ** -30, 2.0 ** 30)]
    for r in range(N):
        if ((d["wc"][r] == 0x7F) | (d["wc"][r] == 0xFF)).any(): b.append("wc: a code that is no number")
        s = mx_ref.live(d["ws"][r])
        if ((s != none) & ((s < least) | (s > most))).any(): b.append("ws: a scale out of range")
        if (((d["wc"][r].reshape(16, 8, 512, 4) & 0x7F) != 0) & (s == none)[:, None, :, None]).any(): b.append("wc: a code other than zero under the scale of zeros")
    return b
def powers(a):
    k = [np.tile(PLACE, (8, 1))]
    for i in range(C // 2 - 1): k.append(a[GROUP, k[-1]])
    return np.stack(k)
def mirror(p, q, stop):
    ahead, back = powers(q[GROUP, p]), powers(p[GROUP, q])
    i, j = np.argmax(stop[GROUP, ahead], axis=0), np.argmax(stop[GROUP, back], axis=0)
    return ahead[i, GROUP, back[j, GROUP, PLACE]]
def reference(x, u, v, pl, ql, ml, wc, ws):
    qu = [mx_ref.quantize(u[r]) for r in range(N)]
    lay = [pk(wc[r], ws[r]) for r in range(N)]
    p, q, mu = [[gentries(a[r]).astype(np.int64) for r in range(N)] for a in (pl, ql, ml)]
    now = [x[r] for r in range(N)]
    for step in STEP:
        own, sent, image = [], [], []
        for r in range(N):
            t = mx_ref.quantize(now[r])
            s = mx_ref.matmul(qu[r], t)[::16] + np.float32(0.0)
            d = decode(t).astype(BF)
            m = mirror(p[r], q[r], s < 0)
            z = (gcols(d, m).astype(np.float32) + gcols(d, q[r][GROUP, p[r]]).astype(np.float32)) * np.float32(0.5)
            sent.append(mx_ref.quantize(z.astype(BF)))
            w = (PLACE < mu[r]) & (s[GROUP, m] > s[GROUP, m[GROUP, mu[r]]])
            e = np.where(w | w[GROUP, mu[r]], mu[r], PLACE)
            q[r] = e[GROUP, q[r][GROUP, e]]
            own.append(d)
            image.append(m)
        now = [tile([gpick(mx_ref.matmul(pick(lay[r], np.arange(128 * b, 128 * b + 128)), sent[r ^ step]) * np.float32(0.03125), image[r]) + own[r][:, b::4].astype(np.float32) for b in range(4)]) for r in range(N)]
    y, qo = np.zeros((N, 128, C), np.float32), np.zeros((N, 8, C), np.float32)
    oc, osc = np.zeros((N, 128, 4 * C), np.uint8), np.zeros((N, 16, C), np.uint8)
    for r in range(N):
        t = mx_ref.quantize(now[r])
        y[r] = mx_ref.matmul(mx_ref.quantize(v[r]), t)
        qo[r] = q[r]
        oc[r], osc[r] = emit(t)
    return {"y": y, "qo": qo, "oc": oc, "osc": osc}

@@ -1,0 +1,462 @@
+from concourse.mybir import dt, AluOpType as OP, ActivationFunctionType as AF
+
+C = 384
+HD = (1, 2, 3)
+SCRATCH = {}
+LISTS = ["qw", "pw", "muw", "mupw", "sgw", "uw", "ix0", "ix1", "ix2", "ix3"] + ["l%d" % n for n in (2, 4, 8, 16, 32, 64)] + ["a%d" % s for s in (1, 2, 3)] + ["m%d" % s for s in (1, 2, 3)] + ["ra%d" % s for s in (1, 2, 3)] + ["rm%d" % s for s in (1, 2, 3)]
+
+
+def _sb(names, width, dtype, where="sbuf"):
+    for n in names.split():
+        SCRATCH[n] = (where, [128, width], dtype)
+
+
+_sb("iot murow mpr sgp sgr u16 sg16 qr0 qr1 qr2", C, "bfloat16")
+_sb("wlo wmi whi", 4 * 512, "bfloat16")
+_sb("wtop", 7 * 512, "bfloat16")
+_sb("ssb smr spr dr ysb qr3", C, "float32")
+_sb("rsb", 4 * C, "float32")
+_sb("mk0 mk1 sc0 sc1 k16 ka kb", C, "float16")
+_sb("hf hm h0 h1 hd", C, "bfloat16")
+_sb("hs gs th2 tg2", 416, "bfloat16")
+_sb("th1 tg1", C, "bfloat16")
+_sb("x0 xn z fo fp fa", 4 * C, "bfloat16")
+_sb("ut vt ones", 512, "bfloat16")
+_sb("et", 2048, "bfloat16")
+_sb("eq wq", 512, "float8_e4m3fn_x4")
+_sb("es wsc", 512, "uint8")
+_sb("uq vq up", 128, "float8_e4m3fn_x4")
+_sb("us vs ups", 128, "uint8")
+_sb("tq0 tq1 tq2 tq3 lq1 lq2 lq3 zq1 zq2 zq3", C, "float8_e4m3fn_x4")
+_sb("ts0 ts1 ts2 ts3 lp1 lp2 lp3 zs1 zs2 zs3", C, "uint8")
+_sb("pli qli mli", 24, "int32")
+_sb("ij idi", C, "int32")
+_sb("pi qi", 8, "int32")
+_sb("c24i u8i", 24, "int32")
+_sb("cols", 8, "float32")
+_sb("uoff", 8, "uint16")
+AT = {}
+
+
+def _wrapped(buf, names, dtype):
+    names = names.split()
+    for i, n in enumerate(names):
+        AT[n] = (buf, 24 * i)
+    _sb(buf, 24 * len(names), dtype)
+
+
+_wrapped("wi", "ei ex d3i d2i d1i d0i", "int32")
+_wrapped("wf", "cw pf mupf ww ep eq0 ep2 eq2 ev ne ng nw cur tgt if0 if1 if2 if3 dd du dz dw dsg pmc", "float32")
+_wrapped("wl", " ".join(n for n in LISTS if n[0] != "r"), "uint16")
+_wrapped("wr", " ".join(n for n in LISTS if n[0] == "r"), "uint16")
+_sb("pa pb", 2048, "float32", "psum")
+DMAS = ["dpl", "dql", "dml", "dx", "du_", "dv", "dwc", "dws", "doc", "dos0", "dos1", "dos2", "dos3", "dy0", "dy1", "dqo", "gap_wlo", "gap_wmi", "gap_whi", "gap_wtop"] + ["id%d" % i for i in range(5)]
+SEMAPHORES = ["sv", "sa", "st", "sp", "ls"] + ["%s%d" % (k, s) for s in (1, 2, 3) for k in ("at", "aa", "am")] + DMAS
+
+
+def rank_program(g, core, T, topo):
+    rank = T.rank_of(core)
+    if rank is None:
+        return
+    queue = {"v": g.vector, "a": g.scalar, "t": g.tensor, "p": g, "s": g.sync}
+    count = {"sv": 0, "sa": 0, "st": 0, "sp": 0}
+    own = {"v": "sv", "a": "sa", "t": "st", "p": "sp"}
+    know = {q: {} for q in queue}
+    then = {}
+    writer, readers = {}, {}
+
+    def merge(a, b):
+        for k, v in b.items():
+            if a.get(k, 0) < v:
+                a[k] = v
+
+    def meets(name, part, table):
+        d = table.get(name, {})
+        return [d[k] for k in d if part is None or k is None or k == part]
+
+    def regs(xs):
+        return [(x, None) if not isinstance(x, tuple) else x for x in xs]
+
+    def waits(q, reads, writes):
+        need = {}
+        for n, p in reads + writes:
+            for tok in meets(n, p, writer):
+                need[tok[0]] = max(need.get(tok[0], 0), tok[1])
+        for n, p in writes:
+            for toks in meets(n, p, readers):
+                for tok in toks:
+                    need[tok[0]] = max(need.get(tok[0], 0), tok[1])
+        for s in sorted(need):
+            if know[q].get(s, 0) < need[s]:
+                queue[q].wait_ge(T.sem[s], need[s])
+                know[q][s] = need[s]
+                merge(know[q], then.get((s, need[s]), {}))
+
+    def note(tok, reads, writes):
+        for n, p in reads:
+            readers.setdefault(n, {}).setdefault(p, []).append(tok)
+        for n, p in writes:
+            w = writer.setdefault(n, {})
+            r = readers.setdefault(n, {})
+            if p is None:
+                w.clear()
+                r.clear()
+            r[p] = []
+            w[p] = tok
+
+    def op(q, reads, writes, call, *args, **kw):
+        reads, writes = regs(reads), regs(writes)
+        waits(q, reads, writes)
+        s = own[q]
+        count[s] += 1
+        then[(s, count[s])] = dict(know[q])
+        call(*args, **kw).then_inc(T.sem[s], 1)
+        note((s, count[s]), reads, writes)
+
+    def dma(q, sem, out, in_, reads, writes):
+        reads, writes = regs(reads), regs(writes)
+        if sem not in count:
+            waits(q, reads, writes)
+        count[sem] = n = count.get(sem, 0) + 16
+        then[(sem, n)] = dict(know[q])
+        queue[q].dma_start(out, in_).then_inc(T.sem[sem], 16)
+        note((sem, n), reads, writes)
+
+    V, A, P, M = g.vector, g.scalar, g, g.tensor
+
+    def sl(n, i=None, w=C):
+        if n in AT:
+            buf, o = AT[n]
+            return T[buf][:, o:o + 24]
+        return T[n][:, :] if i is None else T[n][:, w * i:w * i + w]
+
+    def gath(out, oreg, win, wreg, lst):
+        op("a", [wreg, lst], [oreg], A.activation, out, win.indirect(sl(lst)), AF.Copy)
+
+    def both(out, win, lst):
+        buf, o = AT[lst]
+        op("v", [win, lst], [(out, 0)], V.tensor_copy, T[out][:, 0:C // 2], sl(win).indirect(T[buf][:, o:o + 12]))
+        op("a", [win, lst], [(out, 1)], A.activation, T[out][:, C // 2:C], sl(win).indirect(T[buf][:, o + 12:o + 24]), AF.Copy)
+
+    def copy_a(out, reads, writes, in_, func=AF.Copy, **kw):
+        op("a", reads, writes, A.activation, out, in_, func, **kw)
+
+    turn = [0]
+
+    def rowlist(row, rreg, lst, col=0):
+        i = turn[0] = 1 - turn[0]
+        cv = "sc%d" % i
+        op("v", [rreg, "k16"], [cv], V.tensor_tensor_scan, sl(cv), sl("k16"), row, 0.0, OP.add, OP.min)
+        op("v", [cv, ("cols", col)], [lst], V.tensor_scalar, sl(lst), T[cv][:, 15:C:16], T.cols[:, col:col + 1], None, OP.add)
+
+    def level(win, lst, out, dig):
+        i = turn[0] = 1 - turn[0]
+        mk, sc = "mk%d" % i, "sc%d" % i
+        both(mk, win, lst)
+        op("v", [mk, "k16"], [sc], V.tensor_tensor_scan, sl(sc), sl("k16"), sl(mk), 0.0, OP.add, OP.min)
+        if dig:
+            f = "if%s" % out[-1]
+            op("v", [sc, dig], [f], V.tensor_tensor, sl(f), T[sc][:, 15:C:16], sl(dig), OP.add)
+            op("v", [f, ("cols", 0)], [out], V.tensor_scalar, sl(out), sl(f), T.cols[:, 0:1], None, OP.add)
+        else:
+            op("v", [sc, ("cols", 0)], [out], V.tensor_scalar, sl(out), T[sc][:, 15:C:16], T.cols[:, 0:1], None, OP.add)
+
+    def small(out, in0, op0, in1):
+        op("v", [in0, in1], [out], V.tensor_tensor, sl(out), sl(in0), sl(in1), op0)
+
+    def ts(out, in0, s1, s2, o0, o1, reads, writes):
+        if o1 is None:
+            op("v", reads, writes, V.tensor_scalar, out, in0, s1, None, o0)
+        else:
+            op("v", reads, writes, V.tensor_scalar, out, in0, s1, s2, o0, o1)
+
+    def ts1(out, in0, s1, o0):
+        op("v", [in0], [out], V.tensor_scalar, sl(out), sl(in0), s1, None, o0)
+
+    def vcopy(out, in_):
+        op("v", [in_], [out], V.tensor_copy, sl(out), sl(in_))
+
+    def mm(out, oreg, lq, lqs, a, rq, rs):
+        op("t", [lq, lqs, rq, rs], [oreg], M.matmul_mx, out, T[lq][:, a:a + 128], T[lqs][:, a:a + 128], sl(rq), sl(rs), True, True)
+
+    dma("s", "dpl", sl("pli"), T.pl[:, :], [], ["pli"])
+    dma("a", "dx", sl("x0"), T.x[:, :], [], ["x0"])
+    dma("s", "dql", sl("qli"), T.ql[:, :], [], ["qli"])
+    dma("s", "du_", sl("ut"), T.u[:, :], [], ["ut"])
+    waits("s", [("x0", None)], [])
+    dma("s", "dml", sl("mli"), T.ml[:, :], [], ["mli"])
+    dma("s", "dwc", T.wq[:, :].bitcast(dt.uint8), T.wc[:, :], [], ["wq"])
+    dma("s", "dws", sl("wsc"), T.ws[:, :], [], ["wsc"])
+    dma("s", "dv", sl("vt"), T.v[:, :], [], ["vt"])
+
+    op("p", [], ["pi"], P.iota, T.pi[:, 0:1], [[1, 1]], 0, 1)
+    op("p", [], ["ij"], P.iota, sl("ij"), [[1, C]], 128, -1)
+    op("p", [], ["iot"], P.iota, sl("iot"), [[1, C]], -192, 0, allow_small_or_imprecise_dtypes=True)
+    op("p", [], ["u8i"], P.iota, T.u8i[:, 0:8], [[16, 8]], 0, 0)
+    op("p", [], ["c24i"], P.iota, sl("c24i"), [[16, 24]], 0, 0)
+    op("p", [], ["ones"], P.iota, sl("ones"), [[0, 512]], 1, 0, allow_small_or_imprecise_dtypes=True)
+    for i, (w, j) in enumerate((("wlo", 0), ("wmi", 0), ("whi", 0), ("wtop", 0), ("wtop", 3))):
+        dma("s", "id%d" % i, T[w][:, j * 512:j * 512 + C], sl("iot"), ["iot"], [(w, j)])
+    for w, n in (("wlo", 4), ("wmi", 4), ("whi", 4), ("wtop", 7)):
+        for j in range(n):
+            dma("s", "gap_" + w, T[w][:, j * 512 + C:j * 512 + 512], T.ones[:, 0:128], ["ones"], [(w, "gap")])
+    for b in range(4):
+        op("p", ["ones"], [("et", b)], P.affine_select, sl("et", b, 512), sl("ones"), [[-1, 512]], OP.is_equal, 0.0, b, 4)
+    ts(T.qi[:, 0:1], T.pi[:, 0:1], 15, None, OP.bitwise_and, None, ["pi"], [("qi", 0)])
+    ts(T.cols[:, 6:7], T.qi[:, 0:1], 15, 1024.0, OP.is_lt, OP.mult, [("qi", 0)], [("cols", 6)])
+    ts(T.cols[:, 0:1], T.cols[:, 6:7], 192.0, None, OP.add, None, [("cols", 6)], [("cols", 0)])
+    ts1("idi", "ij", 15, OP.bitwise_and)
+    ts(sl("ka"), sl("idi"), 0, 2048.0, OP.is_equal, OP.mult, ["idi"], ["ka"])
+    vcopy("pw", "pli")
+    vcopy("qw", "qli")
+    gath(sl("qr0"), "qr0", sl("iot"), "iot", "qw")
+    gath(T.wlo[:, 512:512 + C], ("wlo", 1), sl("qr0"), "qr0", "pw")
+    gath(T.wtop[:, 2048:2048 + C], ("wtop", 4), sl("iot"), "iot", "pw")
+    ts(sl("kb"), sl("idi"), 1, -1024.0, OP.is_equal, OP.mult, ["idi"], ["kb"])
+    small("k16", "ka", OP.add, "kb")
+    op("v", ["u8i"], ["uoff"], V.tensor_copy, sl("uoff"), T.u8i[:, 0:8])
+    op("v", ["ut"], ["uq", "us"], V.quantize_mx, sl("uq"), sl("us"), sl("ut"))
+    op("v", ["uq", "uoff"], ["up"], V.tensor_copy, T.up[:, :].bitcast(dt.uint32), T.uq[:, :].bitcast(dt.uint32).indirect(T.uoff[:, :]))
+    op("v", ["us", "uoff"], ["ups"], V.tensor_copy, sl("ups"), T.us[:, :].indirect(T.uoff[:, :]))
+    ts(T.qi[:, 1:2], T.pi[:, 0:1], 31, None, OP.bitwise_and, None, ["pi"], [("qi", 1)])
+    ts(T.cols[:, 1:2], T.qi[:, 0:1], 8, 256.0, OP.is_lt, OP.mult, [("qi", 0)], [("cols", 1)])
+    ts(T.cols[:, 2:3], T.qi[:, 0:1], 8, 256.0, OP.is_ge, OP.mult, [("qi", 0)], [("cols", 2)])
+
+    def rest_v():
+        ts(T.cols[:, 3:4], T.qi[:, 1:2], 16, 512.0, OP.is_lt, OP.mult, [("qi", 1)], [("cols", 3)])
+        ts(T.cols[:, 4:5], T.qi[:, 1:2], 16, 512.0, OP.is_ge, OP.mult, [("qi", 1)], [("cols", 4)])
+        ts(T.cols[:, 5:6], T.qi[:, 0:1], 0, None, OP.add, None, [("qi", 0)], [("cols", 5)])
+        ts(sl("cw"), sl("c24i"), T.cols[:, 5:6], None, OP.add, None, ["c24i", ("cols", 5)], ["cw"])
+        vcopy("pf", "pli")
+        small("pmc", "pf", OP.subtract, "cw")
+        ts1("pmc", "pmc", 2.0 ** -17, OP.mult)
+        op("v", [], [("hs", 1)], V.memset, T.hs[:, 0:16], 0.0)
+        op("v", [], [("hs", 2)], V.memset, T.hs[:, 400:416], 0.0)
+        op("v", [], [("gs", 1)], V.memset, T.gs[:, 0:16], 0.0)
+        op("v", [], [("gs", 2)], V.memset, T.gs[:, 400:416], 0.0)
+        vcopy("muw", "mli")
+
+    def rest_b():
+        rowlist(sl("mpr"), "mpr", "mupf")
+        vcopy("mupw", "mupf")
+        small("ww", "mupf", OP.subtract, "pf")
+        ts(sl("du"), sl("ww"), 0.0, 2.0, OP.is_lt, OP.mult, ["ww"], ["du"])
+        ts1("dd", "du", -1.0, OP.add)
+        ts(sl("tgt"), sl("dd"), T.cols[:, 6:7], None, OP.subtract, None, ["dd", ("cols", 6)], ["tgt"])
+        op("v", ["vt"], ["vq", "vs"], V.quantize_mx, sl("vq"), sl("vs"), sl("vt"))
+
+    slot = {}
+    for n in (1, 2, 3):
+        slot[n], slot[4 * n], slot[16 * n] = ("wlo", n), ("wmi", n), ("whi", n)
+    slot[64], slot[128], slot["p"], slot["p64"], slot["p128"] = [("wtop", i) for i in (1, 2, 4, 5, 6)]
+
+    def row(n):
+        w, i = slot[n]
+        return T[w][:, 512 * i:512 * i + C]
+
+    def lname(s, n):
+        return "a%d" % s if n == 1 else "l%d" % n
+
+    def power(s, to, n, by):
+        gath(row(to), slot[to], row(n), slot[n], lname(s, by))
+
+    def chain_row(s, i):
+        power(s, 2 << i, 1 << i, 1 << i)
+
+    def chain_list(s, i):
+        rowlist(row(2 << i), slot[2 << i], lname(s, 2 << i))
+
+    send_n = [0]
+
+    def send(s, dst, sem, out, in_, reads):
+        waits("p", regs(reads), [])
+        rid, pid, _ = topo.addr(dst)
+        g.remote_dma(out, in_, T.sem[sem], T.sem.ls, pid, rid, topo.mask(core, dst))
+        send_n[0] += len(topo.engines(core, dst))
+
+    steps = T.tables["STEP"] if "STEP" in T.tables else [1, 2, 3]
+    for s in (1, 2, 3):
+        dst = T.cores[rank ^ steps[s - 1]]
+        ne = len(topo.engines(core, dst))
+        tq, tsn, lq, lp = "tq%d" % (s - 1), "ts%d" % (s - 1), "lq%d" % s, "lp%d" % s
+        xin = "x0" if s == 1 else "xn"
+        mw, rm, ra = "m%d" % s, "rm%d" % s, "ra%d" % s
+        op("v", [xin], [tq, tsn], V.quantize_mx, sl(tq), sl(tsn), sl(xin))
+        mm(T.pb[:, 0:C], ("pb", 0), "up", "ups", 0, tq, tsn)
+        send(s, dst, "at%d" % s, T[lq][:, :].bitcast(dt.uint8), T[tq][:, :].bitcast(dt.uint8), [tq])
+        send(s, dst, "at%d" % s, sl(lp), sl(tsn), [tsn])
+        if s == 1:
+            rowlist(row(1), slot[1], "a1")
+            chain_row(1, 0)
+        send(s, dst, "aa%d" % s, sl(ra), sl("a%d" % s), ["a%d" % s])
+        for tok, names in ((("at%d" % s, 2 * ne), [lq, lp]), (("aa%d" % s, ne), [ra]), (("am%d" % s, ne), [rm])):
+            count[tok[0]] = tok[1]
+            note(tok, [], regs(names))
+        if s > 1:
+            chain_list(s, 0)
+        ts(sl("hm"), T.pb[:, 0:C], 0.0, T.cols[:, 2:3], OP.is_ge, OP.mult, [("cols", 2)], ["hm", ("pb", 0)])
+        ts(sl("hf"), T.pb[:, 0:C], 0.0, T.cols[:, 1:2], OP.is_ge, OP.mult, [("cols", 1)], ["hf", ("pb", 0)])
+        if s == 1:
+            chain_list(s, 0)
+        op("v", ["hm", "pw", "hf"], ["h0"], V.tensor_tensor, sl("h0"), T.hm[:, :].indirect(sl("pw")), sl("hf"), OP.add)
+
+        def unpack():
+            for b in range(4):
+                mm(T.pa[:, 512 * b:512 * b + C], ("pa", b), "eq", "es", 128 * b, tq, tsn)
+            for b in range(1, 4):
+                mm(T.pb[:, 512 * b:512 * b + C], ("pb", b), "eq", "es", 128 * b, lq, lp)
+
+        jobs = [(0, lambda: copy_a(sl("ssb"), [], ["ssb", ("pb", 0)], T.pb[:, 0:C]))]
+        if s == 1:
+            jobs.append((1, rest_v))
+            jobs.append((2, lambda: op("v", ["et"], ["eq", "es"], V.quantize_mx, sl("eq"), sl("es"), sl("et"))))
+            jobs.append((2, unpack))
+            jobs.append((3, lambda: gath(sl("murow"), "murow", sl("iot"), "iot", "muw")))
+            jobs.append((4, lambda: gath(sl("mpr"), "mpr", sl("murow"), "murow", "pw")))
+        else:
+            unpack()
+        jobs.append((3, lambda: power(s, 3, 1, 2)))
+        jobs.append((4, lambda: power(s, 12, 4, 8)))
+        for b in range(4):
+            jobs.append((5, lambda b=b: copy_a(sl("fo", b), [], [("fo", b), ("pa", b)], T.pa[:, 512 * b:512 * b + C])))
+        jobs += [(5, lambda: power(s, 48, 16, 32)), (6, lambda: power(s, 128, 64, 64)), (6, lambda: power(s, "p64", "p", 64))]
+
+        def some(i, k):
+            while jobs and k and jobs[0][0] <= i:
+                jobs.pop(0)[1]()
+                k -= 1
+
+        cur = "h0"
+        for i, n in enumerate((1, 2, 4, 8, 16, 32, 64, 64)):
+            if i in HD:
+                copy_a(sl("hd"), [cur], ["hd"], sl(cur), bias=float(-n))
+            else:
+                ts(sl("hd"), sl(cur), float(-n), None, OP.add, None, [cur], ["hd"])
+            if i < 5:
+                chain_row(s, i + 1)
+            some(i, (1, 3, 3, 1, 1, 2, 2, 2)[i])
+            nxt = "h1" if cur == "h0" else "h0"
+            oreg, out = (nxt, sl(nxt)) if i < 7 else (("hs", 0), T.hs[:, 16:16 + C])
+            op("v", [cur, lname(s, n), "hd"], [oreg], V.tensor_tensor, out, T[cur][:, :].indirect(sl(lname(s, n))), sl("hd"), OP.min)
+            if i < 5:
+                chain_list(s, i + 1)
+            cur = nxt
+
+        def pback(b):
+            copy_a(sl("fp", b), [], [("fp", b), ("pb", b)], T.pb[:, 512 * b:512 * b + C], scale=0.5)
+
+        gath(T.gs[:, 16:16 + C], ("gs", 0), T.hs[:, 16:16 + C], "hs", "pw")
+        op("v", ["hs"], ["th1"], V.transpose, sl("th1"), T.hs[:, 16:16 + C])
+        op("v", ["hs"], ["th2"], V.transpose, sl("th2"), sl("hs"))
+        some(9, 99)
+        mm(T.pb[:, 0:C], ("pb", 0), "eq", "es", 0, lq, lp)
+        op("v", ["gs"], ["tg1"], V.transpose, sl("tg1"), T.gs[:, 16:16 + C])
+        op("v", ["gs"], ["tg2"], V.transpose, sl("tg2"), sl("gs"))
+        for out, k, a, a0, a1, b, b0, b1 in (("ep", 0, "th1", 0, 384, "tg1", 8, 384), ("eq0", 1, "th1", 16, 384, "tg1", 24, 384), ("eq0", 0, "th2", 16, 400, "tg2", 24, 400), ("ep", 1, "th2", 32, 416, "tg2", 40, 416)):
+            op("v", [a, b], [(out, k)], V.tensor_tensor, T[AT[out][0]][:, AT[out][1] + k:AT[out][1] + 24:2], T[a][:, a0:a1:32], T[b][:, b0:b1:32], OP.subtract)
+        ts(sl("ep2"), sl("ep"), T.cols[:, 3:4], None, OP.mult, None, ["ep", ("cols", 3)], ["ep2"])
+        ts(sl("eq2"), sl("eq0"), T.cols[:, 4:5], None, OP.mult, None, ["eq0", ("cols", 4)], ["eq2"])
+        small("ev", "ep2", OP.add, "eq2")
+        ts1("ne", "ev", -1.0, OP.mult)
+        ts(sl("ng"), sl("ev"), 0.0, 131072.0, OP.is_lt, OP.mult, ["ev"], ["ng"])
+        small("ei", "ev", OP.max, "ne")
+        small("nw", "ng", OP.mult, "pmc")
+        ts1("d0i", "ei", 1536, OP.bitwise_and)
+        small("cur", "nw", OP.add, "cw")
+        ts(sl("d1i"), sl("ei"), 2, 1536, OP.logical_shift_right, OP.bitwise_and, ["ei"], ["d1i"])
+        small("if0", "d0i", OP.add, "cur")
+        ts(sl("d2i"), sl("ei"), 4, 1536, OP.logical_shift_right, OP.bitwise_and, ["ei"], ["d2i"])
+        vcopy("ix0", "if0")
+        level("wlo", "ix0", "ix1", "d1i")
+        power(s, "p128", "p64", 64)
+        small("ex", "ei", OP.add, "ng")
+        level("wmi", "ix1", "ix2", "d2i")
+        pback(0)
+        ts(sl("d3i"), sl("ex"), 6, 3584, OP.logical_shift_right, OP.bitwise_and, ["ex"], ["d3i"])
+        level("whi", "ix2", "ix3", "d3i")
+        pback(1)
+        level("wtop", "ix3", mw, None)
+        send(s, dst, "am%d" % s, sl(rm), sl(mw), [mw])
+        pback(2)
+        if s == 1:
+            rest_b()
+        qr, zq, zs = "qr%d" % (s - 1), "zq%d" % s, "zs%d" % s
+
+        def half(b):
+            gath(sl("fa", b), ("fa", b), sl("fp", b), ("fp", b), ra)
+
+        def zpart(b):
+            op("v", [("fp", b), rm, ("fa", b)], [("z", b)], V.tensor_tensor, T.z[:, b:4 * C:4], sl("fp", b).indirect(sl(rm)), sl("fa", b), OP.add)
+
+        def sigma():
+            i = turn[0] = 1 - turn[0]
+            cv = "sc%d" % i
+            op("v", ["sg16", "k16"], [cv], V.tensor_tensor_scan, sl(cv), sl("k16"), sl("sg16"), 0.0, OP.add, OP.min)
+            op("v", [cv, "tgt"], ["dz"], V.tensor_tensor, sl("dz"), T[cv][:, 15:C:16], sl("tgt"), OP.is_equal)
+            small("dw", "dz", OP.mult, "ww")
+            small("dsg", "dw", OP.add, "pf")
+            vcopy("sgw", "dsg")
+
+        both("smr", "ssb", mw)
+        both("spr", "smr", "pw")
+        pback(3)
+        half(0)
+        op("v", ["smr", "mupw", "spr"], ["dr"], V.tensor_tensor, sl("dr"), T.smr[:, :].indirect(sl("mupw")), sl("spr"), OP.subtract)
+        copy_a(sl("sg16"), ["dr"], ["sg16"], sl("dr"), func=AF.Sign)
+        half(1)
+        if s < 3:
+            sigma()
+            zpart(0)
+            gath(sl("u16"), "u16", sl(qr), qr, "sgw")
+            half(2)
+            zpart(1)
+            rowlist(sl("u16"), "u16", "uw")
+            gath(sl("sgp"), "sgp", sl("iot"), "iot", "sgw")
+            half(3)
+            gath(sl("sgr"), "sgr", sl("sgp"), "sgp", "pw")
+        else:
+            zpart(0)
+            half(2)
+            zpart(1)
+            half(3)
+        zpart(2)
+        zpart(3)
+        op("v", ["z"], [zq, zs], V.quantize_mx, sl(zq), sl(zs), sl("z"))
+        for b in range(4):
+            mm(T.pa[:, 512 * b:512 * b + C], ("pa", b), "wq", "wsc", 128 * b, zq, zs)
+        if s < 3:
+            gath(row(1), slot[1], sl("sgr"), "sgr", "uw")
+        else:
+            sigma()
+        for b in range(4):
+            copy_a(sl("rsb", b), [], [("rsb", b), ("pa", b)], T.pa[:, 512 * b:512 * b + C], scale=0.03125)
+            if b == 2 and s < 3:
+                rowlist(row(1), slot[1], "a%d" % (s + 1))
+                chain_row(s + 1, 0)
+        if s == 3:
+            gath(sl("u16"), "u16", sl(qr), qr, "sgw")
+            gath(sl("sgp"), "sgp", sl("iot"), "iot", "sgw")
+            gath(sl("sgr"), "sgr", sl("sgp"), "sgp", "pw")
+        else:
+            gath(sl("qr%d" % s), "qr%d" % s, row(1), slot[1], "pw")
+        for b in range(4):
+            op("v", [("rsb", b), mw, ("fo", b)], [("xn", b)], V.tensor_tensor, T.xn[:, b:4 * C:4], sl("rsb", b).indirect(sl(mw)), sl("fo", b), OP.add)
+            if s == 3 and b == 2:
+                rowlist(sl("u16"), "u16", "uw")
+                gath(row(1), slot[1], sl("sgr"), "sgr", "uw")
+    h = C // 2
+    for k in range(2):
+        op("v", ["xn"], [("tq3", k), ("ts3", k)], V.quantize_mx, T.tq3[:, h * k:h * k + h], T.ts3[:, h * k:h * k + h], T.xn[:, 4 * h * k:4 * h * k + 4 * h])
+        op("t", ["vq", "vs", ("tq3", k), ("ts3", k)], [("pb", k)], M.matmul_mx, T.pb[:, 512 * k:512 * k + h], sl("vq"), sl("vs"), T.tq3[:, h * k:h * k + h], T.ts3[:, h * k:h * k + h], True, True)
+    for k in range(2):
+        copy_a(T.ysb[:, h * k:h * k + h], [], [("ysb", k), ("pb", k)], T.pb[:, 512 * k:512 * k + h])
+        dma("a" if k else "s", "dy%d" % k, T.y[:, h * k:h * k + h], T.ysb[:, h * k:h * k + h], [("ysb", k)], [])
+    dma("s", "doc", T.oc[:, :], T.tq3[:, :].bitcast(dt.uint8), ["tq3"], [])
+    copy_a(sl("qr3"), [slot[1], "pw"], ["qr3"], row(1).indirect(sl("pw")), bias=192.0)
+    for k in range(4):
+        dma("s", "dos%d" % k, T.osc[4 * k:4 * k + 4, 0:C], T.ts3[32 * k:32 * k + 4, 0:C], ["ts3"], [])
+    dma("s", "dqo", T.qo[:, :], T.qr3[0:128:16, :], ["qr3"], [])
+    for sem in sorted(count):
+        if know["p"].get(sem, 0) < count[sem]:
+            g.wait_ge(T.sem[sem], count[sem])
+    g.wait_ge(T.sem.ls, send_n[0])

@@ -1,9 +1,10 @@
 from concourse.mybir import dt, AluOpType as OP, ActivationFunctionType as AF
 
 C = 384
-HD = (1, 2, 3)
+H = C // 2
+STEPS = (1, 2, 4, 8, 16, 32, 64, 64)
 SCRATCH = {}
-LISTS = ["qw", "pw", "muw", "mupw", "sgw", "uw", "ix0", "ix1", "ix2", "ix3"] + ["l%d" % n for n in (2, 4, 8, 16, 32, 64)] + ["a%d" % s for s in (1, 2, 3)] + ["m%d" % s for s in (1, 2, 3)] + ["ra%d" % s for s in (1, 2, 3)] + ["rm%d" % s for s in (1, 2, 3)]
+AT = {}
 
 
 def _sb(names, width, dtype, where="sbuf"):
@@ -11,15 +12,23 @@ def _sb(names, width, dtype, where="sbuf"):
         SCRATCH[n] = (where, [128, width], dtype)
 
 
-_sb("iot murow mpr sgp sgr u16 sg16 qr0 qr1 qr2", C, "bfloat16")
-_sb("wlo wmi whi", 4 * 512, "bfloat16")
-_sb("wtop", 7 * 512, "bfloat16")
-_sb("ssb smr spr dr ysb qr3", C, "float32")
+def _wrapped(buf, names, dtype):
+    names = names.split()
+    for i, n in enumerate(names):
+        AT[n] = (buf, 24 * i)
+    _sb(buf, 24 * len(names), dtype)
+
+
+_sb("iot prow qrow murow mpr pmr hrow urow pprow vrow lrow drow erow marks flag mrow", C, "bfloat16")
+_sb("pw2", 7 * C, "bfloat16")
+_sb("order mk sf sr unit", 2 * C, "bfloat16")
+_sb("fr le k16 sc0 sc1 sc2", 2 * C, "float16")
+_sb("scl", C, "float16")
+_sb("k16f ones2 markp", C, "bfloat16")
+_sb("kseed", 32, "bfloat16")
+_sb("ssb smr shp ysb qr3 scf key0 key1 ka kb khd", C, "float32")
+_sb("idc", 2 * C, "float32")
 _sb("rsb", 4 * C, "float32")
-_sb("mk0 mk1 sc0 sc1 k16 ka kb", C, "float16")
-_sb("hf hm h0 h1 hd", C, "bfloat16")
-_sb("hs gs th2 tg2", 416, "bfloat16")
-_sb("th1 tg1", C, "bfloat16")
 _sb("x0 xn z fo fp fa", 4 * C, "bfloat16")
 _sb("ut vt ones", 512, "bfloat16")
 _sb("et", 2048, "bfloat16")
@@ -30,99 +39,92 @@ _sb("us vs ups", 128, "uint8")
 _sb("tq0 tq1 tq2 tq3 lq1 lq2 lq3 zq1 zq2 zq3", C, "float8_e4m3fn_x4")
 _sb("ts0 ts1 ts2 ts3 lp1 lp2 lp3 zs1 zs2 zs3", C, "uint8")
 _sb("pli qli mli", 24, "int32")
-_sb("ij idi", C, "int32")
-_sb("pi qi", 8, "int32")
-_sb("c24i u8i", 24, "int32")
+_sb("pi qi u8i", 8, "int32")
+_sb("j16", 16, "float32")
+_sb("c24i", 24, "int32")
 _sb("cols", 8, "float32")
 _sb("uoff", 8, "uint16")
-AT = {}
-
-
-def _wrapped(buf, names, dtype):
-    names = names.split()
-    for i, n in enumerate(names):
-        AT[n] = (buf, 24 * i)
-    _sb(buf, 24 * len(names), dtype)
-
-
-_wrapped("wi", "ei ex d3i d2i d1i d0i", "int32")
-_wrapped("wf", "cw pf mupf ww ep eq0 ep2 eq2 ev ne ng nw cur tgt if0 if1 if2 if3 dd du dz dw dsg pmc", "float32")
-_wrapped("wl", " ".join(n for n in LISTS if n[0] != "r"), "uint16")
-_wrapped("wr", " ".join(n for n in LISTS if n[0] == "r"), "uint16")
+_sb("rl", 48, "uint16")
+_wrapped("wi", "kw loi di oi", "int32")
+_wrapped("wf", "cw pmc mupf pmpf ww2 wk lo_ hi_ mn gt idf f1 f2 sg a0 nz b0 c0 c1 a1_ a2_ v0 v1 t0 t1 sp lw w1 w2 pos2 pos1 lim0 lim1 clf clr e0 g0 y0 gl tg", "float32")
+_wrapped("wl", "pw qw muw lpw hpw mupw idl piw uw lol vl spl p2l p1l opl osl tl l2 l4 l8 l16 l32 l64 a1 a2 a3 m1 m2 m3", "uint16")
+_wrapped("wr", "ra1 ra2 ra3 rm1 rm2 rm3", "uint16")
 _sb("pa pb", 2048, "float32", "psum")
-DMAS = ["dpl", "dql", "dml", "dx", "du_", "dv", "dwc", "dws", "doc", "dos0", "dos1", "dos2", "dos3", "dy0", "dy1", "dqo", "gap_wlo", "gap_wmi", "gap_whi", "gap_wtop"] + ["id%d" % i for i in range(5)]
+DMAS = ["dpl", "dql", "dml", "dx", "du_", "dv", "dwc", "dws", "doc", "dos0", "dos1", "dos2", "dos3", "dy0", "dy1", "dqo"]
 SEMAPHORES = ["sv", "sa", "st", "sp", "ls"] + ["%s%d" % (k, s) for s in (1, 2, 3) for k in ("at", "aa", "am")] + DMAS
+
+CYC, GATHER, SCATTER, LEAST = 0.00104, 0.0013, 0.0032, 0.07
+SAME, CROSS, AHEAD = 0.12, 0.16, 0.1
+YIELD = {"v": 3.0, "a": 0.3, "t": 1.0, "p": 1.0, "s": 1.0, "n": 1.0}
+LOAD, ISSUE, FLIGHT = 1.8, 0.5, 2.0
 
 
 def rank_program(g, core, T, topo):
     rank = T.rank_of(core)
     if rank is None:
         return
-    queue = {"v": g.vector, "a": g.scalar, "t": g.tensor, "p": g, "s": g.sync}
-    count = {"sv": 0, "sa": 0, "st": 0, "sp": 0}
+    V, A, P, M = g.vector, g.scalar, g, g.tensor
+    queue = {"v": V, "a": A, "t": M, "p": P, "s": g.sync}
     own = {"v": "sv", "a": "sa", "t": "st", "p": "sp"}
-    know = {q: {} for q in queue}
-    then = {}
+    calls = []
     writer, readers = {}, {}
-
-    def merge(a, b):
-        for k, v in b.items():
-            if a.get(k, 0) < v:
-                a[k] = v
 
     def meets(name, part, table):
         d = table.get(name, {})
         return [d[k] for k in d if part is None or k is None or k == part]
 
-    def regs(xs):
-        return [(x, None) if not isinstance(x, tuple) else x for x in xs]
-
-    def waits(q, reads, writes):
-        need = {}
+    def add(q, reads, writes, hold, late, emit, after=()):
+        reads = [x if isinstance(x, tuple) else (x, None) for x in reads]
+        writes = [x if isinstance(x, tuple) else (x, None) for x in writes]
+        deps = set(after)
         for n, p in reads + writes:
-            for tok in meets(n, p, writer):
-                need[tok[0]] = max(need.get(tok[0], 0), tok[1])
+            deps.update(meets(n, p, writer))
         for n, p in writes:
-            for toks in meets(n, p, readers):
-                for tok in toks:
-                    need[tok[0]] = max(need.get(tok[0], 0), tok[1])
-        for s in sorted(need):
-            if know[q].get(s, 0) < need[s]:
-                queue[q].wait_ge(T.sem[s], need[s])
-                know[q][s] = need[s]
-                merge(know[q], then.get((s, need[s]), {}))
-
-    def note(tok, reads, writes):
+            for rs in meets(n, p, readers):
+                deps.update(rs)
+        me = len(calls)
+        calls.append({"q": q, "deps": sorted(deps), "hold": hold, "late": late, "emit": emit})
         for n, p in reads:
-            readers.setdefault(n, {}).setdefault(p, []).append(tok)
+            readers.setdefault(n, {}).setdefault(p, []).append(me)
         for n, p in writes:
-            w = writer.setdefault(n, {})
-            r = readers.setdefault(n, {})
+            w, r = writer.setdefault(n, {}), readers.setdefault(n, {})
             if p is None:
                 w.clear()
                 r.clear()
             r[p] = []
-            w[p] = tok
+            w[p] = me
+        return me
 
-    def op(q, reads, writes, call, *args, **kw):
-        reads, writes = regs(reads), regs(writes)
-        waits(q, reads, writes)
-        s = own[q]
-        count[s] += 1
-        then[(s, count[s])] = dict(know[q])
-        call(*args, **kw).then_inc(T.sem[s], 1)
-        note((s, count[s]), reads, writes)
+    count = {"sv": 0, "sa": 0, "st": 0, "sp": 0}
 
-    def dma(q, sem, out, in_, reads, writes):
-        reads, writes = regs(reads), regs(writes)
-        if sem not in count:
-            waits(q, reads, writes)
-        count[sem] = n = count.get(sem, 0) + 16
-        then[(sem, n)] = dict(know[q])
-        queue[q].dma_start(out, in_).then_inc(T.sem[sem], 16)
-        note((sem, n), reads, writes)
+    def op(q, reads, writes, hold, call, *args, **kw):
+        def emit():
+            count[own[q]] += 1
+            call(*args, **kw).then_inc(T.sem[own[q]], 1)
+            return own[q], count[own[q]]
+        return add(q, reads, writes, max(hold, LEAST), 0.0, emit)
 
-    V, A, P, M = g.vector, g.scalar, g, g.tensor
+    def dma(q, sem, out, in_, reads, writes, kib, after=()):
+        def emit():
+            count[sem] = 16
+            queue[q].dma_start(out, in_).then_inc(T.sem[sem], 16)
+            return sem, 16
+        return add(q, reads, writes, 0.1, LOAD + kib / 190.0, emit, after)
+
+    sent = [0]
+
+    def send(dst, sem, out, in_, reads):
+        def emit():
+            rid, pid, _ = topo.addr(dst)
+            g.remote_dma(out, in_, T.sem[sem], T.sem.ls, pid, rid, topo.mask(core, dst))
+            sent[0] += len(topo.engines(core, dst))
+        return add("p", reads, [], ISSUE, 0.0, emit)
+
+    def arrive(sem, n, names, sends, late):
+        def emit():
+            count[sem] = n
+            return sem, n
+        return add("n", [], names, 0.0, late, emit, sends)
 
     def sl(n, i=None, w=C):
         if n in AT:
@@ -130,333 +132,348 @@ def rank_program(g, core, T, topo):
             return T[buf][:, o:o + 24]
         return T[n][:, :] if i is None else T[n][:, w * i:w * i + w]
 
-    def gath(out, oreg, win, wreg, lst):
-        op("a", [wreg, lst], [oreg], A.activation, out, win.indirect(sl(lst)), AF.Copy)
+    def two(n):
+        buf, o = AT[n]
+        return T[buf][:, o:o + 48]
 
-    def both(out, win, lst):
+    def gath(how, out, win, lst, o0=0, wreg=None, oreg=None, wcols=None, **kw):
         buf, o = AT[lst]
-        op("v", [win, lst], [(out, 0)], V.tensor_copy, T[out][:, 0:C // 2], sl(win).indirect(T[buf][:, o:o + 12]))
-        op("a", [win, lst], [(out, 1)], A.activation, T[out][:, C // 2:C], sl(win).indirect(T[buf][:, o + 12:o + 24]), AF.Copy)
+        w = T[win][:, wcols[0]:wcols[1]] if wcols else sl(win)
+        wreg = wreg or [win]
+        for k, q in enumerate(how[::-1]):
+            n = C // len(how)
+            dst, src = T[out][:, o0 + n * k:o0 + n * k + n], w.indirect(T[buf][:, o + n // 16 * k:o + n // 16 * (k + 1)])
+            regs = [(out, (o0 + n * k) // H + i) for i in range(n // H)]
+            if q == "a":
+                op("a", wreg + [lst], regs, 0.065 + n * GATHER, A.activation, dst, src, AF.Copy, **kw)
+            elif kw:
+                op("v", wreg + [lst], regs, 0.05 + n * GATHER, V.tensor_scalar, dst, src, kw["scale"], kw["bias"], OP.mult, OP.add)
+            else:
+                op("v", wreg + [lst], regs, 0.05 + n * GATHER, V.tensor_copy, dst, src)
 
-    def copy_a(out, reads, writes, in_, func=AF.Copy, **kw):
-        op("a", reads, writes, A.activation, out, in_, func, **kw)
+    def halves(n, o0=0, k=2):
+        return [(n, o0 // H + i) for i in range(k)]
+
+    def fused(out, oreg, win, wreg, lst, o, in1, ireg):
+        op("v", wreg + [lst] + ireg, oreg, 0.05 + C * GATHER, V.tensor_tensor, out, win.indirect(sl(lst)), in1, o)
+
+    def copy_a(out, reads, writes, in_, n=C, func=AF.Copy, **kw):
+        op("a", reads, writes, n * CYC, A.activation, out, in_, func, **kw)
 
     turn = [0]
 
-    def rowlist(row, rreg, lst, col=0):
-        i = turn[0] = 1 - turn[0]
-        cv = "sc%d" % i
-        op("v", [rreg, "k16"], [cv], V.tensor_tensor_scan, sl(cv), sl("k16"), row, 0.0, OP.add, OP.min)
-        op("v", [cv, ("cols", col)], [lst], V.tensor_scalar, sl(lst), T[cv][:, 15:C:16], T.cols[:, col:col + 1], None, OP.add)
+    def pick(row, rreg, n=C):
+        turn[0] = (turn[0] + 1) % 3
+        cv = "sc%d" % turn[0]
+        op("v", rreg + ["k16"], [cv], n * CYC / 2, V.tensor_tensor_scan, T[cv][:, 0:n], T.k16[:, 0:n], row, 0.0, OP.add, OP.min)
+        return cv
 
-    def level(win, lst, out, dig):
-        i = turn[0] = 1 - turn[0]
-        mk, sc = "mk%d" % i, "sc%d" % i
-        both(mk, win, lst)
-        op("v", [mk, "k16"], [sc], V.tensor_tensor_scan, sl(sc), sl("k16"), sl(mk), 0.0, OP.add, OP.min)
-        if dig:
-            f = "if%s" % out[-1]
-            op("v", [sc, dig], [f], V.tensor_tensor, sl(f), T[sc][:, 15:C:16], sl(dig), OP.add)
-            op("v", [f, ("cols", 0)], [out], V.tensor_scalar, sl(out), sl(f), T.cols[:, 0:1], None, OP.add)
-        else:
-            op("v", [sc, ("cols", 0)], [out], V.tensor_scalar, sl(out), T[sc][:, 15:C:16], T.cols[:, 0:1], None, OP.add)
+    def rowlist(row, rreg, lst):
+        cv = pick(row, rreg)
+        op("v", [cv, ("cols", 0)], [lst], 0, V.tensor_scalar, sl(lst), T[cv][:, 15:C:16], T.cols[:, 0:1], None, OP.add)
 
-    def small(out, in0, op0, in1):
-        op("v", [in0, in1], [out], V.tensor_tensor, sl(out), sl(in0), sl(in1), op0)
+    def small(out, in0, o, in1):
+        op("v", [in0, in1], [out], 0, V.tensor_tensor, sl(out), sl(in0), sl(in1), o)
 
-    def ts(out, in0, s1, s2, o0, o1, reads, writes):
+    def ts(out, in0, s1, o0, s2=None, o1=None):
         if o1 is None:
-            op("v", reads, writes, V.tensor_scalar, out, in0, s1, None, o0)
+            op("v", [in0], [out], 0, V.tensor_scalar, sl(out), sl(in0), s1, None, o0)
         else:
-            op("v", reads, writes, V.tensor_scalar, out, in0, s1, s2, o0, o1)
-
-    def ts1(out, in0, s1, o0):
-        op("v", [in0], [out], V.tensor_scalar, sl(out), sl(in0), s1, None, o0)
+            op("v", [in0], [out], 0, V.tensor_scalar, sl(out), sl(in0), s1, s2, o0, o1)
 
     def vcopy(out, in_):
-        op("v", [in_], [out], V.tensor_copy, sl(out), sl(in_))
+        op("v", [in_], [out], 0, V.tensor_copy, sl(out), sl(in_))
 
-    def mm(out, oreg, lq, lqs, a, rq, rs):
-        op("t", [lq, lqs, rq, rs], [oreg], M.matmul_mx, out, T[lq][:, a:a + 128], T[lqs][:, a:a + 128], sl(rq), sl(rs), True, True)
+    def quant(q, s, x, a=0, n=C, part=None, xreg=None):
+        op("v", xreg or [x], [(q, part), (s, part)], 0.015 + 0.0011 * n, V.quantize_mx, T[q][:, a:a + n], T[s][:, a:a + n], T[x][:, 4 * a:4 * a + 4 * n])
 
-    dma("s", "dpl", sl("pli"), T.pl[:, :], [], ["pli"])
-    dma("a", "dx", sl("x0"), T.x[:, :], [], ["x0"])
-    dma("s", "dql", sl("qli"), T.ql[:, :], [], ["qli"])
-    dma("s", "du_", sl("ut"), T.u[:, :], [], ["ut"])
-    waits("s", [("x0", None)], [])
-    dma("s", "dml", sl("mli"), T.ml[:, :], [], ["mli"])
-    dma("s", "dwc", T.wq[:, :].bitcast(dt.uint8), T.wc[:, :], [], ["wq"])
-    dma("s", "dws", sl("wsc"), T.ws[:, :], [], ["wsc"])
-    dma("s", "dv", sl("vt"), T.v[:, :], [], ["vt"])
+    def mm(bank, lq, lqs, a, rq, rs, b=0, n=C, part=None):
+        op("t", [lq, lqs, (rq, part), (rs, part)], [bank], (n + 16) * 0.00125, M.matmul_mx, T[bank[0]][:, 512 * bank[1]:512 * bank[1] + n],
+           T[lq][:, a:a + 128], T[lqs][:, a:a + 128], T[rq][:, b:b + n], T[rs][:, b:b + n], True, True)
 
-    op("p", [], ["pi"], P.iota, T.pi[:, 0:1], [[1, 1]], 0, 1)
-    op("p", [], ["ij"], P.iota, sl("ij"), [[1, C]], 128, -1)
-    op("p", [], ["iot"], P.iota, sl("iot"), [[1, C]], -192, 0, allow_small_or_imprecise_dtypes=True)
-    op("p", [], ["u8i"], P.iota, T.u8i[:, 0:8], [[16, 8]], 0, 0)
-    op("p", [], ["c24i"], P.iota, sl("c24i"), [[16, 24]], 0, 0)
-    op("p", [], ["ones"], P.iota, sl("ones"), [[0, 512]], 1, 0, allow_small_or_imprecise_dtypes=True)
-    for i, (w, j) in enumerate((("wlo", 0), ("wmi", 0), ("whi", 0), ("wtop", 0), ("wtop", 3))):
-        dma("s", "id%d" % i, T[w][:, j * 512:j * 512 + C], sl("iot"), ["iot"], [(w, j)])
-    for w, n in (("wlo", 4), ("wmi", 4), ("whi", 4), ("wtop", 7)):
-        for j in range(n):
-            dma("s", "gap_" + w, T[w][:, j * 512 + C:j * 512 + 512], T.ones[:, 0:128], ["ones"], [(w, "gap")])
+    def bank(b, n=C):
+        return T[b[0]][:, 512 * b[1]:512 * b[1] + n]
+
+    dma("s", "dpl", sl("pli"), T.pl[:, :], [], ["pli"], 12)
+    dma("s", "dql", sl("qli"), T.ql[:, :], [], ["qli"], 12)
+    later = [calls.index(calls[-1])]
+    dma("s", "dml", sl("mli"), T.ml[:, :], [], ["mli"], 12, later)
+    for sem, out, in_, name in (("dx", sl("x0"), T.x, "x0"), ("du_", sl("ut"), T.u, "ut"), ("dwc", T.wq[:, :].bitcast(dt.uint8), T.wc, "wq"),
+                                ("dws", sl("wsc"), T.ws, "wsc"), ("dv", sl("vt"), T.v, "vt")):
+        dma("s", sem, out, in_[:, :], [], [name], 1000 if name in ("x0", "ut") else 1600, later)
+
+    def iota(n, pattern, base, cm, cols, view=None):
+        kw = {} if SCRATCH[n][2] == "int32" else {"allow_small_or_imprecise_dtypes": True}
+        op("p", [], [n], 0.13 + 2 * cols * CYC, P.iota, view or sl(n), pattern, base, cm, **kw)
+
+    iota("pi", [[1, 1]], 0, 1, 1, T.pi[:, 0:1])
+    iota("j16", [[1, 16]], 0, 0, 16)
+    iota("iot", [[1, C]], -H, 0, C)
+    iota("u8i", [[16, 8]], 0, 0, 8)
+    iota("c24i", [[16, 24]], 0, 0, 24)
+    for k in range(2):
+        copy_a(sl("idc", k), ["iot"], [("idc", k)], sl("iot"), scale=1024.0, bias=1024.0 * H + 512 * k - 1)
+    op("v", [], ["ones"], 256 * CYC, V.memset, sl("ones"), 1.0)
+    op("v", [], ["ones2"], H * CYC, V.memset, sl("ones2"), 1.0)
+    op("v", [], ["unit"], C * CYC, V.memset, sl("unit"), 2.0 ** -7)
     for b in range(4):
-        op("p", ["ones"], [("et", b)], P.affine_select, sl("et", b, 512), sl("ones"), [[-1, 512]], OP.is_equal, 0.0, b, 4)
-    ts(T.qi[:, 0:1], T.pi[:, 0:1], 15, None, OP.bitwise_and, None, ["pi"], [("qi", 0)])
-    ts(T.cols[:, 6:7], T.qi[:, 0:1], 15, 1024.0, OP.is_lt, OP.mult, [("qi", 0)], [("cols", 6)])
-    ts(T.cols[:, 0:1], T.cols[:, 6:7], 192.0, None, OP.add, None, [("cols", 6)], [("cols", 0)])
-    ts1("idi", "ij", 15, OP.bitwise_and)
-    ts(sl("ka"), sl("idi"), 0, 2048.0, OP.is_equal, OP.mult, ["idi"], ["ka"])
+        op("p", ["ones"], [("et", b)], 0.17 + 1024 * CYC, P.affine_select, sl("et", b, 512), sl("ones"), [[-1, 512]], OP.is_equal, 0.0, b, 4)
+    quant("eq", "es", "et", n=512)
+
+    def col(i, in0, reg, s1, o0, s2=None, o1=None):
+        if o1 is None:
+            op("v", [reg], [("cols", i)], 0, V.tensor_scalar, T.cols[:, i:i + 1], in0, s1, None, o0)
+        else:
+            op("v", [reg], [("cols", i)], 0, V.tensor_scalar, T.cols[:, i:i + 1], in0, s1, s2, o0, o1)
+
+    op("v", ["pi"], ["qi"], 0, V.tensor_scalar, T.qi[:, 0:1], T.pi[:, 0:1], 15, None, OP.bitwise_and)
+    col(5, T.qi[:, 0:1], "qi", 0, OP.add)
+    col(4, T.qi[:, 0:1], "qi", 1, OP.add)
+    col(6, T.qi[:, 0:1], "qi", 15, OP.is_lt, 1024.0, OP.mult)
+    col(0, T.cols[:, 6:7], ("cols", 6), float(H), OP.add)
+    col(1, T.cols[:, 6:7], ("cols", 6), 512.0, OP.mult)
+    col(2, T.cols[:, 1:2], ("cols", 1), -352.0, OP.add)
+    col(3, T.cols[:, 6:7], ("cols", 6), 512.0, OP.add)
+    op("v", [], [("cols", 7)], 0, V.memset, T.cols[:, 7:8], 2.0 ** -100)
+    op("v", ["j16", ("cols", 5)], ["f1"], 0, V.tensor_scalar, T.wf[:, AT["f1"][1]:AT["f1"][1] + 16], sl("j16"), T.cols[:, 5:6], 2048.0, OP.is_equal, OP.mult)
+    op("v", ["j16", ("cols", 4)], ["f2"], 0, V.tensor_scalar, T.wf[:, AT["f2"][1]:AT["f2"][1] + 16], sl("j16"), T.cols[:, 4:5], -1024.0, OP.is_equal, OP.mult)
+    op("v", ["f1", "f2"], ["kseed"], 0, V.tensor_tensor, T.kseed[:, 0:16], T.wf[:, AT["f1"][1]:AT["f1"][1] + 16], T.wf[:, AT["f2"][1]:AT["f2"][1] + 16], OP.add)
+    op("v", ["c24i", ("cols", 5)], ["cw"], 0, V.tensor_scalar, sl("cw"), sl("c24i"), T.cols[:, 5:6], None, OP.add)
+    op("v", ["c24i", ("cols", 5)], ["rl"], 0, V.tensor_scalar, T.rl[:, 0:24], sl("c24i"), 0.0, T.cols[:, 5:6], OP.mult, OP.add)
+    seed = T.kseed[:, 0:16].indirect(T.rl[:, 0:24])
+    op("v", ["kseed", "rl"], [("k16", 0)], 0.05 + C * GATHER, V.tensor_copy, T.k16[:, 0:C], seed)
+    op("a", ["kseed", "rl"], ["k16f"], 0.065 + C * GATHER, A.activation, sl("k16f"), seed, AF.Copy, scale=512.0)
+    op("v", [("k16", 0)], [("k16", 1)], H * CYC, V.tensor_copy, T.k16[:, C:2 * C], T.k16[:, 0:C])
+
+    op("v", ["u8i"], ["uoff"], 0, V.tensor_copy, sl("uoff"), T.u8i[:, 0:8])
+    quant("uq", "us", "ut", n=128)
+    op("v", ["uq", "uoff"], ["up"], 0.05 + 128 * GATHER, V.tensor_copy, T.up[:, :].bitcast(dt.uint32), T.uq[:, :].bitcast(dt.uint32).indirect(T.uoff[:, :]))
+    op("v", ["us", "uoff"], ["ups"], 0.05 + 128 * GATHER, V.tensor_copy, sl("ups"), T.us[:, :].indirect(T.uoff[:, :]))
+    quant("vq", "vs", "vt", n=128)
+
     vcopy("pw", "pli")
     vcopy("qw", "qli")
-    gath(sl("qr0"), "qr0", sl("iot"), "iot", "qw")
-    gath(T.wlo[:, 512:512 + C], ("wlo", 1), sl("qr0"), "qr0", "pw")
-    gath(T.wtop[:, 2048:2048 + C], ("wtop", 4), sl("iot"), "iot", "pw")
-    ts(sl("kb"), sl("idi"), 1, -1024.0, OP.is_equal, OP.mult, ["idi"], ["kb"])
-    small("k16", "ka", OP.add, "kb")
-    op("v", ["u8i"], ["uoff"], V.tensor_copy, sl("uoff"), T.u8i[:, 0:8])
-    op("v", ["ut"], ["uq", "us"], V.quantize_mx, sl("uq"), sl("us"), sl("ut"))
-    op("v", ["uq", "uoff"], ["up"], V.tensor_copy, T.up[:, :].bitcast(dt.uint32), T.uq[:, :].bitcast(dt.uint32).indirect(T.uoff[:, :]))
-    op("v", ["us", "uoff"], ["ups"], V.tensor_copy, sl("ups"), T.us[:, :].indirect(T.uoff[:, :]))
-    ts(T.qi[:, 1:2], T.pi[:, 0:1], 31, None, OP.bitwise_and, None, ["pi"], [("qi", 1)])
-    ts(T.cols[:, 1:2], T.qi[:, 0:1], 8, 256.0, OP.is_lt, OP.mult, [("qi", 0)], [("cols", 1)])
-    ts(T.cols[:, 2:3], T.qi[:, 0:1], 8, 256.0, OP.is_ge, OP.mult, [("qi", 0)], [("cols", 2)])
+    vcopy("muw", "mli")
+    gath("av", "qrow", "iot", "qw")
+    gath("av", "pw2", "qrow", "pw")
+    gath("a", "prow", "iot", "pw")
+    small("pmc", "pli", OP.subtract, "cw")
+    small("mn", "pli", OP.min, "cw")
+    ts("gt", "pmc", 0.0, OP.is_lt, float(C), OP.mult)
+    small("idf", "mn", OP.add, "gt")
+    vcopy("idl", "idf")
+    gath("a", "key0", "idc", "idl", bias=float(H))
+    copy_a(sl("key1"), ["key0"], ["key1"], sl("key0"), bias=-1.0)
+    gath("a", "murow", "iot", "muw")
+    gath("a", "mpr", "murow", "pw")
+    rowlist(sl("mpr"), ["mpr"], "mupf")
+    vcopy("mupw", "mupf")
+    small("lo_", "mupf", OP.min, "pli")
+    small("hi_", "mupf", OP.max, "pli")
+    vcopy("lpw", "lo_")
+    vcopy("hpw", "hi_")
+    gath("a", "pmr", "prow", "mupw")
+    rowlist(sl("pmr"), ["pmr"], "pmpf")
+    small("ww2", "pmpf", OP.subtract, "cw")
+    op("v", ["ww2", ("cols", 6)], ["wk"], 0, V.tensor_scalar, sl("wk"), sl("ww2"), T.cols[:, 6:7], None, OP.mult)
+    small("wk", "wk", OP.add, "cw")
 
-    def rest_v():
-        ts(T.cols[:, 3:4], T.qi[:, 1:2], 16, 512.0, OP.is_lt, OP.mult, [("qi", 1)], [("cols", 3)])
-        ts(T.cols[:, 4:5], T.qi[:, 1:2], 16, 512.0, OP.is_ge, OP.mult, [("qi", 1)], [("cols", 4)])
-        ts(T.cols[:, 5:6], T.qi[:, 0:1], 0, None, OP.add, None, [("qi", 0)], [("cols", 5)])
-        ts(sl("cw"), sl("c24i"), T.cols[:, 5:6], None, OP.add, None, ["c24i", ("cols", 5)], ["cw"])
-        vcopy("pf", "pli")
-        small("pmc", "pf", OP.subtract, "cw")
-        ts1("pmc", "pmc", 2.0 ** -17, OP.mult)
-        op("v", [], [("hs", 1)], V.memset, T.hs[:, 0:16], 0.0)
-        op("v", [], [("hs", 2)], V.memset, T.hs[:, 400:416], 0.0)
-        op("v", [], [("gs", 1)], V.memset, T.gs[:, 0:16], 0.0)
-        op("v", [], [("gs", 2)], V.memset, T.gs[:, 400:416], 0.0)
-        vcopy("muw", "mli")
+    def power(i):
+        return sl("pw2", i), halves("pw2", C * i)
 
-    def rest_b():
-        rowlist(sl("mpr"), "mpr", "mupf")
-        vcopy("mupw", "mupf")
-        small("ww", "mupf", OP.subtract, "pf")
-        ts(sl("du"), sl("ww"), 0.0, 2.0, OP.is_lt, OP.mult, ["ww"], ["du"])
-        ts1("dd", "du", -1.0, OP.add)
-        ts(sl("tgt"), sl("dd"), T.cols[:, 6:7], None, OP.subtract, None, ["dd", ("cols", 6)], ["tgt"])
-        op("v", ["vt"], ["vq", "vs"], V.quantize_mx, sl("vq"), sl("vs"), sl("vt"))
+    def lay_out(s):
+        a = "a%d" % s
+        rowlist(*power(0), a)
+        gath("a", "hrow", "prow", a)
+        cur, hd = "key0", "key1"
+        for i, n in enumerate(STEPS):
+            lst = a if n == 1 else "l%d" % n
+            if i < 6:
+                gath(ROWS[i], "pw2", "pw2", lst, o0=C * (i + 1), wreg=power(i)[1], wcols=(C * i, C * i + C))
+                rowlist(*power(i + 1), "l%d" % (2 * n))
+            if i:
+                hd = "khd"
+                copy_a(sl(hd), [cur], [hd], sl(cur), bias=float(-n))
+            nxt = "kb" if cur == "ka" else "ka"
+            fused(sl(nxt), [nxt], sl(cur), [cur], lst, OP.min, sl(hd), [hd])
+            cur = nxt
+        op("v", [cur, "k16f"], ["scf"], C * CYC, V.tensor_tensor_scan, sl("scf"), sl("k16f"), sl(cur), 0.0, OP.add, OP.min)
+        op("v", ["scf", ("cols", 1)], ["kw"], 0, V.tensor_scalar, sl("kw"), T.scf[:, 15:C:16], T.cols[:, 1:2], None, OP.add)
+        op("v", ["scf", ("cols", 2)], ["lol"], 0, V.tensor_scalar, sl("lol"), T.scf[:, 15:C:16], T.cols[:, 2:3], 2.0 ** -10, OP.add, OP.mult)
+        ts("di", "kw", 1023, OP.bitwise_and)
+        ts("oi", "di", 512.0, OP.is_ge)
+        fused(sl("drow"), ["drow"], sl(cur), [cur], a, OP.subtract, sl("idc", 0), ["idc"])
+        copy_a(sl("lrow"), ["drow"], ["lrow"], sl("drow"), func=AF.Relu, scale=2.0)
+        op("v", ["lrow", "ones2"], ["erow"], H * CYC, V.tensor_tensor_scan, sl("erow"), sl("lrow"), sl("ones2", 0), 0.0, OP.add, OP.mult)
+        gath("a", "le", "drow", "lol", o0=C)
+        gath("av", "le", "erow", "lol")
+        small("v0", "oi", OP.mult, "pmc")
+        small("v1", "v0", OP.add, "cw")
+        vcopy("vl", "v1")
+        gath("a", "vrow", "iot", "vl")
+        op("v", ["di", ("cols", 3)], ["sg"], 0, V.tensor_scalar, sl("sg"), sl("di"), -1.0, T.cols[:, 3:4], OP.mult, OP.add)
+        op("v", ["di", ("cols", 6)], ["nz"], 0, V.tensor_scalar, sl("nz"), sl("di"), T.cols[:, 6:7], None, OP.add)
+        small("a0", "nz", OP.min, "sg")
+        ts("c0", "di", -513.0, OP.add, 0.0, OP.min)
+        ts("c1", "c0", -2.0, OP.max)
+        op("v", halves("le", C) + ["k16"], ["scl"], H * CYC, V.tensor_tensor_scan, sl("scl"), sl("k16", 0), sl("le", 1), 0.0, OP.add, OP.min)
+        op("v", ["scl", ("cols", 6)], ["lw"], 0, V.tensor_scalar, sl("lw"), T.scl[:, 15:C:16], T.cols[:, 6:7], None, OP.add)
+        small("t1", "lw", OP.mult, "c1")
+        small("t0", "t1", OP.add, "a0")
+        ce = pick(sl("le", 0), halves("le"))
+        op("v", [ce, "t0"], ["sp"], 0, V.tensor_tensor, sl("sp"), T[ce][:, 15:C:16], sl("t0"), OP.add)
+        vcopy("spl", "sp")
+        op("v", ["vrow", "spl"], halves("order"), 0.05 + C * SCATTER, V.tensor_copy, sl("order", 0).indirect(sl("spl")), sl("vrow"))
+        rowlist(sl("order", 0), halves("order"), "opl")
+        gath("a", "order", "prow", "opl", o0=C)
+        ts("w1", "lw", -1.0, OP.mult, float(C), OP.add)
+        small("w2", "w1", OP.mult, "oi")
+        small("pos1", "sp", OP.add, "w2")
+        small("pos2", "pos1", OP.add, "lw")
+        op("v", ["pos1", "pos2"], ["p1l", "p2l"], 0, V.tensor_copy, two("p2l"), two("pos2"))
 
-    slot = {}
-    for n in (1, 2, 3):
-        slot[n], slot[4 * n], slot[16 * n] = ("wlo", n), ("wmi", n), ("whi", n)
-    slot[64], slot[128], slot["p"], slot["p64"], slot["p128"] = [("wtop", i) for i in (1, 2, 4, 5, 6)]
+    def mirror(mw):
+        gath("v", "mk", "marks", "opl")
+        gath("a", "mk", "markp", "opl", o0=C)
+        op("v", ["mk", "unit"], ["sf"], C * CYC, V.tensor_tensor_scan, sl("sf"), sl("unit"), sl("mk"), 1.0, OP.add, OP.min)
+        op("v", ["mk", "unit"], ["sr"], C * CYC, V.tensor_tensor_scan, T.sr[:, ::-1], sl("unit"), T.mk[:, ::-1], 1.0, OP.add, OP.min)
+        gath("a", "fr", "sf", "p2l", scale=128.0, bias=128.0)
+        gath("v", "fr", "sr", "p1l", o0=C, scale=128.0, bias=128.0)
+        cv = pick(sl("fr"), ["fr"], 2 * C)
+        op("v", [cv, "scl"], ["clf"], 0, V.tensor_tensor, sl("clf"), T[cv][:, 15:C:16], T.scl[:, 15:C:16], OP.min)
+        op("v", [cv, "scl"], ["clr"], 0, V.tensor_tensor, sl("clr"), T[cv][:, C + 15:2 * C:16], T.scl[:, 15:C:16], OP.min)
+        small("e0", "clr", OP.subtract, "clf")
+        small("g0", "clr", OP.is_lt, "clf")
+        small("y0", "e0", OP.add, "pos1")
+        small("gl", "g0", OP.mult, "lw")
+        small("tg", "y0", OP.add, "gl")
+        vcopy("tl", "tg")
+        gath("av", "mrow", "order", "tl")
+        rowlist(sl("mrow"), ["mrow"], mw)
 
-    def row(n):
-        w, i = slot[n]
-        return T[w][:, 512 * i:512 * i + C]
+    def conjugate(mw):
+        gath("av", "smr", "ssb", mw)
+        gath("av", "shp", "smr", "hpw")
+        fused(sl("flag"), ["flag"], sl("smr"), ["smr"], "lpw", OP.is_gt, sl("shp"), ["shp"])
+        cv = pick(sl("flag"), ["flag"])
+        op("v", [cv, "ww2"], ["f1"], 0, V.tensor_tensor, sl("f1"), T[cv][:, 15:C:16], sl("ww2"), OP.mult)
+        small("f2", "f1", OP.add, "wk")
+        vcopy("piw", "f2")
+        gath("av", "urow", "hrow", "piw")
+        gath("a", "pprow", "prow", "piw")
+        rowlist(sl("urow"), ["urow"], "uw")
+        gath("av", "pw2", "pprow", "uw")
 
-    def lname(s, n):
-        return "a%d" % s if n == 1 else "l%d" % n
-
-    def power(s, to, n, by):
-        gath(row(to), slot[to], row(n), slot[n], lname(s, by))
-
-    def chain_row(s, i):
-        power(s, 2 << i, 1 << i, 1 << i)
-
-    def chain_list(s, i):
-        rowlist(row(2 << i), slot[2 << i], lname(s, 2 << i))
-
-    send_n = [0]
-
-    def send(s, dst, sem, out, in_, reads):
-        waits("p", regs(reads), [])
-        rid, pid, _ = topo.addr(dst)
-        g.remote_dma(out, in_, T.sem[sem], T.sem.ls, pid, rid, topo.mask(core, dst))
-        send_n[0] += len(topo.engines(core, dst))
-
+    ROWS = ("a", "a", "a", "a", "a", "a")
     steps = T.tables["STEP"] if "STEP" in T.tables else [1, 2, 3]
     for s in (1, 2, 3):
         dst = T.cores[rank ^ steps[s - 1]]
         ne = len(topo.engines(core, dst))
         tq, tsn, lq, lp = "tq%d" % (s - 1), "ts%d" % (s - 1), "lq%d" % s, "lp%d" % s
-        xin = "x0" if s == 1 else "xn"
-        mw, rm, ra = "m%d" % s, "rm%d" % s, "ra%d" % s
-        op("v", [xin], [tq, tsn], V.quantize_mx, sl(tq), sl(tsn), sl(xin))
-        mm(T.pb[:, 0:C], ("pb", 0), "up", "ups", 0, tq, tsn)
-        send(s, dst, "at%d" % s, T[lq][:, :].bitcast(dt.uint8), T[tq][:, :].bitcast(dt.uint8), [tq])
-        send(s, dst, "at%d" % s, sl(lp), sl(tsn), [tsn])
-        if s == 1:
-            rowlist(row(1), slot[1], "a1")
-            chain_row(1, 0)
-        send(s, dst, "aa%d" % s, sl(ra), sl("a%d" % s), ["a%d" % s])
-        for tok, names in ((("at%d" % s, 2 * ne), [lq, lp]), (("aa%d" % s, ne), [ra]), (("am%d" % s, ne), [rm])):
-            count[tok[0]] = tok[1]
-            note(tok, [], regs(names))
-        if s > 1:
-            chain_list(s, 0)
-        ts(sl("hm"), T.pb[:, 0:C], 0.0, T.cols[:, 2:3], OP.is_ge, OP.mult, [("cols", 2)], ["hm", ("pb", 0)])
-        ts(sl("hf"), T.pb[:, 0:C], 0.0, T.cols[:, 1:2], OP.is_ge, OP.mult, [("cols", 1)], ["hf", ("pb", 0)])
-        if s == 1:
-            chain_list(s, 0)
-        op("v", ["hm", "pw", "hf"], ["h0"], V.tensor_tensor, sl("h0"), T.hm[:, :].indirect(sl("pw")), sl("hf"), OP.add)
-
-        def unpack():
-            for b in range(4):
-                mm(T.pa[:, 512 * b:512 * b + C], ("pa", b), "eq", "es", 128 * b, tq, tsn)
-            for b in range(1, 4):
-                mm(T.pb[:, 512 * b:512 * b + C], ("pb", b), "eq", "es", 128 * b, lq, lp)
-
-        jobs = [(0, lambda: copy_a(sl("ssb"), [], ["ssb", ("pb", 0)], T.pb[:, 0:C]))]
-        if s == 1:
-            jobs.append((1, rest_v))
-            jobs.append((2, lambda: op("v", ["et"], ["eq", "es"], V.quantize_mx, sl("eq"), sl("es"), sl("et"))))
-            jobs.append((2, unpack))
-            jobs.append((3, lambda: gath(sl("murow"), "murow", sl("iot"), "iot", "muw")))
-            jobs.append((4, lambda: gath(sl("mpr"), "mpr", sl("murow"), "murow", "pw")))
-        else:
-            unpack()
-        jobs.append((3, lambda: power(s, 3, 1, 2)))
-        jobs.append((4, lambda: power(s, 12, 4, 8)))
+        mw, rm, ra, zq, zs = "m%d" % s, "rm%d" % s, "ra%d" % s, "zq%d" % s, "zs%d" % s
+        lay_out(s)
+        arrive("aa%d" % s, ne, [ra], [send(dst, "aa%d" % s, sl(ra), sl("a%d" % s), ["a%d" % s])], FLIGHT + 0.8)
+        quant(tq, tsn, "x0" if s == 1 else "xn")
+        mm(("pb", 0), "up", "ups", 0, tq, tsn)
+        both = [send(dst, "at%d" % s, T[lq][:, :].bitcast(dt.uint8), T[tq][:, :].bitcast(dt.uint8), [tq]), send(dst, "at%d" % s, sl(lp), sl(tsn), [tsn])]
+        arrive("at%d" % s, 2 * ne, [lq, lp], both, FLIGHT + 3.5)
+        copy_a(sl("marks"), [("cols", 7)], ["marks", ("pb", 0)], bank(("pb", 0)), func=AF.Sign, bias=T.cols[:, 7:8])
+        gath("a", "markp", "marks", "pw")
+        copy_a(sl("ssb"), [], ["ssb", ("pb", 0)], bank(("pb", 0)))
         for b in range(4):
-            jobs.append((5, lambda b=b: copy_a(sl("fo", b), [], [("fo", b), ("pa", b)], T.pa[:, 512 * b:512 * b + C])))
-        jobs += [(5, lambda: power(s, 48, 16, 32)), (6, lambda: power(s, 128, 64, 64)), (6, lambda: power(s, "p64", "p", 64))]
-
-        def some(i, k):
-            while jobs and k and jobs[0][0] <= i:
-                jobs.pop(0)[1]()
-                k -= 1
-
-        cur = "h0"
-        for i, n in enumerate((1, 2, 4, 8, 16, 32, 64, 64)):
-            if i in HD:
-                copy_a(sl("hd"), [cur], ["hd"], sl(cur), bias=float(-n))
-            else:
-                ts(sl("hd"), sl(cur), float(-n), None, OP.add, None, [cur], ["hd"])
-            if i < 5:
-                chain_row(s, i + 1)
-            some(i, (1, 3, 3, 1, 1, 2, 2, 2)[i])
-            nxt = "h1" if cur == "h0" else "h0"
-            oreg, out = (nxt, sl(nxt)) if i < 7 else (("hs", 0), T.hs[:, 16:16 + C])
-            op("v", [cur, lname(s, n), "hd"], [oreg], V.tensor_tensor, out, T[cur][:, :].indirect(sl(lname(s, n))), sl("hd"), OP.min)
-            if i < 5:
-                chain_list(s, i + 1)
-            cur = nxt
-
-        def pback(b):
-            copy_a(sl("fp", b), [], [("fp", b), ("pb", b)], T.pb[:, 512 * b:512 * b + C], scale=0.5)
-
-        gath(T.gs[:, 16:16 + C], ("gs", 0), T.hs[:, 16:16 + C], "hs", "pw")
-        op("v", ["hs"], ["th1"], V.transpose, sl("th1"), T.hs[:, 16:16 + C])
-        op("v", ["hs"], ["th2"], V.transpose, sl("th2"), sl("hs"))
-        some(9, 99)
-        mm(T.pb[:, 0:C], ("pb", 0), "eq", "es", 0, lq, lp)
-        op("v", ["gs"], ["tg1"], V.transpose, sl("tg1"), T.gs[:, 16:16 + C])
-        op("v", ["gs"], ["tg2"], V.transpose, sl("tg2"), sl("gs"))
-        for out, k, a, a0, a1, b, b0, b1 in (("ep", 0, "th1", 0, 384, "tg1", 8, 384), ("eq0", 1, "th1", 16, 384, "tg1", 24, 384), ("eq0", 0, "th2", 16, 400, "tg2", 24, 400), ("ep", 1, "th2", 32, 416, "tg2", 40, 416)):
-            op("v", [a, b], [(out, k)], V.tensor_tensor, T[AT[out][0]][:, AT[out][1] + k:AT[out][1] + 24:2], T[a][:, a0:a1:32], T[b][:, b0:b1:32], OP.subtract)
-        ts(sl("ep2"), sl("ep"), T.cols[:, 3:4], None, OP.mult, None, ["ep", ("cols", 3)], ["ep2"])
-        ts(sl("eq2"), sl("eq0"), T.cols[:, 4:5], None, OP.mult, None, ["eq0", ("cols", 4)], ["eq2"])
-        small("ev", "ep2", OP.add, "eq2")
-        ts1("ne", "ev", -1.0, OP.mult)
-        ts(sl("ng"), sl("ev"), 0.0, 131072.0, OP.is_lt, OP.mult, ["ev"], ["ng"])
-        small("ei", "ev", OP.max, "ne")
-        small("nw", "ng", OP.mult, "pmc")
-        ts1("d0i", "ei", 1536, OP.bitwise_and)
-        small("cur", "nw", OP.add, "cw")
-        ts(sl("d1i"), sl("ei"), 2, 1536, OP.logical_shift_right, OP.bitwise_and, ["ei"], ["d1i"])
-        small("if0", "d0i", OP.add, "cur")
-        ts(sl("d2i"), sl("ei"), 4, 1536, OP.logical_shift_right, OP.bitwise_and, ["ei"], ["d2i"])
-        vcopy("ix0", "if0")
-        level("wlo", "ix0", "ix1", "d1i")
-        power(s, "p128", "p64", 64)
-        small("ex", "ei", OP.add, "ng")
-        level("wmi", "ix1", "ix2", "d2i")
-        pback(0)
-        ts(sl("d3i"), sl("ex"), 6, 3584, OP.logical_shift_right, OP.bitwise_and, ["ex"], ["d3i"])
-        level("whi", "ix2", "ix3", "d3i")
-        pback(1)
-        level("wtop", "ix3", mw, None)
-        send(s, dst, "am%d" % s, sl(rm), sl(mw), [mw])
-        pback(2)
-        if s == 1:
-            rest_b()
-        qr, zq, zs = "qr%d" % (s - 1), "zq%d" % s, "zs%d" % s
-
-        def half(b):
-            gath(sl("fa", b), ("fa", b), sl("fp", b), ("fp", b), ra)
-
-        def zpart(b):
-            op("v", [("fp", b), rm, ("fa", b)], [("z", b)], V.tensor_tensor, T.z[:, b:4 * C:4], sl("fp", b).indirect(sl(rm)), sl("fa", b), OP.add)
-
-        def sigma():
-            i = turn[0] = 1 - turn[0]
-            cv = "sc%d" % i
-            op("v", ["sg16", "k16"], [cv], V.tensor_tensor_scan, sl(cv), sl("k16"), sl("sg16"), 0.0, OP.add, OP.min)
-            op("v", [cv, "tgt"], ["dz"], V.tensor_tensor, sl("dz"), T[cv][:, 15:C:16], sl("tgt"), OP.is_equal)
-            small("dw", "dz", OP.mult, "ww")
-            small("dsg", "dw", OP.add, "pf")
-            vcopy("sgw", "dsg")
-
-        both("smr", "ssb", mw)
-        both("spr", "smr", "pw")
-        pback(3)
-        half(0)
-        op("v", ["smr", "mupw", "spr"], ["dr"], V.tensor_tensor, sl("dr"), T.smr[:, :].indirect(sl("mupw")), sl("spr"), OP.subtract)
-        copy_a(sl("sg16"), ["dr"], ["sg16"], sl("dr"), func=AF.Sign)
-        half(1)
-        if s < 3:
-            sigma()
-            zpart(0)
-            gath(sl("u16"), "u16", sl(qr), qr, "sgw")
-            half(2)
-            zpart(1)
-            rowlist(sl("u16"), "u16", "uw")
-            gath(sl("sgp"), "sgp", sl("iot"), "iot", "sgw")
-            half(3)
-            gath(sl("sgr"), "sgr", sl("sgp"), "sgp", "pw")
-        else:
-            zpart(0)
-            half(2)
-            zpart(1)
-            half(3)
-        zpart(2)
-        zpart(3)
-        op("v", ["z"], [zq, zs], V.quantize_mx, sl(zq), sl(zs), sl("z"))
+            mm(("pa", b), "eq", "es", 128 * b, tq, tsn)
+            copy_a(sl("fo", b), [], [("fo", b), ("pa", b)], bank(("pa", b)))
+        for b in (1, 2, 3, 0):
+            mm(("pb", b), "eq", "es", 128 * b, lq, lp)
+            copy_a(sl("fp", b), [], [("fp", b), ("pb", b)], bank(("pb", b)), scale=0.5)
+            gath("a", "fa", "fp", ra, o0=C * b, wreg=[("fp", b)], wcols=(C * b, C * b + C))
+        mirror(mw)
+        arrive("am%d" % s, ne, [rm], [send(dst, "am%d" % s, sl(rm), sl(mw), [mw])], FLIGHT + 0.8)
+        conjugate(mw)
         for b in range(4):
-            mm(T.pa[:, 512 * b:512 * b + C], ("pa", b), "wq", "wsc", 128 * b, zq, zs)
-        if s < 3:
-            gath(row(1), slot[1], sl("sgr"), "sgr", "uw")
-        else:
-            sigma()
+            fused(T.z[:, b:4 * C:4], [("z", b)], sl("fp", b), [("fp", b)], rm, OP.add, sl("fa", b), halves("fa", C * b))
+        quant(zq, zs, "z")
         for b in range(4):
-            copy_a(sl("rsb", b), [], [("rsb", b), ("pa", b)], T.pa[:, 512 * b:512 * b + C], scale=0.03125)
-            if b == 2 and s < 3:
-                rowlist(row(1), slot[1], "a%d" % (s + 1))
-                chain_row(s + 1, 0)
-        if s == 3:
-            gath(sl("u16"), "u16", sl(qr), qr, "sgw")
-            gath(sl("sgp"), "sgp", sl("iot"), "iot", "sgw")
-            gath(sl("sgr"), "sgr", sl("sgp"), "sgp", "pw")
-        else:
-            gath(sl("qr%d" % s), "qr%d" % s, row(1), slot[1], "pw")
-        for b in range(4):
-            op("v", [("rsb", b), mw, ("fo", b)], [("xn", b)], V.tensor_tensor, T.xn[:, b:4 * C:4], sl("rsb", b).indirect(sl(mw)), sl("fo", b), OP.add)
-            if s == 3 and b == 2:
-                rowlist(sl("u16"), "u16", "uw")
-                gath(row(1), slot[1], sl("sgr"), "sgr", "uw")
-    h = C // 2
+            mm(("pa", b), "wq", "wsc", 128 * b, zq, zs)
+            copy_a(sl("rsb", b), [], [("rsb", b), ("pa", b)], bank(("pa", b)), scale=0.03125)
+            fused(T.xn[:, b:4 * C:4], [("xn", b)], sl("rsb", b), [("rsb", b)], mw, OP.add, sl("fo", b), [("fo", b)])
+    gath("a", "qr3", "pw2", "pw", wreg=power(0)[1], wcols=(0, C), bias=float(H))
+    dma("s", "dqo", T.qo[:, :], T.qr3[0:128:16, :], ["qr3"], [], 12)
     for k in range(2):
-        op("v", ["xn"], [("tq3", k), ("ts3", k)], V.quantize_mx, T.tq3[:, h * k:h * k + h], T.ts3[:, h * k:h * k + h], T.xn[:, 4 * h * k:4 * h * k + 4 * h])
-        op("t", ["vq", "vs", ("tq3", k), ("ts3", k)], [("pb", k)], M.matmul_mx, T.pb[:, 512 * k:512 * k + h], sl("vq"), sl("vs"), T.tq3[:, h * k:h * k + h], T.ts3[:, h * k:h * k + h], True, True)
-    for k in range(2):
-        copy_a(T.ysb[:, h * k:h * k + h], [], [("ysb", k), ("pb", k)], T.pb[:, 512 * k:512 * k + h])
-        dma("a" if k else "s", "dy%d" % k, T.y[:, h * k:h * k + h], T.ysb[:, h * k:h * k + h], [("ysb", k)], [])
-    dma("s", "doc", T.oc[:, :], T.tq3[:, :].bitcast(dt.uint8), ["tq3"], [])
-    copy_a(sl("qr3"), [slot[1], "pw"], ["qr3"], row(1).indirect(sl("pw")), bias=192.0)
+        quant("tq3", "ts3", "xn", H * k, H, k)
+        mm(("pb", k), "vq", "vs", 0, "tq3", "ts3", H * k, H, k)
+        copy_a(T.ysb[:, H * k:H * k + H], [], [("ysb", k), ("pb", k)], bank(("pb", k), H), n=H)
+        dma("a" if k else "s", "dy%d" % k, T.y[:, H * k:H * k + H], T.ysb[:, H * k:H * k + H], [("ysb", k)], [], 96)
+    dma("s", "doc", T.oc[:, :], T.tq3[:, :].bitcast(dt.uint8), ["tq3"], [], 192)
     for k in range(4):
-        dma("s", "dos%d" % k, T.osc[4 * k:4 * k + 4, 0:C], T.ts3[32 * k:32 * k + 4, 0:C], ["ts3"], [])
-    dma("s", "dqo", T.qo[:, :], T.qr3[0:128:16, :], ["qr3"], [])
+        dma("s", "dos%d" % k, T.osc[4 * k:4 * k + 4, 0:C], T.ts3[32 * k:32 * k + 4, 0:C], ["ts3"], [], 2)
+
+    def gap(d, c):
+        return d["late"] + (0.0 if c["q"] == "n" else SAME if d["q"] == c["q"] else CROSS)
+
+    users = [[] for _ in calls]
+    for i, c in enumerate(calls):
+        for d in c["deps"]:
+            users[d].append(i)
+    for i in reversed(range(len(calls))):
+        c = calls[i]
+        c["way"] = c["hold"] + max([gap(c, calls[u]) + calls[u]["way"] for u in users[i]] + [c["late"]])
+    free = {q: 0.0 for q in "vatpsn"}
+    left = [len(c["deps"]) for c in calls]
+    ready = [i for i, n in enumerate(left) if n == 0]
+    order = []
+    todo = list(range(len(calls)))
+    while ready:
+        for i in todo:
+            c = calls[i]
+            c["can"] = max([free[c["q"]]] + [calls[d]["end"] + gap(calls[d], c) for d in c["deps"]])
+            c["end"] = c["can"] + c["hold"]
+        bound = max(calls[i]["can"] + calls[i]["way"] for i in todo)
+        soon = calls[min(ready, key=lambda i: calls[i]["can"])]
+        q, now = soon["q"], soon["can"]
+        mine = [calls[i] for i in todo if calls[i]["q"] == q and calls[i]["can"] < now + 1.5]
+
+        def fits(c):
+            held = [u for u in mine if u["way"] > c["way"] and u["can"] < c["end"]]
+            return all(c["end"] + u["way"] - bound <= YIELD[q] * (u["can"] - c["can"]) for u in held)
+
+        good = [i for i in ready if calls[i]["q"] == q and calls[i]["can"] <= now + AHEAD and fits(calls[i])]
+        if not good:
+            free[q] = now + AHEAD
+            continue
+        i = max(good, key=lambda i: calls[i]["way"])
+        c = calls[i]
+        free[q] = c["end"]
+        order.append(i)
+        ready.remove(i)
+        todo.remove(i)
+        for u in users[i]:
+            left[u] -= 1
+            if left[u] == 0:
+                ready.append(u)
+
+    know = {q: {} for q in queue}
+    for i in order:
+        c = calls[i]
+        q = c["q"]
+        if q == "n":
+            c["tok"], c["then"] = c["emit"](), {}
+            continue
+        need = {}
+        for d in c["deps"]:
+            tok = calls[d]["tok"]
+            if tok and need.get(tok[0], (0,))[0] < tok[1]:
+                need[tok[0]] = (tok[1], d)
+        for sem in sorted(need, key=lambda k: -calls[need[k][1]]["end"]):
+            n, d = need[sem]
+            if know[q].get(sem, 0) < n:
+                queue[q].wait_ge(T.sem[sem], n)
+                know[q][sem] = n
+                for k, v in calls[d]["then"].items():
+                    know[q][k] = max(know[q].get(k, 0), v)
+        c["then"] = dict(know[q])
+        c["tok"] = c["emit"]()
     for sem in sorted(count):
         if know["p"].get(sem, 0) < count[sem]:
             g.wait_ge(T.sem[sem], count[sem])
-    g.wait_ge(T.sem.ls, send_n[0])
+    g.wait_ge(T.sem.ls, sent[0])

@@ -21,15 +21,18 @@ def _wrapped(buf, names, dtype):
 
 _sb("iot prow qrow murow mpr pmr hrow urow pprow vrow lrow drow erow marks flag mrow", C, "bfloat16")
 _sb("pw2", 7 * C, "bfloat16")
-_sb("order mk sf sr unit", 2 * C, "bfloat16")
-_sb("fr le k16 sc0 sc1 sc2", 2 * C, "float16")
-_sb("scl", C, "float16")
+_sb("order mk sf sr unit hh", 2 * C, "bfloat16")
+SLOTS = 16
+_sb("fr le k16", 2 * C, "float16")
+_sb("sc", SLOTS * 2 * C, "float16")
 _sb("k16f ones2 markp", C, "bfloat16")
 _sb("kseed", 32, "bfloat16")
 _sb("ssb smr shp ysb qr3 scf key0 key1 ka kb khd", C, "float32")
 _sb("idc", 2 * C, "float32")
 _sb("rsb", 4 * C, "float32")
 _sb("x0 xn z fo fp fa", 4 * C, "bfloat16")
+_sb("ssp", C, "float32")
+_sb("laid", 2 * C, "float32")
 _sb("ut vt ones", 512, "bfloat16")
 _sb("et", 2048, "bfloat16")
 _sb("eq wq", 512, "float8_e4m3fn_x4")
@@ -42,21 +45,22 @@ _sb("pli qli mli", 24, "int32")
 _sb("pi qi u8i", 8, "int32")
 _sb("j16", 16, "float32")
 _sb("c24i", 24, "int32")
-_sb("cols", 8, "float32")
+_sb("cols", 16, "float32")
 _sb("uoff", 8, "uint16")
 _sb("rl", 48, "uint16")
 _wrapped("wi", "kw loi di oi", "int32")
-_wrapped("wf", "cw pmc mupf pmpf ww2 wk lo_ hi_ mn gt idf f1 f2 sg a0 nz b0 c0 c1 a1_ a2_ v0 v1 t0 t1 sp lw w1 w2 pos2 pos1 lim0 lim1 clf clr e0 g0 y0 gl tg", "float32")
-_wrapped("wl", "pw qw muw lpw hpw mupw idl piw uw lol vl spl p2l p1l opl osl tl l2 l4 l8 l16 l32 l64 a1 a2 a3 m1 m2 m3", "uint16")
+_wrapped("wf", "cw pmc mupf pmpf ww2 wk hk lo_ hi_ mn gt idf f1 f3 f2 f4 sg a0 nz c0 c1 v0 v1 t0 t1 sp lw w1 w2 pos2 pos1 clf clr e0 g0 y0 gl tg hd_ h1", "float32")
+_wrapped("wl", "pw qw muw lpw hpw mupw pmpw idl piw uw lol vl spl p2l p1l opl osl tl l2 l4 l8 l16 l32 l64 a1 a2 a3 m1 m2 m3", "uint16")
 _wrapped("wr", "ra1 ra2 ra3 rm1 rm2 rm3", "uint16")
 _sb("pa pb", 2048, "float32", "psum")
 DMAS = ["dpl", "dql", "dml", "dx", "du_", "dv", "dwc", "dws", "doc", "dos0", "dos1", "dos2", "dos3", "dy0", "dy1", "dqo"]
 SEMAPHORES = ["sv", "sa", "st", "sp", "ls"] + ["%s%d" % (k, s) for s in (1, 2, 3) for k in ("at", "aa", "am")] + DMAS
 
 CYC, GATHER, SCATTER, LEAST = 0.00104, 0.0013, 0.0032, 0.07
-SAME, CROSS, AHEAD = 0.12, 0.16, 0.1
-YIELD = {"v": 3.0, "a": 0.3, "t": 1.0, "p": 1.0, "s": 1.0, "n": 1.0}
+SAME, CROSS, AHEAD, MARGIN = 0.12, 0.16, 0.1, 0.3
+YIELD = {"v": 10.0, "a": 0.1, "t": 1.0, "p": 1.0, "s": 1.0, "n": 1.0}
 LOAD, ISSUE, FLIGHT = 1.8, 0.5, 2.0
+ORDER = []
 
 
 def rank_program(g, core, T, topo):
@@ -104,21 +108,21 @@ def rank_program(g, core, T, topo):
             return own[q], count[own[q]]
         return add(q, reads, writes, max(hold, LEAST), 0.0, emit)
 
-    def dma(q, sem, out, in_, reads, writes, kib, after=()):
+    def dma(q, sem, out, in_, reads, writes, kib, after=(), **kw):
         def emit():
             count[sem] = 16
-            queue[q].dma_start(out, in_).then_inc(T.sem[sem], 16)
+            queue[q].dma_start(out, in_, **kw).then_inc(T.sem[sem], 16)
             return sem, 16
-        return add(q, reads, writes, 0.1, LOAD + kib / 190.0, emit, after)
+        return add(q, reads, writes, ISSUE if q == "p" else 0.1, LOAD + kib / 190.0, emit, after)
 
     sent = [0]
 
-    def send(dst, sem, out, in_, reads):
+    def send(dst, sem, out, in_, reads, first=False):
         def emit():
             rid, pid, _ = topo.addr(dst)
             g.remote_dma(out, in_, T.sem[sem], T.sem.ls, pid, rid, topo.mask(core, dst))
             sent[0] += len(topo.engines(core, dst))
-        return add("p", reads, [], ISSUE, 0.0, emit)
+        return add("p", reads, [], ISSUE + (FLIGHT if first else 0.0), 0.0, emit)
 
     def arrive(sem, n, names, sends, late):
         def emit():
@@ -163,14 +167,13 @@ def rank_program(g, core, T, topo):
     turn = [0]
 
     def pick(row, rreg, n=C):
-        turn[0] = (turn[0] + 1) % 3
-        cv = "sc%d" % turn[0]
-        op("v", rreg + ["k16"], [cv], n * CYC / 2, V.tensor_tensor_scan, T[cv][:, 0:n], T.k16[:, 0:n], row, 0.0, OP.add, OP.min)
-        return cv
+        turn[0] = k = (turn[0] + 1) % SLOTS
+        op("v", rreg + ["k16"], [("sc", k)], n * CYC / 2, V.tensor_tensor_scan, T.sc[:, 2 * C * k:2 * C * k + n], T.k16[:, 0:n], row, 0.0, OP.add, OP.min)
+        return ("sc", k), T.sc[:, 2 * C * k + 15:2 * C * k + C:16], T.sc[:, 2 * C * k + C + 15:2 * C * k + 2 * C:16]
 
     def rowlist(row, rreg, lst):
-        cv = pick(row, rreg)
-        op("v", [cv, ("cols", 0)], [lst], 0, V.tensor_scalar, sl(lst), T[cv][:, 15:C:16], T.cols[:, 0:1], None, OP.add)
+        cv, got, _ = pick(row, rreg)
+        op("v", [cv, ("cols", 0)], [lst], 0, V.tensor_scalar, sl(lst), got, T.cols[:, 0:1], None, OP.add)
 
     def small(out, in0, o, in1):
         op("v", [in0, in1], [out], 0, V.tensor_tensor, sl(out), sl(in0), sl(in1), o)
@@ -196,11 +199,12 @@ def rank_program(g, core, T, topo):
 
     dma("s", "dpl", sl("pli"), T.pl[:, :], [], ["pli"], 12)
     dma("s", "dql", sl("qli"), T.ql[:, :], [], ["qli"], 12)
-    later = [calls.index(calls[-1])]
-    dma("s", "dml", sl("mli"), T.ml[:, :], [], ["mli"], 12, later)
+    later = [len(calls) - 1]
+    dma("s", "dml", sl("mli"), T.ml[:, :], [], ["mli"], 200)
     for sem, out, in_, name in (("dx", sl("x0"), T.x, "x0"), ("du_", sl("ut"), T.u, "ut"), ("dwc", T.wq[:, :].bitcast(dt.uint8), T.wc, "wq"),
                                 ("dws", sl("wsc"), T.ws, "wsc"), ("dv", sl("vt"), T.v, "vt")):
         dma("s", sem, out, in_[:, :], [], [name], 1000 if name in ("x0", "ut") else 1600, later)
+    loads = len(calls)
 
     def iota(n, pattern, base, cm, cols, view=None):
         kw = {} if SCRATCH[n][2] == "int32" else {"allow_small_or_imprecise_dtypes": True}
@@ -213,9 +217,9 @@ def rank_program(g, core, T, topo):
     iota("c24i", [[16, 24]], 0, 0, 24)
     for k in range(2):
         copy_a(sl("idc", k), ["iot"], [("idc", k)], sl("iot"), scale=1024.0, bias=1024.0 * H + 512 * k - 1)
-    op("v", [], ["ones"], 256 * CYC, V.memset, sl("ones"), 1.0)
+    iota("ones", [[0, 512]], 1, 0, 512)
     op("v", [], ["ones2"], H * CYC, V.memset, sl("ones2"), 1.0)
-    op("v", [], ["unit"], C * CYC, V.memset, sl("unit"), 2.0 ** -7)
+    op("v", [], ["unit"], C * CYC, V.memset, sl("unit"), 2.0 ** -8)
     for b in range(4):
         op("p", ["ones"], [("et", b)], 0.17 + 1024 * CYC, P.affine_select, sl("et", b, 512), sl("ones"), [[-1, 512]], OP.is_equal, 0.0, b, 4)
     quant("eq", "es", "et", n=512)
@@ -274,6 +278,7 @@ def rank_program(g, core, T, topo):
     vcopy("hpw", "hi_")
     gath("a", "pmr", "prow", "mupw")
     rowlist(sl("pmr"), ["pmr"], "pmpf")
+    vcopy("pmpw", "pmpf")
     small("ww2", "pmpf", OP.subtract, "cw")
     op("v", ["ww2", ("cols", 6)], ["wk"], 0, V.tensor_scalar, sl("wk"), sl("ww2"), T.cols[:, 6:7], None, OP.mult)
     small("wk", "wk", OP.add, "cw")
@@ -284,12 +289,17 @@ def rank_program(g, core, T, topo):
     def lay_out(s):
         a = "a%d" % s
         rowlist(*power(0), a)
-        gath("a", "hrow", "prow", a)
+        gath("a", "hh", "prow", a)
+        gath("a", "hh", "hh", "pmpw", o0=C, wreg=halves("hh"), wcols=(0, C))
+        cv, stay, swap = pick(sl("hh"), ["hh"], 2 * C)
+        op("v", [cv], ["hd_"], 0, V.tensor_tensor, sl("hd_"), swap, stay, OP.subtract)
+        op("v", ["hd_", ("cols", 6), ("cols", 0)], ["h1"], 0, V.tensor_scalar, sl("h1"), sl("hd_"), T.cols[:, 6:7], T.cols[:, 0:1], OP.mult, OP.add)
+        op("v", [cv, "h1"], ["hk"], 0, V.tensor_tensor, sl("hk"), stay, sl("h1"), OP.add)
         cur, hd = "key0", "key1"
         for i, n in enumerate(STEPS):
             lst = a if n == 1 else "l%d" % n
             if i < 6:
-                gath(ROWS[i], "pw2", "pw2", lst, o0=C * (i + 1), wreg=power(i)[1], wcols=(C * i, C * i + C))
+                gath("a", "pw2", "pw2", lst, o0=C * (i + 1), wreg=power(i)[1], wcols=(C * i, C * i + C))
                 rowlist(*power(i + 1), "l%d" % (2 * n))
             if i:
                 hd = "khd"
@@ -306,7 +316,7 @@ def rank_program(g, core, T, topo):
         copy_a(sl("lrow"), ["drow"], ["lrow"], sl("drow"), func=AF.Relu, scale=2.0)
         op("v", ["lrow", "ones2"], ["erow"], H * CYC, V.tensor_tensor_scan, sl("erow"), sl("lrow"), sl("ones2", 0), 0.0, OP.add, OP.mult)
         gath("a", "le", "drow", "lol", o0=C)
-        gath("av", "le", "erow", "lol")
+        gath("a", "le", "erow", "lol")
         small("v0", "oi", OP.mult, "pmc")
         small("v1", "v0", OP.add, "cw")
         vcopy("vl", "v1")
@@ -316,12 +326,12 @@ def rank_program(g, core, T, topo):
         small("a0", "nz", OP.min, "sg")
         ts("c0", "di", -513.0, OP.add, 0.0, OP.min)
         ts("c1", "c0", -2.0, OP.max)
-        op("v", halves("le", C) + ["k16"], ["scl"], H * CYC, V.tensor_tensor_scan, sl("scl"), sl("k16", 0), sl("le", 1), 0.0, OP.add, OP.min)
-        op("v", ["scl", ("cols", 6)], ["lw"], 0, V.tensor_scalar, sl("lw"), T.scl[:, 15:C:16], T.cols[:, 6:7], None, OP.add)
+        cl, lens, _ = pick(sl("le", 1), halves("le", C))
+        op("v", [cl, ("cols", 6)], ["lw"], 0, V.tensor_scalar, sl("lw"), lens, T.cols[:, 6:7], None, OP.add)
         small("t1", "lw", OP.mult, "c1")
         small("t0", "t1", OP.add, "a0")
-        ce = pick(sl("le", 0), halves("le"))
-        op("v", [ce, "t0"], ["sp"], 0, V.tensor_tensor, sl("sp"), T[ce][:, 15:C:16], sl("t0"), OP.add)
+        ce, ends, _ = pick(sl("le", 0), halves("le"))
+        op("v", [ce, "t0"], ["sp"], 0, V.tensor_tensor, sl("sp"), ends, sl("t0"), OP.add)
         vcopy("spl", "sp")
         op("v", ["vrow", "spl"], halves("order"), 0.05 + C * SCATTER, V.tensor_copy, sl("order", 0).indirect(sl("spl")), sl("vrow"))
         rowlist(sl("order", 0), halves("order"), "opl")
@@ -331,55 +341,59 @@ def rank_program(g, core, T, topo):
         small("pos1", "sp", OP.add, "w2")
         small("pos2", "pos1", OP.add, "lw")
         op("v", ["pos1", "pos2"], ["p1l", "p2l"], 0, V.tensor_copy, two("p2l"), two("pos2"))
+        return cl, lens
 
-    def mirror(mw):
-        gath("v", "mk", "marks", "opl")
-        gath("a", "mk", "markp", "opl", o0=C)
-        op("v", ["mk", "unit"], ["sf"], C * CYC, V.tensor_tensor_scan, sl("sf"), sl("unit"), sl("mk"), 1.0, OP.add, OP.min)
-        op("v", ["mk", "unit"], ["sr"], C * CYC, V.tensor_tensor_scan, T.sr[:, ::-1], sl("unit"), T.mk[:, ::-1], 1.0, OP.add, OP.min)
-        gath("a", "fr", "sf", "p2l", scale=128.0, bias=128.0)
-        gath("v", "fr", "sr", "p1l", o0=C, scale=128.0, bias=128.0)
-        cv = pick(sl("fr"), ["fr"], 2 * C)
-        op("v", [cv, "scl"], ["clf"], 0, V.tensor_tensor, sl("clf"), T[cv][:, 15:C:16], T.scl[:, 15:C:16], OP.min)
-        op("v", [cv, "scl"], ["clr"], 0, V.tensor_tensor, sl("clr"), T[cv][:, C + 15:2 * C:16], T.scl[:, 15:C:16], OP.min)
+    def mirror(mw, cl, lens):
+        op("v", ["ssb", "opl"], halves("mk"), 0.05 + C * GATHER, V.tensor_scalar, sl("mk", 0), sl("ssb").indirect(sl("opl")), 0.0, -0.5, OP.is_ge, OP.add)
+        gath("a", "mk", "markp", "opl", o0=C, scale=0.5)
+        op("v", ["mk", "unit"], ["sf"], C * CYC, V.tensor_tensor_scan, sl("sf"), sl("unit"), sl("mk"), 0.5, OP.add, OP.min)
+        op("v", ["mk", "unit"], ["sr"], C * CYC, V.tensor_tensor_scan, T.sr[:, ::-1], sl("unit"), T.mk[:, ::-1], 0.5, OP.add, OP.min)
+        gath("a", "fr", "sf", "p2l", scale=256.0, bias=128.0)
+        gath("v", "fr", "sr", "p1l", o0=C, scale=256.0, bias=128.0)
+        cv, before, behind = pick(sl("fr"), ["fr"], 2 * C)
+        op("v", [cv, cl], ["clf"], 0, V.tensor_tensor, sl("clf"), before, lens, OP.min)
+        op("v", [cv, cl], ["clr"], 0, V.tensor_tensor, sl("clr"), behind, lens, OP.min)
         small("e0", "clr", OP.subtract, "clf")
         small("g0", "clr", OP.is_lt, "clf")
         small("y0", "e0", OP.add, "pos1")
         small("gl", "g0", OP.mult, "lw")
         small("tg", "y0", OP.add, "gl")
         vcopy("tl", "tg")
-        gath("av", "mrow", "order", "tl")
+        gath("av" if mw == "m3" else "v", "mrow", "order", "tl")
         rowlist(sl("mrow"), ["mrow"], mw)
 
     def conjugate(mw):
-        gath("av", "smr", "ssb", mw)
+        if mw == "m3":
+            gath("a", "smr", "ssb", mw)
+        else:
+            gath("a", "ssp", "ssb", "pw")
+            gath("a", "laid", "ssb", "opl")
+            gath("a", "laid", "ssp", "opl", o0=C)
+            gath("a", "smr", "laid", "tl")
         gath("av", "shp", "smr", "hpw")
         fused(sl("flag"), ["flag"], sl("smr"), ["smr"], "lpw", OP.is_gt, sl("shp"), ["shp"])
-        cv = pick(sl("flag"), ["flag"])
-        op("v", [cv, "ww2"], ["f1"], 0, V.tensor_tensor, sl("f1"), T[cv][:, 15:C:16], sl("ww2"), OP.mult)
-        small("f2", "f1", OP.add, "wk")
-        vcopy("piw", "f2")
-        gath("av", "urow", "hrow", "piw")
-        gath("a", "pprow", "prow", "piw")
-        rowlist(sl("urow"), ["urow"], "uw")
+        cv, got, _ = pick(sl("flag"), ["flag"])
+        op("v", [cv, "ww2"], ["f1"], 0, V.tensor_tensor, sl("f1"), got, sl("ww2"), OP.mult)
+        op("v", [cv, "hd_"], ["f3"], 0, V.tensor_tensor, sl("f3"), got, sl("hd_"), OP.mult)
+        op("v", ["f1", "f3", "wk", "hk"], ["f2", "f4"], 0.1, V.tensor_tensor, two("f2"), two("f1"), two("wk"), OP.add)
+        op("v", ["f2", "f4"], ["piw", "uw"], 0, V.tensor_copy, two("piw"), two("f2"))
+        gath("av", "pprow", "prow", "piw")
         gath("av", "pw2", "pprow", "uw")
 
-    ROWS = ("a", "a", "a", "a", "a", "a")
     steps = T.tables["STEP"] if "STEP" in T.tables else [1, 2, 3]
     for s in (1, 2, 3):
         dst = T.cores[rank ^ steps[s - 1]]
         ne = len(topo.engines(core, dst))
         tq, tsn, lq, lp = "tq%d" % (s - 1), "ts%d" % (s - 1), "lq%d" % s, "lp%d" % s
         mw, rm, ra, zq, zs = "m%d" % s, "rm%d" % s, "ra%d" % s, "zq%d" % s, "zs%d" % s
-        lay_out(s)
-        arrive("aa%d" % s, ne, [ra], [send(dst, "aa%d" % s, sl(ra), sl("a%d" % s), ["a%d" % s])], FLIGHT + 0.8)
+        lengths = lay_out(s)
+        arrive("aa%d" % s, ne, [ra], [send(dst, "aa%d" % s, sl(ra), sl("a%d" % s), ["a%d" % s], s == 1)], FLIGHT + 0.8)
         quant(tq, tsn, "x0" if s == 1 else "xn")
         mm(("pb", 0), "up", "ups", 0, tq, tsn)
         both = [send(dst, "at%d" % s, T[lq][:, :].bitcast(dt.uint8), T[tq][:, :].bitcast(dt.uint8), [tq]), send(dst, "at%d" % s, sl(lp), sl(tsn), [tsn])]
         arrive("at%d" % s, 2 * ne, [lq, lp], both, FLIGHT + 3.5)
-        copy_a(sl("marks"), [("cols", 7)], ["marks", ("pb", 0)], bank(("pb", 0)), func=AF.Sign, bias=T.cols[:, 7:8])
-        gath("a", "markp", "marks", "pw")
         copy_a(sl("ssb"), [], ["ssb", ("pb", 0)], bank(("pb", 0)))
+        op("a", ["ssb", "pw", ("cols", 7)], ["markp"], 0.065 + C * GATHER, A.activation, sl("markp"), sl("ssb").indirect(sl("pw")), AF.Sign, bias=T.cols[:, 7:8])
         for b in range(4):
             mm(("pa", b), "eq", "es", 128 * b, tq, tsn)
             copy_a(sl("fo", b), [], [("fo", b), ("pa", b)], bank(("pa", b)))
@@ -387,7 +401,7 @@ def rank_program(g, core, T, topo):
             mm(("pb", b), "eq", "es", 128 * b, lq, lp)
             copy_a(sl("fp", b), [], [("fp", b), ("pb", b)], bank(("pb", b)), scale=0.5)
             gath("a", "fa", "fp", ra, o0=C * b, wreg=[("fp", b)], wcols=(C * b, C * b + C))
-        mirror(mw)
+        mirror(mw, *lengths)
         arrive("am%d" % s, ne, [rm], [send(dst, "am%d" % s, sl(rm), sl(mw), [mw])], FLIGHT + 0.8)
         conjugate(mw)
         for b in range(4):
@@ -423,10 +437,11 @@ def rank_program(g, core, T, topo):
     ready = [i for i, n in enumerate(left) if n == 0]
     order = []
     todo = list(range(len(calls)))
-    while ready:
+    while ready and not ORDER:
         for i in todo:
             c = calls[i]
             c["can"] = max([free[c["q"]]] + [calls[d]["end"] + gap(calls[d], c) for d in c["deps"]])
+            c["sure"] = max([0.0] + [calls[d]["end"] + gap(calls[d], c) + MARGIN for d in c["deps"] if calls[d]["q"] != c["q"]])
             c["end"] = c["can"] + c["hold"]
         bound = max(calls[i]["can"] + calls[i]["way"] for i in todo)
         soon = calls[min(ready, key=lambda i: calls[i]["can"])]
@@ -434,10 +449,14 @@ def rank_program(g, core, T, topo):
         mine = [calls[i] for i in todo if calls[i]["q"] == q and calls[i]["can"] < now + 1.5]
 
         def fits(c):
+            if c["sure"] > now and any(u["way"] > c["way"] and u["can"] < c["sure"] + c["hold"] for u in mine):
+                return False
             held = [u for u in mine if u["way"] > c["way"] and u["can"] < c["end"]]
             return all(c["end"] + u["way"] - bound <= YIELD[q] * (u["can"] - c["can"]) for u in held)
 
         good = [i for i in ready if calls[i]["q"] == q and calls[i]["can"] <= now + AHEAD and fits(calls[i])]
+        if todo[0] < loads:
+            good, q = todo[:1], calls[todo[0]]["q"]
         if not good:
             free[q] = now + AHEAD
             continue
@@ -453,8 +472,10 @@ def rank_program(g, core, T, topo):
                 ready.append(u)
 
     know = {q: {} for q in queue}
-    for i in order:
+    ORDER.extend(order)
+    for k, i in enumerate(ORDER):
         c = calls[i]
+        c["end"] = k
         q = c["q"]
         if q == "n":
             c["tok"], c["then"] = c["emit"](), {}

@@ -19,18 +19,28 @@ def _wrapped(buf, names, dtype):
     _sb(buf, 24 * len(names), dtype)
 
 
-_sb("iot prow qrow murow mpr pmr hrow urow pprow vrow lrow drow erow marks flag mrow", C, "bfloat16")
+_sb("iot prow qrow murow mpr pmr pprow vrow drow flag mrow", C, "bfloat16")
+_sb("lrow", C + 16, "bfloat16")
+_sb("sums", 4 * C, "bfloat16")
+EG = "a"
+SPLIT = 0
+HOME = ()
+TILE = 3.5
+XV = 0
+PX = 1
+PA = 1
+PIECES = (3, 3, 1)
 _sb("pw2", 7 * C, "bfloat16")
-_sb("order mk sf sr unit hh", 2 * C, "bfloat16")
+_sb("ip order mk sf sr unit hh", 2 * C, "bfloat16")
 SLOTS = 16
 _sb("fr le k16", 2 * C, "float16")
 _sb("sc", SLOTS * 2 * C, "float16")
-_sb("k16f ones2 markp", C, "bfloat16")
+_sb("k16f markp", C, "bfloat16")
 _sb("kseed", 32, "bfloat16")
 _sb("ssb smr shp ysb qr3 scf key0 key1 ka kb khd", C, "float32")
 _sb("idc", 2 * C, "float32")
-_sb("rsb", 4 * C, "float32")
-_sb("x0 xn z fo fp fa", 4 * C, "bfloat16")
+_sb("rsb mg", 4 * C, "float32")
+_sb("x0 xn xe z fo fp fa", 4 * C, "bfloat16")
 _sb("ssp", C, "float32")
 _sb("laid", 2 * C, "float32")
 _sb("ut vt ones", 512, "bfloat16")
@@ -50,16 +60,17 @@ _sb("uoff", 8, "uint16")
 _sb("rl", 48, "uint16")
 _wrapped("wi", "kw loi di oi", "int32")
 _wrapped("wf", "cw pmc mupf pmpf ww2 wk hk lo_ hi_ mn gt idf f1 f3 f2 f4 sg a0 nz c0 c1 v0 v1 t0 t1 sp lw w1 w2 pos2 pos1 clf clr e0 g0 y0 gl tg hd_ h1", "float32")
-_wrapped("wl", "pw qw muw lpw hpw mupw pmpw idl piw uw lol vl spl p2l p1l opl osl tl l2 l4 l8 l16 l32 l64 a1 a2 a3 m1 m2 m3", "uint16")
+_wrapped("wl", "pw qw muw lpw hpw mupw pmpw idl piw uw lol vl spl p2l p1l opl el tl l2 l4 l8 l16 l32 l64 a1 a2 a3 m1 m2 m3", "uint16")
 _wrapped("wr", "ra1 ra2 ra3 rm1 rm2 rm3", "uint16")
 _sb("pa pb", 2048, "float32", "psum")
-DMAS = ["dpl", "dql", "dml", "dx", "du_", "dv", "dwc", "dws", "doc", "dos0", "dos1", "dos2", "dos3", "dy0", "dy1", "dqo"]
+DMAS = ["dpl", "dql", "dml", "dx", "du_", "dv", "dwc", "dws", "doc0", "doc1", "dos0", "dos1", "dos2", "dos3", "dy0", "dy1", "dqo"]
 SEMAPHORES = ["sv", "sa", "st", "sp", "ls"] + ["%s%d" % (k, s) for s in (1, 2, 3) for k in ("at", "aa", "am")] + DMAS
 
-CYC, GATHER, SCATTER, LEAST = 0.00104, 0.0013, 0.0032, 0.07
-SAME, CROSS, AHEAD, MARGIN = 0.12, 0.16, 0.1, 0.3
-YIELD = {"v": 10.0, "a": 0.1, "t": 1.0, "p": 1.0, "s": 1.0, "n": 1.0}
-LOAD, ISSUE, FLIGHT = 1.8, 0.5, 2.0
+CYC, GATHER, SCATTER, LEAST = 0.00095, 0.0015, 0.0036, 0.065
+SAME, CROSS = 0.18, 0.24
+RULES = [(ahead, margin, {"v": v, "a": a}) for ahead in (0.03, 0.06, 0.1) for margin in (0.2,) for v in (2.0, 10.0) for a in (0.1, 0.5)]
+EARLY, FIRST = 26.0, {"v": 0.3, "a": 0.1}
+LOAD, ISSUE, FLIGHT = 1.4, 0.5, 1.4
 ORDER = []
 
 
@@ -144,10 +155,13 @@ def rank_program(g, core, T, topo):
         buf, o = AT[lst]
         w = T[win][:, wcols[0]:wcols[1]] if wcols else sl(win)
         wreg = wreg or [win]
-        for k, q in enumerate(how[::-1]):
-            n = C // len(how)
-            dst, src = T[out][:, o0 + n * k:o0 + n * k + n], w.indirect(T[buf][:, o + n // 16 * k:o + n // 16 * (k + 1)])
-            regs = [(out, (o0 + n * k) // H + i) for i in range(n // H)]
+        cut = {"a": 0, "v": C, "av": H, "aav": 128}[how]
+        for q, a, b in (("v", 0, cut), ("a", cut, C)):
+            n = b - a
+            if not n:
+                continue
+            dst, src = T[out][:, o0 + a:o0 + b], w.indirect(T[buf][:, o + a // 16:o + b // 16])
+            regs = halves(out, o0) if n == C else [(out, o0 // H + (q == "a"))]
             if q == "a":
                 op("a", wreg + [lst], regs, 0.065 + n * GATHER, A.activation, dst, src, AF.Copy, **kw)
             elif kw:
@@ -168,7 +182,7 @@ def rank_program(g, core, T, topo):
 
     def pick(row, rreg, n=C):
         turn[0] = k = (turn[0] + 1) % SLOTS
-        op("v", rreg + ["k16"], [("sc", k)], n * CYC / 2, V.tensor_tensor_scan, T.sc[:, 2 * C * k:2 * C * k + n], T.k16[:, 0:n], row, 0.0, OP.add, OP.min)
+        op("v", rreg + [("k16", 0) if n == C else "k16"], [("sc", k)], n * CYC / 2, V.tensor_tensor_scan, T.sc[:, 2 * C * k:2 * C * k + n], T.k16[:, 0:n], row, 0.0, OP.add, OP.min)
         return ("sc", k), T.sc[:, 2 * C * k + 15:2 * C * k + C:16], T.sc[:, 2 * C * k + C + 15:2 * C * k + 2 * C:16]
 
     def rowlist(row, rreg, lst):
@@ -204,7 +218,6 @@ def rank_program(g, core, T, topo):
     for sem, out, in_, name in (("dx", sl("x0"), T.x, "x0"), ("du_", sl("ut"), T.u, "ut"), ("dwc", T.wq[:, :].bitcast(dt.uint8), T.wc, "wq"),
                                 ("dws", sl("wsc"), T.ws, "wsc"), ("dv", sl("vt"), T.v, "vt")):
         dma("s", sem, out, in_[:, :], [], [name], 1000 if name in ("x0", "ut") else 1600, later)
-    loads = len(calls)
 
     def iota(n, pattern, base, cm, cols, view=None):
         kw = {} if SCRATCH[n][2] == "int32" else {"allow_small_or_imprecise_dtypes": True}
@@ -212,13 +225,13 @@ def rank_program(g, core, T, topo):
 
     iota("pi", [[1, 1]], 0, 1, 1, T.pi[:, 0:1])
     iota("j16", [[1, 16]], 0, 0, 16)
-    iota("iot", [[1, C]], -H, 0, C)
-    iota("u8i", [[16, 8]], 0, 0, 8)
     iota("c24i", [[16, 24]], 0, 0, 24)
+    iota("iot", [[1, C]], -H, 0, C)
+    loads = len(calls)
+    iota("u8i", [[16, 8]], 0, 0, 8)
     for k in range(2):
-        copy_a(sl("idc", k), ["iot"], [("idc", k)], sl("iot"), scale=1024.0, bias=1024.0 * H + 512 * k - 1)
+        copy_a(sl("idc", k), ["iot"], [("idc", k)], sl("iot"), scale=1024.0, bias=1024.0 * H + 511 * k - 1)
     iota("ones", [[0, 512]], 1, 0, 512)
-    op("v", [], ["ones2"], H * CYC, V.memset, sl("ones2"), 1.0)
     op("v", [], ["unit"], C * CYC, V.memset, sl("unit"), 2.0 ** -8)
     for b in range(4):
         op("p", ["ones"], [("et", b)], 0.17 + 1024 * CYC, P.affine_select, sl("et", b, 512), sl("ones"), [[-1, 512]], OP.is_equal, 0.0, b, 4)
@@ -237,7 +250,10 @@ def rank_program(g, core, T, topo):
     col(0, T.cols[:, 6:7], ("cols", 6), float(H), OP.add)
     col(1, T.cols[:, 6:7], ("cols", 6), 512.0, OP.mult)
     col(2, T.cols[:, 1:2], ("cols", 1), -352.0, OP.add)
-    col(3, T.cols[:, 6:7], ("cols", 6), 512.0, OP.add)
+    col(3, T.cols[:, 6:7], ("cols", 6), 511.0 + H, OP.add)
+    col(8, T.cols[:, 1:2], ("cols", 1), -127.5, OP.add)
+    op("v", [], [("sums", 3)], H * CYC, V.memset, T.sums[:, 3:4 * C:4], 0.0)
+    op("v", [], [("lrow", 0)], 0, V.memset, T.lrow[:, 0:1], 0.0)
     op("v", [], [("cols", 7)], 0, V.memset, T.cols[:, 7:8], 2.0 ** -100)
     op("v", ["j16", ("cols", 5)], ["f1"], 0, V.tensor_scalar, T.wf[:, AT["f1"][1]:AT["f1"][1] + 16], sl("j16"), T.cols[:, 5:6], 2048.0, OP.is_equal, OP.mult)
     op("v", ["j16", ("cols", 4)], ["f2"], 0, V.tensor_scalar, T.wf[:, AT["f2"][1]:AT["f2"][1] + 16], sl("j16"), T.cols[:, 4:5], -1024.0, OP.is_equal, OP.mult)
@@ -261,13 +277,15 @@ def rank_program(g, core, T, topo):
     gath("av", "qrow", "iot", "qw")
     gath("av", "pw2", "qrow", "pw")
     gath("a", "prow", "iot", "pw")
+    copy_a(sl("ip", 0), ["iot"], [("ip", 0)], sl("iot"))
+    copy_a(sl("ip", 1), ["prow"], [("ip", 1)], sl("prow"))
     small("pmc", "pli", OP.subtract, "cw")
     small("mn", "pli", OP.min, "cw")
     ts("gt", "pmc", 0.0, OP.is_lt, float(C), OP.mult)
     small("idf", "mn", OP.add, "gt")
     vcopy("idl", "idf")
     gath("a", "key0", "idc", "idl", bias=float(H))
-    copy_a(sl("key1"), ["key0"], ["key1"], sl("key0"), bias=-1.0)
+    gath("v", "key1", "idc", "idl", scale=1.0, bias=H - 1.0)
     gath("a", "murow", "iot", "muw")
     gath("a", "mpr", "murow", "pw")
     rowlist(sl("mpr"), ["mpr"], "mupf")
@@ -299,47 +317,50 @@ def rank_program(g, core, T, topo):
         for i, n in enumerate(STEPS):
             lst = a if n == 1 else "l%d" % n
             if i < 6:
-                gath("a", "pw2", "pw2", lst, o0=C * (i + 1), wreg=power(i)[1], wcols=(C * i, C * i + C))
+                gath("aav" if s == 1 or i > 4 else "a", "pw2", "pw2", lst, o0=C * (i + 1), wreg=power(i)[1], wcols=(C * i, C * i + C))
                 rowlist(*power(i + 1), "l%d" % (2 * n))
-            if i:
-                hd = "khd"
-                copy_a(sl(hd), [cur], [hd], sl(cur), bias=float(-n))
-            nxt = "kb" if cur == "ka" else "ka"
-            fused(sl(nxt), [nxt], sl(cur), [cur], lst, OP.min, sl(hd), [hd])
+            nxt, o = "kb" if cur == "ka" else "ka", AT[lst][1]
+            if i < SPLIT:
+                if i:
+                    hd = "khd"
+                    copy_a(sl(hd), [cur], [hd], sl(cur), bias=float(-n))
+                fused(sl(nxt), [nxt], sl(cur), [cur], lst, OP.min, sl(hd), [hd])
+            for k in range(2 if i >= SPLIT else 0):
+                if i:
+                    hd = "khd"
+                    copy_a(sl(hd, k, H), [(cur, k)], [(hd, k)], sl(cur, k, H), n=H, bias=float(-n))
+                op("v", [cur, lst, (hd, k)], [(nxt, k)], 0.05 + H * GATHER, V.tensor_tensor, sl(nxt, k, H), sl(cur).indirect(T.wl[:, o + 12 * k:o + 12 * k + 12]), sl(hd, k, H), OP.min)
             cur = nxt
         op("v", [cur, "k16f"], ["scf"], C * CYC, V.tensor_tensor_scan, sl("scf"), sl("k16f"), sl(cur), 0.0, OP.add, OP.min)
         op("v", ["scf", ("cols", 1)], ["kw"], 0, V.tensor_scalar, sl("kw"), T.scf[:, 15:C:16], T.cols[:, 1:2], None, OP.add)
         op("v", ["scf", ("cols", 2)], ["lol"], 0, V.tensor_scalar, sl("lol"), T.scf[:, 15:C:16], T.cols[:, 2:3], 2.0 ** -10, OP.add, OP.mult)
         ts("di", "kw", 1023, OP.bitwise_and)
-        ts("oi", "di", 512.0, OP.is_ge)
         fused(sl("drow"), ["drow"], sl(cur), [cur], a, OP.subtract, sl("idc", 0), ["idc"])
-        copy_a(sl("lrow"), ["drow"], ["lrow"], sl("drow"), func=AF.Relu, scale=2.0)
-        op("v", ["lrow", "ones2"], ["erow"], H * CYC, V.tensor_tensor_scan, sl("erow"), sl("lrow"), sl("ones2", 0), 0.0, OP.add, OP.mult)
-        gath("a", "le", "drow", "lol", o0=C)
-        gath("a", "le", "erow", "lol")
-        small("v0", "oi", OP.mult, "pmc")
+        copy_a(T.lrow[:, 1:C + 1], ["drow"], [("lrow", 1)], sl("drow"), func=AF.Relu)
+        now, last = T.lrow[:, 1:C + 1], T.lrow[:, 0:C]
+        for k, (d0, d1) in enumerate(((last, last), (now, last), (now, now))):
+            op("v", ["lrow"], [("sums", k)], H * CYC, V.tensor_tensor_scan, T.sums[:, k:4 * C:4], d0, d1, -float(H), OP.add, OP.add)
+        op("v", ["scf", ("cols", 8)], ["el"], 0, V.tensor_scalar, sl("el"), T.scf[:, 15:C:16], T.cols[:, 8:9], 2.0 ** -8, OP.add, OP.mult)
+        gath("av" if s == 1 else "a", "le", "sums", "el")
+        gath("av" if s == 1 else "a", "le", "drow", "lol", o0=C)
+        ts("v0", "di", 511.0, OP.is_ge, float(C), OP.mult)
         small("v1", "v0", OP.add, "cw")
         vcopy("vl", "v1")
-        gath("a", "vrow", "iot", "vl")
+        gath("a", "vrow", "ip", "vl")
         op("v", ["di", ("cols", 3)], ["sg"], 0, V.tensor_scalar, sl("sg"), sl("di"), -1.0, T.cols[:, 3:4], OP.mult, OP.add)
-        op("v", ["di", ("cols", 6)], ["nz"], 0, V.tensor_scalar, sl("nz"), sl("di"), T.cols[:, 6:7], None, OP.add)
+        op("v", ["di", ("cols", 0)], ["nz"], 0, V.tensor_scalar, sl("nz"), sl("di"), T.cols[:, 0:1], None, OP.add)
         small("a0", "nz", OP.min, "sg")
-        ts("c0", "di", -513.0, OP.add, 0.0, OP.min)
-        ts("c1", "c0", -2.0, OP.max)
         cl, lens, _ = pick(sl("le", 1), halves("le", C))
         op("v", [cl, ("cols", 6)], ["lw"], 0, V.tensor_scalar, sl("lw"), lens, T.cols[:, 6:7], None, OP.add)
-        small("t1", "lw", OP.mult, "c1")
-        small("t0", "t1", OP.add, "a0")
         ce, ends, _ = pick(sl("le", 0), halves("le"))
-        op("v", [ce, "t0"], ["sp"], 0, V.tensor_tensor, sl("sp"), ends, sl("t0"), OP.add)
+        op("v", [ce, "a0"], ["sp"], 0, V.tensor_tensor, sl("sp"), ends, sl("a0"), OP.add)
         vcopy("spl", "sp")
         op("v", ["vrow", "spl"], halves("order"), 0.05 + C * SCATTER, V.tensor_copy, sl("order", 0).indirect(sl("spl")), sl("vrow"))
         rowlist(sl("order", 0), halves("order"), "opl")
         gath("a", "order", "prow", "opl", o0=C)
-        ts("w1", "lw", -1.0, OP.mult, float(C), OP.add)
-        small("w2", "w1", OP.mult, "oi")
-        small("pos1", "sp", OP.add, "w2")
-        small("pos2", "pos1", OP.add, "lw")
+        small("w1", "v0", OP.max, "lw")
+        small("pos2", "sp", OP.add, "w1")
+        small("pos1", "pos2", OP.subtract, "lw")
         op("v", ["pos1", "pos2"], ["p1l", "p2l"], 0, V.tensor_copy, two("p2l"), two("pos2"))
         return cl, lens
 
@@ -364,21 +385,23 @@ def rank_program(g, core, T, topo):
 
     def conjugate(mw):
         if mw == "m3":
-            gath("a", "smr", "ssb", mw)
+            gath("v", "smr", "ssb", mw)
         else:
             gath("a", "ssp", "ssb", "pw")
             gath("a", "laid", "ssb", "opl")
             gath("a", "laid", "ssp", "opl", o0=C)
             gath("a", "smr", "laid", "tl")
-        gath("av", "shp", "smr", "hpw")
+        how = "v" if mw == "m3" else "av"
+        gath(how, "shp", "smr", "hpw")
         fused(sl("flag"), ["flag"], sl("smr"), ["smr"], "lpw", OP.is_gt, sl("shp"), ["shp"])
         cv, got, _ = pick(sl("flag"), ["flag"])
         op("v", [cv, "ww2"], ["f1"], 0, V.tensor_tensor, sl("f1"), got, sl("ww2"), OP.mult)
         op("v", [cv, "hd_"], ["f3"], 0, V.tensor_tensor, sl("f3"), got, sl("hd_"), OP.mult)
         op("v", ["f1", "f3", "wk", "hk"], ["f2", "f4"], 0.1, V.tensor_tensor, two("f2"), two("f1"), two("wk"), OP.add)
         op("v", ["f2", "f4"], ["piw", "uw"], 0, V.tensor_copy, two("piw"), two("f2"))
-        gath("av", "pprow", "prow", "piw")
-        gath("av", "pw2", "pprow", "uw")
+        how = "a" if mw == "m3" else "av"
+        gath(how, "pprow", "prow", "piw")
+        gath(how, "pw2", "pprow", "uw")
 
     steps = T.tables["STEP"] if "STEP" in T.tables else [1, 2, 3]
     for s in (1, 2, 3):
@@ -387,38 +410,73 @@ def rank_program(g, core, T, topo):
         tq, tsn, lq, lp = "tq%d" % (s - 1), "ts%d" % (s - 1), "lq%d" % s, "lp%d" % s
         mw, rm, ra, zq, zs = "m%d" % s, "rm%d" % s, "ra%d" % s, "zq%d" % s, "zs%d" % s
         lengths = lay_out(s)
-        arrive("aa%d" % s, ne, [ra], [send(dst, "aa%d" % s, sl(ra), sl("a%d" % s), ["a%d" % s], s == 1)], FLIGHT + 0.8)
+        home = s in HOME
+
+        def tile_over(q, sc):
+            both = [send(dst, "at%d" % s, T[lq][:, :].bitcast(dt.uint8), T[q][:, :].bitcast(dt.uint8), [q], s == 1 and home), send(dst, "at%d" % s, sl(lp), sl(sc), [sc])]
+            arrive("at%d" % s, 2 * ne, [lq, lp], both, FLIGHT + TILE)
+
+        if not home:
+            arrive("aa%d" % s, ne, [ra], [send(dst, "aa%d" % s, sl(ra), sl("a%d" % s), ["a%d" % s], s == 1)], FLIGHT + 0.8)
         quant(tq, tsn, "x0" if s == 1 else "xn")
         mm(("pb", 0), "up", "ups", 0, tq, tsn)
-        both = [send(dst, "at%d" % s, T[lq][:, :].bitcast(dt.uint8), T[tq][:, :].bitcast(dt.uint8), [tq]), send(dst, "at%d" % s, sl(lp), sl(tsn), [tsn])]
-        arrive("at%d" % s, 2 * ne, [lq, lp], both, FLIGHT + 3.5)
+        if not home:
+            tile_over(tq, tsn)
         copy_a(sl("ssb"), [], ["ssb", ("pb", 0)], bank(("pb", 0)))
         op("a", ["ssb", "pw", ("cols", 7)], ["markp"], 0.065 + C * GATHER, A.activation, sl("markp"), sl("ssb").indirect(sl("pw")), AF.Sign, bias=T.cols[:, 7:8])
         for b in range(4):
             mm(("pa", b), "eq", "es", 128 * b, tq, tsn)
-            copy_a(sl("fo", b), [], [("fo", b), ("pa", b)], bank(("pa", b)))
+            if s == 3 or b < XV:
+                copy_a(sl("fo", b), [], [("fo", b), ("pa", b)], bank(("pa", b)))
         for b in (1, 2, 3, 0):
-            mm(("pb", b), "eq", "es", 128 * b, lq, lp)
-            copy_a(sl("fp", b), [], [("fp", b), ("pb", b)], bank(("pb", b)), scale=0.5)
-            gath("a", "fa", "fp", ra, o0=C * b, wreg=[("fp", b)], wcols=(C * b, C * b + C))
+            src = ("pa" if home else "pb", b)
+            if not home:
+                mm(src, "eq", "es", 128 * b, lq, lp)
+            copy_a(sl("fp", b), [], [("fp", b), src], bank(src), scale=0.5)
+            gath("a", "fa", "fp", "a%d" % s if home else ra, o0=C * b, wreg=[("fp", b)], wcols=(C * b, C * b + C))
         mirror(mw, *lengths)
-        arrive("am%d" % s, ne, [rm], [send(dst, "am%d" % s, sl(rm), sl(mw), [mw])], FLIGHT + 0.8)
+        if not home:
+            arrive("am%d" % s, ne, [rm], [send(dst, "am%d" % s, sl(rm), sl(mw), [mw])], FLIGHT + (0.8 if s < 3 else 0.1))
         conjugate(mw)
         for b in range(4):
-            fused(T.z[:, b:4 * C:4], [("z", b)], sl("fp", b), [("fp", b)], rm, OP.add, sl("fa", b), halves("fa", C * b))
+            buf, o = AT[mw if home else rm]
+            n = C // PIECES[s - 1]
+            for a in range(0, C, n):
+                op("v", [("fp", b), mw if home else rm] + halves("fa", C * b), [("z", (b, a))], 0.05 + n * GATHER, V.tensor_tensor, T.z[:, 4 * a + b:4 * (a + n):4],
+                   sl("fp", b).indirect(T[buf][:, o + a // 16:o + (a + n) // 16]), T.fa[:, C * b + a:C * b + a + n], OP.add)
         quant(zq, zs, "z")
+        if home:
+            tile_over(zq, zs)
+            zq, zs = lq, lp
         for b in range(4):
-            mm(("pa", b), "wq", "wsc", 128 * b, zq, zs)
-            copy_a(sl("rsb", b), [], [("rsb", b), ("pa", b)], bank(("pa", b)), scale=0.03125)
-            fused(T.xn[:, b:4 * C:4], [("xn", b)], sl("rsb", b), [("rsb", b)], mw, OP.add, sl("fo", b), [("fo", b)])
+            mm(("pb", b), "wq", "wsc", 128 * b, zq, zs)
+            copy_a(sl("rsb", b), [], [("rsb", b), ("pb", b)], bank(("pb", b)), scale=0.03125)
+            if s < 3 and b < XV:
+                o, n = AT[mw][1], C // PX
+                for a in range(0, C, n):
+                    op("v", [("rsb", b), mw, ("fo", b)], [("xn", (b, a))], 0.05 + n * GATHER, V.tensor_tensor, T.xn[:, 4 * a + b:4 * (a + n):4],
+                       sl("rsb", b).indirect(T.wl[:, o + a // 16:o + (a + n) // 16]), T.fo[:, C * b + a:C * b + a + n], OP.add)
+            elif s < 3:
+                o, n = AT[mw][1], C // PX
+                for a in range(0, C, n):
+                    op("a", [("rsb", b), mw], [("mg", (b, a))], 0.065 + n * GATHER, A.activation, T.mg[:, C * b + a:C * b + a + n],
+                       sl("rsb", b).indirect(T.wl[:, o + a // 16:o + (a + n) // 16]), AF.Copy)
+                m = C // PA
+                for a in range(0, C, m):
+                    op("v", [("mg", (b, k)) for k in range(0, C, n) if k < a + m and a < k + n], [("xn", (b, a)), ("pa", b)], m * CYC, V.tensor_tensor,
+                       T.xn[:, 4 * a + b:4 * (a + m):4], T.pa[:, 512 * b + a:512 * b + a + m], T.mg[:, C * b + a:C * b + a + m], OP.add)
     gath("a", "qr3", "pw2", "pw", wreg=power(0)[1], wcols=(0, C), bias=float(H))
     dma("s", "dqo", T.qo[:, :], T.qr3[0:128:16, :], ["qr3"], [], 12)
+    o = AT["m3"][1]
     for k in range(2):
-        quant("tq3", "ts3", "xn", H * k, H, k)
-        mm(("pb", k), "vq", "vs", 0, "tq3", "ts3", H * k, H, k)
-        copy_a(T.ysb[:, H * k:H * k + H], [], [("ysb", k), ("pb", k)], bank(("pb", k), H), n=H)
-        dma("a" if k else "s", "dy%d" % k, T.y[:, H * k:H * k + H], T.ysb[:, H * k:H * k + H], [("ysb", k)], [], 96)
-    dma("s", "doc", T.oc[:, :], T.tq3[:, :].bitcast(dt.uint8), ["tq3"], [], 192)
+        for b in range(4):
+            op("v", [("rsb", b), "m3", ("fo", b)], [("xe", 4 * k + b)], 0.05 + H * GATHER, V.tensor_tensor, T.xe[:, 4 * H * k + b:4 * H * (k + 1):4],
+               sl("rsb", b).indirect(T.wl[:, o + 12 * k:o + 12 * k + 12]), T.fo[:, C * b + H * k:C * b + H * k + H], OP.add)
+        quant("tq3", "ts3", "xe", H * k, H, k, [("xe", 4 * k + b) for b in range(4)])
+        mm(("pa", k), "vq", "vs", 0, "tq3", "ts3", H * k, H, k)
+        copy_a(T.ysb[:, H * k:H * k + H], [], [("ysb", k), ("pa", k)], bank(("pa", k), H), n=H)
+        dma("a" if k else "s", "dy%d" % k, T.y[:, H * k:H * k + H], T.ysb[:, H * k:H * k + H], [("ysb", k)], [], 400 - 300 * k)
+        dma("s", "doc%d" % k, T.oc[:, 4 * H * k:4 * H * (k + 1)], sl("tq3", k, H).bitcast(dt.uint8), [("tq3", k)], [], 400 - 300 * k)
     for k in range(4):
         dma("s", "dos%d" % k, T.osc[4 * k:4 * k + 4, 0:C], T.ts3[32 * k:32 * k + 4, 0:C], ["ts3"], [], 2)
 
@@ -432,44 +490,50 @@ def rank_program(g, core, T, topo):
     for i in reversed(range(len(calls))):
         c = calls[i]
         c["way"] = c["hold"] + max([gap(c, calls[u]) + calls[u]["way"] for u in users[i]] + [c["late"]])
-    free = {q: 0.0 for q in "vatpsn"}
-    left = [len(c["deps"]) for c in calls]
-    ready = [i for i, n in enumerate(left) if n == 0]
-    order = []
-    todo = list(range(len(calls)))
-    while ready and not ORDER:
-        for i in todo:
-            c = calls[i]
-            c["can"] = max([free[c["q"]]] + [calls[d]["end"] + gap(calls[d], c) for d in c["deps"]])
-            c["sure"] = max([0.0] + [calls[d]["end"] + gap(calls[d], c) + MARGIN for d in c["deps"] if calls[d]["q"] != c["q"]])
-            c["end"] = c["can"] + c["hold"]
-        bound = max(calls[i]["can"] + calls[i]["way"] for i in todo)
-        soon = calls[min(ready, key=lambda i: calls[i]["can"])]
-        q, now = soon["q"], soon["can"]
-        mine = [calls[i] for i in todo if calls[i]["q"] == q and calls[i]["can"] < now + 1.5]
+    for c in calls:
+        c["in"] = [(calls[d], gap(calls[d], c), calls[d]["q"] != c["q"]) for d in c["deps"]]
 
-        def fits(c):
-            if c["sure"] > now and any(u["way"] > c["way"] and u["can"] < c["sure"] + c["hold"] for u in mine):
-                return False
-            held = [u for u in mine if u["way"] > c["way"] and u["can"] < c["end"]]
-            return all(c["end"] + u["way"] - bound <= YIELD[q] * (u["can"] - c["can"]) for u in held)
+    def arrange(ahead, margin, give):
+        free = {q: 0.0 for q in "vatpsn"}
+        left = [len(c["deps"]) for c in calls]
+        ready = [i for i, n in enumerate(left) if n == 0]
+        order = []
+        todo = list(range(len(calls)))
+        while ready:
+            for i in todo:
+                c = calls[i]
+                c["can"] = max([free[c["q"]]] + [d["end"] + t for d, t, _ in c["in"]])
+                c["end"] = c["can"] + c["hold"]
+            bound = max(calls[i]["can"] + calls[i]["way"] for i in todo)
+            soon = calls[min(ready, key=lambda i: calls[i]["can"])]
+            q, now = soon["q"], soon["can"]
+            mine = [calls[i] for i in todo if calls[i]["q"] == q and calls[i]["can"] < now + 1.5]
 
-        good = [i for i in ready if calls[i]["q"] == q and calls[i]["can"] <= now + AHEAD and fits(calls[i])]
-        if todo[0] < loads:
-            good, q = todo[:1], calls[todo[0]]["q"]
-        if not good:
-            free[q] = now + AHEAD
-            continue
-        i = max(good, key=lambda i: calls[i]["way"])
-        c = calls[i]
-        free[q] = c["end"]
-        order.append(i)
-        ready.remove(i)
-        todo.remove(i)
-        for u in users[i]:
-            left[u] -= 1
-            if left[u] == 0:
-                ready.append(u)
+            def fits(c):
+                sure = max([0.0] + [d["end"] + t + margin for d, t, other in c["in"] if other])
+                if sure > now and any(u["way"] > c["way"] and u["can"] < sure + c["hold"] for u in mine):
+                    return False
+                held = [u for u in mine if u["way"] > c["way"] and u["can"] < c["end"]]
+                return all(c["end"] + u["way"] - bound <= (FIRST if now < EARLY else give).get(q, 1.0) * (u["can"] - c["can"]) for u in held)
+
+            good = [i for i in ready if calls[i]["q"] == q and calls[i]["can"] <= now + ahead and fits(calls[i])]
+            if todo[0] < loads:
+                good, q = todo[:1], calls[todo[0]]["q"]
+            if not good:
+                free[q] = now + ahead
+                continue
+            i = max(good, key=lambda i: calls[i]["way"])
+            free[q] = calls[i]["end"]
+            order.append(i)
+            ready.remove(i)
+            todo.remove(i)
+            for u in users[i]:
+                left[u] -= 1
+                if left[u] == 0:
+                    ready.append(u)
+        return max(c["end"] + c["late"] for c in calls), order
+
+    order = [] if ORDER else min(arrange(*rule) for rule in RULES)[1]
 
     know = {q: {} for q in queue}
     ORDER.extend(order)

@@ -22,15 +22,18 @@ def _wrapped(buf, names, dtype):
 _sb("iot prow qrow murow mpr pmr pprow vrow drow flag mrow", C, "bfloat16")
 _sb("lrow", C + 16, "bfloat16")
 _sb("sums", 4 * C, "bfloat16")
-EG = "a"
-SPLIT = 0
-HOME = ()
 TILE = 3.5
-XV = 0
-PX = 1
-PA = 1
-PIECES = (3, 3, 1)
-_sb("pw2", 7 * C, "bfloat16")
+XLOAD = 450
+WCUT = 192
+W1 = 192
+CUT = 256
+PIECE = 128
+TABLES = ((0, 512, tuple(range(8))), (3968, C, tuple(range(0, 64, 8))), (7040, C, (0, 64, 128, "p", "p64", "p128")))
+ROW = {n: a + w * i for a, w, ns in TABLES for i, n in enumerate(ns) if n}
+_sb("pw2", 9344, "bfloat16")
+_sb("hf hm h0 h1 hdb th1 tg1", C, "bfloat16")
+_sb("hs gs th2 tg2", C + 32, "bfloat16")
+_sb("lv", C, "float16")
 _sb("ip order mk sf sr unit hh", 2 * C, "bfloat16")
 SLOTS = 16
 _sb("fr le k16", 2 * C, "float16")
@@ -39,8 +42,8 @@ _sb("k16f markp", C, "bfloat16")
 _sb("kseed", 32, "bfloat16")
 _sb("ssb smr shp ysb qr3 scf key0 key1 ka kb khd", C, "float32")
 _sb("idc", 2 * C, "float32")
-_sb("rsb mg", 4 * C, "float32")
-_sb("x0 xn xe z fo fp fa", 4 * C, "bfloat16")
+_sb("rsb rl3 mg", 4 * C, "float32")
+_sb("x0 xn xe z ze fo fp fa", 4 * C, "bfloat16")
 _sb("ssp", C, "float32")
 _sb("laid", 2 * C, "float32")
 _sb("ut vt ones", 512, "bfloat16")
@@ -52,24 +55,25 @@ _sb("us vs ups", 128, "uint8")
 _sb("tq0 tq1 tq2 tq3 lq1 lq2 lq3 zq1 zq2 zq3", C, "float8_e4m3fn_x4")
 _sb("ts0 ts1 ts2 ts3 lp1 lp2 lp3 zs1 zs2 zs3", C, "uint8")
 _sb("pli qli mli", 24, "int32")
-_sb("pi qi u8i", 8, "int32")
+_sb("pi qi q32 u8i", 8, "int32")
 _sb("j16", 16, "float32")
 _sb("c24i", 24, "int32")
 _sb("cols", 16, "float32")
 _sb("uoff", 8, "uint16")
 _sb("rl", 48, "uint16")
-_wrapped("wi", "kw loi di oi", "int32")
-_wrapped("wf", "cw pmc mupf pmpf ww2 wk hk lo_ hi_ mn gt idf f1 f3 f2 f4 sg a0 nz c0 c1 v0 v1 t0 t1 sp lw w1 w2 pos2 pos1 clf clr e0 g0 y0 gl tg hd_ h1", "float32")
-_wrapped("wl", "pw qw muw lpw hpw mupw pmpw idl piw uw lol vl spl p2l p1l opl el tl l2 l4 l8 l16 l32 l64 a1 a2 a3 m1 m2 m3", "uint16")
+_wrapped("wi", "kw di ei d0i d1i d2i d3i", "int32")
+_wrapped("wf", "cw pmc mupf pmpf ww2 wk hk lo_ hi_ mn gt idf f1 f3 f2 f4 sg a0 nz v0 v1 sp lw w1 pos2 pos1 clf clr e0 g0 y0 gl tg hd_ h2 "
+         "ep eq0 ep2 eq2 ev ne ng nw cur if0 d1f d2f d3f", "float32")
+_wrapped("wl", "pw qw muw lpw hpw mupw pmpw idl piw uw lol vl spl p2l p1l opl el tl ix l2 l4 l8 l16 l32 l64 a1 a2 a3 m1 m2 m3", "uint16")
 _wrapped("wr", "ra1 ra2 ra3 rm1 rm2 rm3", "uint16")
 _sb("pa pb", 2048, "float32", "psum")
-DMAS = ["dpl", "dql", "dml", "dx", "du_", "dv", "dwc", "dws", "doc0", "doc1", "dos0", "dos1", "dos2", "dos3", "dy0", "dy1", "dqo"]
+DMAS = ["dpl", "dql", "dml", "dx", "du_", "dv", "dwc", "dws", "doc0", "doc1", "dos0", "dos1", "dos2", "dos3", "dy0", "dy1", "dqo"] + ["did%d" % k for k in range(5)]
 SEMAPHORES = ["sv", "sa", "st", "sp", "ls"] + ["%s%d" % (k, s) for s in (1, 2, 3) for k in ("at", "aa", "am")] + DMAS
 
 CYC, GATHER, SCATTER, LEAST = 0.00095, 0.0015, 0.0036, 0.065
 SAME, CROSS = 0.18, 0.24
 RULES = [(ahead, margin, {"v": v, "a": a}) for ahead in (0.03, 0.06, 0.1) for margin in (0.2,) for v in (2.0, 10.0) for a in (0.1, 0.5)]
-EARLY, FIRST = 26.0, {"v": 0.3, "a": 0.1}
+EARLY, FIRST = 22.0, {"v": 4.0, "a": 0.3}
 LOAD, ISSUE, FLIGHT = 1.4, 0.5, 1.4
 ORDER = []
 
@@ -161,7 +165,7 @@ def rank_program(g, core, T, topo):
             if not n:
                 continue
             dst, src = T[out][:, o0 + a:o0 + b], w.indirect(T[buf][:, o + a // 16:o + b // 16])
-            regs = halves(out, o0) if n == C else [(out, o0 // H + (q == "a"))]
+            regs = halves(out, o0) if n == C else [halves(out, o0)[q == "a"]]
             if q == "a":
                 op("a", wreg + [lst], regs, 0.065 + n * GATHER, A.activation, dst, src, AF.Copy, **kw)
             elif kw:
@@ -169,8 +173,8 @@ def rank_program(g, core, T, topo):
             else:
                 op("v", wreg + [lst], regs, 0.05 + n * GATHER, V.tensor_copy, dst, src)
 
-    def halves(n, o0=0, k=2):
-        return [(n, o0 // H + i) for i in range(k)]
+    def halves(n, o0=0):
+        return [(n, (o0, 0)), (n, (o0, 1))]
 
     def fused(out, oreg, win, wreg, lst, o, in1, ireg):
         op("v", wreg + [lst] + ireg, oreg, 0.05 + C * GATHER, V.tensor_tensor, out, win.indirect(sl(lst)), in1, o)
@@ -211,13 +215,15 @@ def rank_program(g, core, T, topo):
     def bank(b, n=C):
         return T[b[0]][:, 512 * b[1]:512 * b[1] + n]
 
+    def power(n):
+        return T.pw2[:, ROW[n]:ROW[n] + C], halves("pw2", ROW[n])
+
     dma("s", "dpl", sl("pli"), T.pl[:, :], [], ["pli"], 12)
     dma("s", "dql", sl("qli"), T.ql[:, :], [], ["qli"], 12)
-    later = [len(calls) - 1]
-    dma("s", "dml", sl("mli"), T.ml[:, :], [], ["mli"], 200)
-    for sem, out, in_, name in (("dx", sl("x0"), T.x, "x0"), ("du_", sl("ut"), T.u, "ut"), ("dwc", T.wq[:, :].bitcast(dt.uint8), T.wc, "wq"),
-                                ("dws", sl("wsc"), T.ws, "wsc"), ("dv", sl("vt"), T.v, "vt")):
-        dma("s", sem, out, in_[:, :], [], [name], 1000 if name in ("x0", "ut") else 1600, later)
+    dma("s", "du_", sl("ut"), T.u[:, :], [], ["ut"], 200)
+    later = [dma("s", "dx", sl("x0"), T.x[:, :], [], ["x0"], XLOAD)]
+    for sem, out, in_, name in (("dml", sl("mli"), T.ml, "mli"), ("dwc", T.wq[:, :].bitcast(dt.uint8), T.wc, "wq"), ("dws", sl("wsc"), T.ws, "wsc"), ("dv", sl("vt"), T.v, "vt")):
+        dma("s", sem, out, in_[:, :], [], [name], 800, later)
 
     def iota(n, pattern, base, cm, cols, view=None):
         kw = {} if SCRATCH[n][2] == "int32" else {"allow_small_or_imprecise_dtypes": True}
@@ -235,7 +241,7 @@ def rank_program(g, core, T, topo):
     op("v", [], ["unit"], C * CYC, V.memset, sl("unit"), 2.0 ** -8)
     for b in range(4):
         op("p", ["ones"], [("et", b)], 0.17 + 1024 * CYC, P.affine_select, sl("et", b, 512), sl("ones"), [[-1, 512]], OP.is_equal, 0.0, b, 4)
-    quant("eq", "es", "et", n=512)
+        quant("eq", "es", "et", 128 * b, 128, b, [("et", b)])
 
     def col(i, in0, reg, s1, o0, s2=None, o1=None):
         if o1 is None:
@@ -252,6 +258,18 @@ def rank_program(g, core, T, topo):
     col(2, T.cols[:, 1:2], ("cols", 1), -352.0, OP.add)
     col(3, T.cols[:, 6:7], ("cols", 6), 511.0 + H, OP.add)
     col(8, T.cols[:, 1:2], ("cols", 1), -127.5, OP.add)
+    col(9, T.qi[:, 0:1], "qi", 8, OP.is_lt, 256.0, OP.mult)
+    col(10, T.qi[:, 0:1], "qi", 8, OP.is_ge, 256.0, OP.mult)
+    op("v", ["pi"], ["q32"], 0, V.tensor_scalar, T.q32[:, 0:1], T.pi[:, 0:1], 31, None, OP.bitwise_and)
+    col(11, T.q32[:, 0:1], "q32", 16, OP.is_lt, 512.0, OP.mult)
+    col(12, T.q32[:, 0:1], "q32", 16, OP.is_ge, -512.0, OP.mult)
+    for n in ("hs", "gs"):
+        for a in (0, C + 16):
+            op("v", [], [(n, "end%d" % a)], 0, V.memset, T[n][:, a:a + 16], 0.0)
+    for k, (a, w, ns) in enumerate(TABLES):
+        dma("s", "did%d" % k, T.pw2[:, a:a + C], sl("iot"), ["iot"], halves("pw2", a), 400)
+    for a in range(C, 7 * 512, 512):
+        copy_a(T.pw2[:, a:a + 512 - C], ["iot"], [("pw2", a)], T.iot[:, 0:512 - C], n=128)
     op("v", [], [("sums", 3)], H * CYC, V.memset, T.sums[:, 3:4 * C:4], 0.0)
     op("v", [], [("lrow", 0)], 0, V.memset, T.lrow[:, 0:1], 0.0)
     op("v", [], [("cols", 7)], 0, V.memset, T.cols[:, 7:8], 2.0 ** -100)
@@ -275,17 +293,18 @@ def rank_program(g, core, T, topo):
     vcopy("qw", "qli")
     vcopy("muw", "mli")
     gath("av", "qrow", "iot", "qw")
-    gath("av", "pw2", "qrow", "pw")
+    gath("av", "pw2", "qrow", "pw", o0=ROW[1])
     gath("a", "prow", "iot", "pw")
     copy_a(sl("ip", 0), ["iot"], [("ip", 0)], sl("iot"))
     copy_a(sl("ip", 1), ["prow"], [("ip", 1)], sl("prow"))
+    dma("s", "did4", power("p")[0], sl("prow"), ["prow"], power("p")[1], 400)
     small("pmc", "pli", OP.subtract, "cw")
     small("mn", "pli", OP.min, "cw")
     ts("gt", "pmc", 0.0, OP.is_lt, float(C), OP.mult)
     small("idf", "mn", OP.add, "gt")
     vcopy("idl", "idf")
     gath("a", "key0", "idc", "idl", bias=float(H))
-    gath("v", "key1", "idc", "idl", scale=1.0, bias=H - 1.0)
+    copy_a(sl("key1"), ["key0"], ["key1"], sl("key0"), bias=-1.0)
     gath("a", "murow", "iot", "muw")
     gath("a", "mpr", "murow", "pw")
     rowlist(sl("mpr"), ["mpr"], "mupf")
@@ -301,36 +320,80 @@ def rank_program(g, core, T, topo):
     op("v", ["ww2", ("cols", 6)], ["wk"], 0, V.tensor_scalar, sl("wk"), sl("ww2"), T.cols[:, 6:7], None, OP.mult)
     small("wk", "wk", OP.add, "cw")
 
-    def power(i):
-        return sl("pw2", i), halves("pw2", C * i)
+    def times(how, to, n, lst):
+        gath(how, "pw2", "pw2", lst, o0=ROW[to], wreg=power(n)[1], wcols=(ROW[n], ROW[n] + C))
 
-    def lay_out(s):
+    def powers(s):
         a = "a%d" % s
-        rowlist(*power(0), a)
+        rowlist(*power(1), a)
         gath("a", "hh", "prow", a)
         gath("a", "hh", "hh", "pmpw", o0=C, wreg=halves("hh"), wcols=(0, C))
         cv, stay, swap = pick(sl("hh"), ["hh"], 2 * C)
         op("v", [cv], ["hd_"], 0, V.tensor_tensor, sl("hd_"), swap, stay, OP.subtract)
-        op("v", ["hd_", ("cols", 6), ("cols", 0)], ["h1"], 0, V.tensor_scalar, sl("h1"), sl("hd_"), T.cols[:, 6:7], T.cols[:, 0:1], OP.mult, OP.add)
-        op("v", [cv, "h1"], ["hk"], 0, V.tensor_tensor, sl("hk"), stay, sl("h1"), OP.add)
-        cur, hd = "key0", "key1"
+        op("v", ["hd_", ("cols", 6), ("cols", 0)], ["h2"], 0, V.tensor_scalar, sl("h2"), sl("hd_"), T.cols[:, 6:7], T.cols[:, 0:1], OP.mult, OP.add)
+        op("v", [cv, "h2"], ["hk"], 0, V.tensor_tensor, sl("hk"), stay, sl("h2"), OP.add)
+        for n in STEPS[:6]:
+            times("aav" if n == 32 else "a", 2 * n, n, a if n == 1 else "l%d" % n)
+            rowlist(*power(2 * n), "l%d" % (2 * n))
+
+    def walk(s, cur, hd, pair, spare, last=None):
         for i, n in enumerate(STEPS):
-            lst = a if n == 1 else "l%d" % n
-            if i < 6:
-                gath("aav" if s == 1 or i > 4 else "a", "pw2", "pw2", lst, o0=C * (i + 1), wreg=power(i)[1], wcols=(C * i, C * i + C))
-                rowlist(*power(i + 1), "l%d" % (2 * n))
-            nxt, o = "kb" if cur == "ka" else "ka", AT[lst][1]
-            if i < SPLIT:
-                if i:
-                    hd = "khd"
-                    copy_a(sl(hd), [cur], [hd], sl(cur), bias=float(-n))
-                fused(sl(nxt), [nxt], sl(cur), [cur], lst, OP.min, sl(hd), [hd])
-            for k in range(2 if i >= SPLIT else 0):
-                if i:
-                    hd = "khd"
-                    copy_a(sl(hd, k, H), [(cur, k)], [(hd, k)], sl(cur, k, H), n=H, bias=float(-n))
-                op("v", [cur, lst, (hd, k)], [(nxt, k)], 0.05 + H * GATHER, V.tensor_tensor, sl(nxt, k, H), sl(cur).indirect(T.wl[:, o + 12 * k:o + 12 * k + 12]), sl(hd, k, H), OP.min)
+            lst = "a%d" % s if n == 1 else "l%d" % n
+            nxt, o = pair[cur == pair[0]], AT[lst][1]
+            for k, (a, e) in enumerate(((0, W1 if last else WCUT), (W1 if last else WCUT, C))):
+                near = spare if i or not hd else hd
+                if near == spare and last:
+                    op("v", [(cur, k) if i else cur], [(spare, k)], (e - a) * CYC / 2, V.tensor_scalar, T[spare][:, a:e], T[cur][:, a:e], float(-n), None, OP.add)
+                elif near == spare:
+                    copy_a(T[spare][:, a:e], [(cur, k) if i else cur], [(spare, k)], T[cur][:, a:e], n=e - a, bias=float(-n))
+                out, reg = (T[last][:, 16 + a:16 + e], (last, k)) if last and i == 7 else (T[nxt][:, a:e], (nxt, k))
+                op("v", [cur, lst, (near, k) if near == spare else near], [reg], 0.05 + (e - a) * GATHER, V.tensor_tensor, out,
+                   sl(cur).indirect(T.wl[:, o + a // 16:o + e // 16]), T[near][:, a:e], OP.min)
             cur = nxt
+        return cur
+
+    def first_mirror():
+        for n, c in (("hm", 10), ("hf", 9)):
+            op("v", [("cols", c)], [n, ("pb", 0)], C * CYC, V.tensor_scalar, sl(n), bank(("pb", 0)), 0.0, T.cols[:, c:c + 1], OP.is_ge, OP.mult)
+        fused(sl("h0"), ["h0"], sl("hm"), ["hm"], "pw", OP.add, sl("hf"), ["hf"])
+        walk(1, "h0", None, ("h0", "h1"), "hdb", "hs")
+        for to, n, lst in ((3, 1, "l2"), (5, 1, "l4"), (6, 2, "l4"), (7, 3, "l4"), (24, 8, "l16"), (40, 8, "l32"), (48, 16, "l32"), (56, 24, "l32"),
+                           (128, 64, "l64"), ("p64", "p", "l64"), ("p128", "p64", "l64")):
+            times("a", to, n, lst)
+        gath("av", "gs", "hs", "pw", o0=16, wcols=(16, 16 + C))
+        for n in ("h", "g"):
+            op("v", [n + "s"], ["t%s1" % n], H * CYC, V.transpose, sl("t%s1" % n), T[n + "s"][:, 16:16 + C])
+            op("v", [n + "s"], ["t%s2" % n], H * CYC, V.transpose, sl("t%s2" % n), sl(n + "s"))
+        for out, k, t, a in (("ep", 0, "1", 0), ("eq0", 1, "1", 16), ("eq0", 0, "2", 16), ("ep", 1, "2", 32)):
+            o = AT[out][1]
+            op("v", ["th" + t, "tg" + t], [(out, k)], 0, V.tensor_tensor, T.wf[:, o + k:o + 24:2], T["th" + t][:, a:a + 353:32], T["tg" + t][:, a + 8:a + 361:32], OP.subtract)
+        for out, src, c in (("ep2", "ep", 11), ("eq2", "eq0", 12)):
+            op("v", [src, ("cols", c)], [out], 0, V.tensor_scalar, sl(out), sl(src), T.cols[:, c:c + 1], None, OP.mult)
+        small("ev", "ep2", OP.subtract, "eq2")
+        small("ne", "eq2", OP.subtract, "ep2")
+        small("ei", "ev", OP.max, "ne")
+        small("ng", "ep2", OP.is_lt, "eq2")
+        small("nw", "ng", OP.mult, "pmc")
+        small("cur", "nw", OP.add, "cw")
+        ts("d0i", "ei", 7 * 512, OP.bitwise_and)
+        small("if0", "d0i", OP.add, "cur")
+        vcopy("ix", "if0")
+        for k in (1, 2):
+            ts("d%di" % k, "ei", 3 * k, OP.logical_shift_right, 7 * 512, OP.bitwise_and)
+            op("v", ["d%di" % k, ("cols", 0)], ["d%df" % k], 0, V.tensor_scalar, sl("d%df" % k), sl("d%di" % k), 0.75, T.cols[:, 0:1], OP.mult, OP.add)
+        ts("nw", "ng", 3.0 * C, OP.mult)
+        small("d2f", "d2f", OP.add, "nw")
+        for k, (a, w, ns) in enumerate(TABLES):
+            gath("av", "lv", "pw2", "ix", wreg=[r for i in range(len(ns)) for r in halves("pw2", a + w * i)] + [("pw2", i) for i in range(C, 7 * 512, 512)], wcols=(a, a + w * (len(ns) - 1) + C))
+            if k == 2:
+                return rowlist(sl("lv"), ["lv"], "m1")
+            cv, got, _ = pick(sl("lv"), ["lv"])
+            op("v", [cv, "d%df" % (k + 1)], ["if0"], 0, V.tensor_tensor, sl("if0"), got, sl("d%df" % (k + 1)), OP.add)
+            vcopy("ix", "if0")
+
+    def lay_out(s):
+        a = "a%d" % s
+        cur = walk(s, "key0", "key1", ("ka", "kb"), "khd")
         op("v", [cur, "k16f"], ["scf"], C * CYC, V.tensor_tensor_scan, sl("scf"), sl("k16f"), sl(cur), 0.0, OP.add, OP.min)
         op("v", ["scf", ("cols", 1)], ["kw"], 0, V.tensor_scalar, sl("kw"), T.scf[:, 15:C:16], T.cols[:, 1:2], None, OP.add)
         op("v", ["scf", ("cols", 2)], ["lol"], 0, V.tensor_scalar, sl("lol"), T.scf[:, 15:C:16], T.cols[:, 2:3], 2.0 ** -10, OP.add, OP.mult)
@@ -341,8 +404,8 @@ def rank_program(g, core, T, topo):
         for k, (d0, d1) in enumerate(((last, last), (now, last), (now, now))):
             op("v", ["lrow"], [("sums", k)], H * CYC, V.tensor_tensor_scan, T.sums[:, k:4 * C:4], d0, d1, -float(H), OP.add, OP.add)
         op("v", ["scf", ("cols", 8)], ["el"], 0, V.tensor_scalar, sl("el"), T.scf[:, 15:C:16], T.cols[:, 8:9], 2.0 ** -8, OP.add, OP.mult)
-        gath("av" if s == 1 else "a", "le", "sums", "el")
-        gath("av" if s == 1 else "a", "le", "drow", "lol", o0=C)
+        gath("a", "le", "sums", "el")
+        gath("a", "le", "drow", "lol", o0=C)
         ts("v0", "di", 511.0, OP.is_ge, float(C), OP.mult)
         small("v1", "v0", OP.add, "cw")
         vcopy("vl", "v1")
@@ -384,8 +447,8 @@ def rank_program(g, core, T, topo):
         rowlist(sl("mrow"), ["mrow"], mw)
 
     def conjugate(mw):
-        if mw == "m3":
-            gath("v", "smr", "ssb", mw)
+        if mw != "m2":
+            gath("v" if mw == "m3" else "av", "smr", "ssb", mw)
         else:
             gath("a", "ssp", "ssb", "pw")
             gath("a", "laid", "ssb", "opl")
@@ -401,7 +464,7 @@ def rank_program(g, core, T, topo):
         op("v", ["f2", "f4"], ["piw", "uw"], 0, V.tensor_copy, two("piw"), two("f2"))
         how = "a" if mw == "m3" else "av"
         gath(how, "pprow", "prow", "piw")
-        gath(how, "pw2", "pprow", "uw")
+        gath(how, "pw2", "pprow", "uw", o0=ROW[1])
 
     steps = T.tables["STEP"] if "STEP" in T.tables else [1, 2, 3]
     for s in (1, 2, 3):
@@ -409,74 +472,64 @@ def rank_program(g, core, T, topo):
         ne = len(topo.engines(core, dst))
         tq, tsn, lq, lp = "tq%d" % (s - 1), "ts%d" % (s - 1), "lq%d" % s, "lp%d" % s
         mw, rm, ra, zq, zs = "m%d" % s, "rm%d" % s, "ra%d" % s, "zq%d" % s, "zs%d" % s
-        lengths = lay_out(s)
-        home = s in HOME
-
-        def tile_over(q, sc):
-            both = [send(dst, "at%d" % s, T[lq][:, :].bitcast(dt.uint8), T[q][:, :].bitcast(dt.uint8), [q], s == 1 and home), send(dst, "at%d" % s, sl(lp), sl(sc), [sc])]
-            arrive("at%d" % s, 2 * ne, [lq, lp], both, FLIGHT + TILE)
-
-        if not home:
-            arrive("aa%d" % s, ne, [ra], [send(dst, "aa%d" % s, sl(ra), sl("a%d" % s), ["a%d" % s], s == 1)], FLIGHT + 0.8)
+        powers(s)
+        arrive("aa%d" % s, ne, [ra], [send(dst, "aa%d" % s, sl(ra), sl("a%d" % s), ["a%d" % s], s == 1)], FLIGHT + 0.8)
         quant(tq, tsn, "x0" if s == 1 else "xn")
         mm(("pb", 0), "up", "ups", 0, tq, tsn)
-        if not home:
-            tile_over(tq, tsn)
+        both = [send(dst, "at%d" % s, T[lq][:, :].bitcast(dt.uint8), T[tq][:, :].bitcast(dt.uint8), [tq]), send(dst, "at%d" % s, sl(lp), sl(tsn), [tsn])]
+        arrive("at%d" % s, 2 * ne, [lq, lp], both, FLIGHT + TILE)
+        if s == 1:
+            first_mirror()
         copy_a(sl("ssb"), [], ["ssb", ("pb", 0)], bank(("pb", 0)))
-        op("a", ["ssb", "pw", ("cols", 7)], ["markp"], 0.065 + C * GATHER, A.activation, sl("markp"), sl("ssb").indirect(sl("pw")), AF.Sign, bias=T.cols[:, 7:8])
+        if s > 1:
+            op("a", ["ssb", "pw", ("cols", 7)], ["markp"], 0.065 + C * GATHER, A.activation, sl("markp"), sl("ssb").indirect(sl("pw")), AF.Sign, bias=T.cols[:, 7:8])
+            mirror(mw, *lay_out(s))
         for b in range(4):
             mm(("pa", b), "eq", "es", 128 * b, tq, tsn)
-            if s == 3 or b < XV:
+            if s == 3:
                 copy_a(sl("fo", b), [], [("fo", b), ("pa", b)], bank(("pa", b)))
         for b in (1, 2, 3, 0):
-            src = ("pa" if home else "pb", b)
-            if not home:
-                mm(src, "eq", "es", 128 * b, lq, lp)
-            copy_a(sl("fp", b), [], [("fp", b), src], bank(src), scale=0.5)
-            gath("a", "fa", "fp", "a%d" % s if home else ra, o0=C * b, wreg=[("fp", b)], wcols=(C * b, C * b + C))
-        mirror(mw, *lengths)
-        if not home:
-            arrive("am%d" % s, ne, [rm], [send(dst, "am%d" % s, sl(rm), sl(mw), [mw])], FLIGHT + (0.8 if s < 3 else 0.1))
+            mm(("pb", b), "eq", "es", 128 * b, lq, lp)
+            copy_a(sl("fp", b), [], [("fp", b), ("pb", b)], bank(("pb", b)), scale=0.5)
+            gath("a", "fa", "fp", ra, o0=C * b, wreg=[("fp", b)], wcols=(C * b, C * b + C))
+        arrive("am%d" % s, ne, [rm], [send(dst, "am%d" % s, sl(rm), sl(mw), [mw])], FLIGHT + (0.8 if s < 3 else 0.1))
         conjugate(mw)
+        if s == 3:
+            break
+        o = AT[rm][1]
         for b in range(4):
-            buf, o = AT[mw if home else rm]
-            n = C // PIECES[s - 1]
-            for a in range(0, C, n):
-                op("v", [("fp", b), mw if home else rm] + halves("fa", C * b), [("z", (b, a))], 0.05 + n * GATHER, V.tensor_tensor, T.z[:, 4 * a + b:4 * (a + n):4],
-                   sl("fp", b).indirect(T[buf][:, o + a // 16:o + (a + n) // 16]), T.fa[:, C * b + a:C * b + a + n], OP.add)
+            for a in range(0, C, PIECE):
+                e = a + PIECE
+                op("v", [("fp", b), rm] + halves("fa", C * b), [("z", (b, a))], 0.05 + PIECE * GATHER, V.tensor_tensor, T.z[:, 4 * a + b:4 * e:4],
+                   sl("fp", b).indirect(T.wr[:, o + a // 16:o + e // 16]), T.fa[:, C * b + a:C * b + e], OP.add)
         quant(zq, zs, "z")
-        if home:
-            tile_over(zq, zs)
-            zq, zs = lq, lp
         for b in range(4):
             mm(("pb", b), "wq", "wsc", 128 * b, zq, zs)
             copy_a(sl("rsb", b), [], [("rsb", b), ("pb", b)], bank(("pb", b)), scale=0.03125)
-            if s < 3 and b < XV:
-                o, n = AT[mw][1], C // PX
-                for a in range(0, C, n):
-                    op("v", [("rsb", b), mw, ("fo", b)], [("xn", (b, a))], 0.05 + n * GATHER, V.tensor_tensor, T.xn[:, 4 * a + b:4 * (a + n):4],
-                       sl("rsb", b).indirect(T.wl[:, o + a // 16:o + (a + n) // 16]), T.fo[:, C * b + a:C * b + a + n], OP.add)
-            elif s < 3:
-                o, n = AT[mw][1], C // PX
-                for a in range(0, C, n):
-                    op("a", [("rsb", b), mw], [("mg", (b, a))], 0.065 + n * GATHER, A.activation, T.mg[:, C * b + a:C * b + a + n],
-                       sl("rsb", b).indirect(T.wl[:, o + a // 16:o + (a + n) // 16]), AF.Copy)
-                m = C // PA
-                for a in range(0, C, m):
-                    op("v", [("mg", (b, k)) for k in range(0, C, n) if k < a + m and a < k + n], [("xn", (b, a)), ("pa", b)], m * CYC, V.tensor_tensor,
-                       T.xn[:, 4 * a + b:4 * (a + m):4], T.pa[:, 512 * b + a:512 * b + a + m], T.mg[:, C * b + a:C * b + a + m], OP.add)
-    gath("a", "qr3", "pw2", "pw", wreg=power(0)[1], wcols=(0, C), bias=float(H))
+            gath("a", "mg", "rsb", mw, o0=C * b, wreg=[("rsb", b)], wcols=(C * b, C * b + C))
+            op("v", halves("mg", C * b), [("xn", b), ("pa", b)], C * CYC, V.tensor_tensor, T.xn[:, b:4 * C:4], bank(("pa", b)), sl("mg", b), OP.add)
+    gath("a", "qr3", "pw2", "pw", wreg=power(1)[1], wcols=(ROW[1], ROW[1] + C), bias=float(H))
     dma("s", "dqo", T.qo[:, :], T.qr3[0:128:16, :], ["qr3"], [], 12)
-    o = AT["m3"][1]
-    for k in range(2):
+    o = AT["rm3"][1]
+    for k, (a, e) in enumerate(((0, CUT), (CUT, C))):
+        for b in (1, 2, 3, 0):
+            op("v", [("fp", b), "rm3"] + halves("fa", C * b), [("ze", (b, k))], 0.05 + (e - a) * GATHER, V.tensor_tensor, T.ze[:, 4 * a + b:4 * e:4],
+               sl("fp", b).indirect(T.wr[:, o + a // 16:o + e // 16]), T.fa[:, C * b + a:C * b + e], OP.add)
+        quant("zq3", "zs3", "ze", a, e - a, k, [("ze", (b, k)) for b in range(4)])
         for b in range(4):
-            op("v", [("rsb", b), "m3", ("fo", b)], [("xe", 4 * k + b)], 0.05 + H * GATHER, V.tensor_tensor, T.xe[:, 4 * H * k + b:4 * H * (k + 1):4],
-               sl("rsb", b).indirect(T.wl[:, o + 12 * k:o + 12 * k + 12]), T.fo[:, C * b + H * k:C * b + H * k + H], OP.add)
-        quant("tq3", "ts3", "xe", H * k, H, k, [("xe", 4 * k + b) for b in range(4)])
-        mm(("pa", k), "vq", "vs", 0, "tq3", "ts3", H * k, H, k)
-        copy_a(T.ysb[:, H * k:H * k + H], [], [("ysb", k), ("pa", k)], bank(("pa", k), H), n=H)
-        dma("a" if k else "s", "dy%d" % k, T.y[:, H * k:H * k + H], T.ysb[:, H * k:H * k + H], [("ysb", k)], [], 400 - 300 * k)
-        dma("s", "doc%d" % k, T.oc[:, 4 * H * k:4 * H * (k + 1)], sl("tq3", k, H).bitcast(dt.uint8), [("tq3", k)], [], 400 - 300 * k)
+            at = ("pa" if k else "pb", b)
+            mm(at, "wq", "wsc", 128 * b, "zq3", "zs3", a, e - a, k)
+            copy_a(T.rl3[:, C * b + a:C * b + e], [], [("rl3", (b, k)), at], bank(at, e - a), n=e - a, scale=0.03125)
+    o = AT["m3"][1]
+    for k, (a, e) in enumerate(((0, CUT), (CUT, C))):
+        for b in range(4):
+            op("v", [("rl3", (b, 0)), ("rl3", (b, 1)), "m3", ("fo", b)], [("xe", 4 * k + b)], 0.05 + (e - a) * GATHER, V.tensor_tensor, T.xe[:, 4 * a + b:4 * e:4],
+               sl("rl3", b).indirect(T.wl[:, o + a // 16:o + e // 16]), T.fo[:, C * b + a:C * b + e], OP.add)
+        quant("tq3", "ts3", "xe", a, e - a, k, [("xe", 4 * k + b) for b in range(4)])
+        mm(("pb", k), "vq", "vs", 0, "tq3", "ts3", a, e - a, k)
+        copy_a(T.ysb[:, a:e], [], [("ysb", k), ("pb", k)], bank(("pb", k), e - a), n=e - a)
+        dma("a" if k else "s", "dy%d" % k, T.y[:, a:e], T.ysb[:, a:e], [("ysb", k)], [], 500 - 400 * k)
+        dma("s", "doc%d" % k, T.oc[:, 4 * a:4 * e], T.tq3[:, a:e].bitcast(dt.uint8), [("tq3", k)], [], 500 - 400 * k)
     for k in range(4):
         dma("s", "dos%d" % k, T.osc[4 * k:4 * k + 4, 0:C], T.ts3[32 * k:32 * k + 4, 0:C], ["ts3"], [], 2)
 

@@ -1,8 +1,14 @@
+import numpy as np
 from concourse.mybir import dt, AluOpType as OP, ActivationFunctionType as AF
 
 C = 384
 H = C // 2
+U = 2.0 ** -7
+SIDE = 703
 STEPS = (1, 2, 4, 8, 16, 32, 64, 64)
+RUNS = ((0, 256), (256, C))
+SHARED = (2, 3)
+PIECE = 128
 SCRATCH = {}
 AT = {}
 
@@ -19,34 +25,24 @@ def _wrapped(buf, names, dtype):
     _sb(buf, 24 * len(names), dtype)
 
 
-_sb("iot prow qrow murow mpr pmr pprow vrow drow flag mrow", C, "bfloat16")
-_sb("lrow", C + 16, "bfloat16")
-_sb("sums", 4 * C, "bfloat16")
-TILE = 3.5
-XLOAD = 450
-WCUT = 192
-W1 = 192
-CUT = 256
-PIECE = 128
 TABLES = ((0, 512, tuple(range(8))), (3968, C, tuple(range(0, 64, 8))), (7040, C, (0, 64, 128, "p", "p64", "p128")))
 ROW = {n: a + w * i for a, w, ns in TABLES for i, n in enumerate(ns) if n}
-_sb("pw2", 9344, "bfloat16")
-_sb("hf hm h0 h1 hdb th1 tg1", C, "bfloat16")
-_sb("hs gs th2 tg2", C + 32, "bfloat16")
-_sb("lv", C, "float16")
-_sb("ip order mk sf sr unit hh", 2 * C, "bfloat16")
 SLOTS = 16
-_sb("fr le k16", 2 * C, "float16")
+_sb("pw2", 9344, "bfloat16")
+_sb("iot prow qrow murow pmr drow mrow vrow markp k16f hf hm h0 h1 hdb th1 tg1", C, "bfloat16")
+_sb("hs gs th2 tg2", C + 32, "bfloat16")
+_sb("lrow", C + 16, "bfloat16")
+_sb("hh fq tau ip order mk sf sr unit", 2 * C, "bfloat16")
+_sb("sums", 2 * C + 16, "bfloat16")
+_sb("lv", C, "float16")
+_sb("dl k16 fr le", 2 * C, "float16")
 _sb("sc", SLOTS * 2 * C, "float16")
-_sb("k16f markp", C, "bfloat16")
 _sb("kseed", 32, "bfloat16")
-_sb("ssb smr shp ysb qr3 scf key0 key1 ka kb khd", C, "float32")
-_sb("idc", 2 * C, "float32")
+_sb("ssb ssp smr shp ysb qr3 scf key0 key1 ka kb khd", C, "float32")
+_sb("idc laid", 2 * C, "float32")
 _sb("rsb rl3 mg", 4 * C, "float32")
 _sb("x0 xn xe z ze fo fp fa", 4 * C, "bfloat16")
-_sb("ssp", C, "float32")
-_sb("laid", 2 * C, "float32")
-_sb("ut vt ones", 512, "bfloat16")
+_sb("ut vt", 512, "bfloat16")
 _sb("et", 2048, "bfloat16")
 _sb("eq wq", 512, "float8_e4m3fn_x4")
 _sb("es wsc", 512, "uint8")
@@ -54,27 +50,27 @@ _sb("uq vq up", 128, "float8_e4m3fn_x4")
 _sb("us vs ups", 128, "uint8")
 _sb("tq0 tq1 tq2 tq3 lq1 lq2 lq3 zq1 zq2 zq3", C, "float8_e4m3fn_x4")
 _sb("ts0 ts1 ts2 ts3 lp1 lp2 lp3 zs1 zs2 zs3", C, "uint8")
-_sb("pli qli mli", 24, "int32")
+_sb("pli qli mli c24i", 24, "int32")
 _sb("pi qi q32 u8i", 8, "int32")
-_sb("j16", 16, "float32")
-_sb("c24i", 24, "int32")
-_sb("cols", 16, "float32")
+_sb("j16 cols", 16, "float32")
 _sb("uoff", 8, "uint16")
 _sb("rl", 48, "uint16")
-_wrapped("wi", "kw di ei d0i d1i d2i d3i", "int32")
-_wrapped("wf", "cw pmc mupf pmpf ww2 wk hk lo_ hi_ mn gt idf f1 f3 f2 f4 sg a0 nz v0 v1 sp lw w1 pos2 pos1 clf clr e0 g0 y0 gl tg hd_ h2 "
-         "ep eq0 ep2 eq2 ev ne ng nw cur if0 d1f d2f d3f", "float32")
-_wrapped("wl", "pw qw muw lpw hpw mupw pmpw idl piw uw lol vl spl p2l p1l opl el tl ix l2 l4 l8 l16 l32 l64 a1 a2 a3 m1 m2 m3", "uint16")
+_wrapped("wi", "kw di ei d0i d1i d2i", "int32")
+_wrapped("wf", "cw pmc mupf lo_ hi_ mn gt idf k1 k2 hk f1 f3 f2 f4 hd_ h2 sg a0 v0 v1 sp lw w1 pos2 pos1 clf clr e0 g0 y0 gl tg "
+         "ep eq0 ep2 eq2 ev ne ng nw cur if0 d1f d2f", "float32")
+_wrapped("wl", "pw qw muw lpw hpw mupw pmpw idl uw lol vl spl p2l p1l el opl tl ix l2 l4 l8 l16 l32 l64 a1 a2 a3 m1 m2 m3", "uint16")
 _wrapped("wr", "ra1 ra2 ra3 rm1 rm2 rm3", "uint16")
 _sb("pa pb", 2048, "float32", "psum")
 DMAS = ["dpl", "dql", "dml", "dx", "du_", "dv", "dwc", "dws", "doc0", "doc1", "dos0", "dos1", "dos2", "dos3", "dy0", "dy1", "dqo"] + ["did%d" % k for k in range(5)]
 SEMAPHORES = ["sv", "sa", "st", "sp", "ls"] + ["%s%d" % (k, s) for s in (1, 2, 3) for k in ("at", "aa", "am")] + DMAS
 
-CYC, GATHER, SCATTER, LEAST = 0.00095, 0.0015, 0.0036, 0.065
-SAME, CROSS = 0.18, 0.24
-RULES = [(ahead, margin, {"v": v, "a": a}) for ahead in (0.03, 0.06, 0.1) for margin in (0.2,) for v in (2.0, 10.0) for a in (0.1, 0.5)]
+CYC, GATHER, SCATTER, LEAST, PE = [np.array(v) for v in ((0.00095, 0.00083, 0.0012), (0.0015, 0.0013, 0.0023), (0.0036, 0.0032, 0.006), (0.065, 0.054, 0.075), (0.00125, 0.00125, 0.0016))]
+SAME, CROSS = (0.18, 0.15, 0.18), (0.24, 0.21, 0.24)
+LOAD, RATE, ISSUE, FLIGHT, LIST, LAST = 1.5, 185.0, 0.5, 1.4, 0.8, np.array((0.1, 0.6, 0.6))
+TILE, COLD = np.array((3.5, 4.0, 6.0)), 6.0
+RULES = [(ahead, margin, {"v": v, "a": a}) for ahead in (0.03, 0.06, 0.1) for margin in (0.1, 0.2) for v, a in ((2.0, 0.1), (10.0, 0.5))]
 EARLY, FIRST = 22.0, {"v": 4.0, "a": 0.3}
-LOAD, ISSUE, FLIGHT = 1.4, 0.5, 1.4
+ROUNDS, REACH = (150, 1500), 5
 ORDER = []
 
 
@@ -102,7 +98,8 @@ def rank_program(g, core, T, topo):
             for rs in meets(n, p, readers):
                 deps.update(rs)
         me = len(calls)
-        calls.append({"q": q, "deps": sorted(deps), "hold": hold, "late": late, "emit": emit})
+        hold, late = [[float(x) for x in v + np.zeros(3)] for v in (hold, late)]
+        calls.append({"q": q, "deps": sorted(deps), "hold": hold[0], "late": late[0], "holds": hold, "lates": late, "emit": emit})
         for n, p in reads:
             readers.setdefault(n, {}).setdefault(p, []).append(me)
         for n, p in writes:
@@ -116,19 +113,20 @@ def rank_program(g, core, T, topo):
 
     count = {"sv": 0, "sa": 0, "st": 0, "sp": 0}
 
-    def op(q, reads, writes, hold, call, *args, **kw):
+    def op(q, reads, writes, hold, call, *args, after=(), **kw):
         def emit():
             count[own[q]] += 1
             call(*args, **kw).then_inc(T.sem[own[q]], 1)
             return own[q], count[own[q]]
-        return add(q, reads, writes, max(hold, LEAST), 0.0, emit)
+        return add(q, reads, writes, np.maximum(hold, LEAST), 0.0, emit, after)
 
-    def dma(q, sem, out, in_, reads, writes, kib, after=(), **kw):
+    def dma(q, sem, out, in_, reads, writes, kib, after=()):
         def emit():
             count[sem] = 16
-            queue[q].dma_start(out, in_, **kw).then_inc(T.sem[sem], 16)
+            queue[q].dma_start(out, in_).then_inc(T.sem[sem], 16)
             return sem, 16
-        return add(q, reads, writes, ISSUE if q == "p" else 0.1, LOAD + kib / 190.0, emit, after)
+        first = add(q, reads, writes, 0.1, LOAD, emit, after)
+        return add("d", reads, writes, kib / RATE, 0.0, lambda: (sem, 16), [first])
 
     sent = [0]
 
@@ -151,27 +149,20 @@ def rank_program(g, core, T, topo):
             return T[buf][:, o:o + 24]
         return T[n][:, :] if i is None else T[n][:, w * i:w * i + w]
 
-    def two(n):
+    def run(n, a, e):
         buf, o = AT[n]
-        return T[buf][:, o:o + 48]
+        return T[buf][:, o + a // 16:o + e // 16]
 
-    def gath(how, out, win, lst, o0=0, wreg=None, oreg=None, wcols=None, **kw):
-        buf, o = AT[lst]
+    def gath(how, out, win, lst, o0=0, wreg=None, wcols=None, **kw):
         w = T[win][:, wcols[0]:wcols[1]] if wcols else sl(win)
-        wreg = wreg or [win]
-        cut = {"a": 0, "v": C, "av": H, "aav": 128}[how]
-        for q, a, b in (("v", 0, cut), ("a", cut, C)):
-            n = b - a
-            if not n:
-                continue
-            dst, src = T[out][:, o0 + a:o0 + b], w.indirect(T[buf][:, o + a // 16:o + b // 16])
-            regs = halves(out, o0) if n == C else [halves(out, o0)[q == "a"]]
+        n = C // len(how)
+        for k, q in enumerate(how[::-1]):
+            dst, src = T[out][:, o0 + n * k:o0 + n * k + n], w.indirect(run(lst, n * k, n * k + n))
+            reads, regs = (wreg or [win]) + [lst if n == C else (lst, k)], halves(out, o0) if n == C else [halves(out, o0)[k]]
             if q == "a":
-                op("a", wreg + [lst], regs, 0.065 + n * GATHER, A.activation, dst, src, AF.Copy, **kw)
-            elif kw:
-                op("v", wreg + [lst], regs, 0.05 + n * GATHER, V.tensor_scalar, dst, src, kw["scale"], kw["bias"], OP.mult, OP.add)
+                op("a", reads, regs, 0.065 + n * GATHER, A.activation, dst, src, AF.Copy, **kw)
             else:
-                op("v", wreg + [lst], regs, 0.05 + n * GATHER, V.tensor_copy, dst, src)
+                op("v", reads, regs, 0.05 + n * GATHER, V.tensor_copy, dst, src)
 
     def halves(n, o0=0):
         return [(n, (o0, 0)), (n, (o0, 1))]
@@ -186,30 +177,31 @@ def rank_program(g, core, T, topo):
 
     def pick(row, rreg, n=C):
         turn[0] = k = (turn[0] + 1) % SLOTS
-        op("v", rreg + [("k16", 0) if n == C else "k16"], [("sc", k)], n * CYC / 2, V.tensor_tensor_scan, T.sc[:, 2 * C * k:2 * C * k + n], T.k16[:, 0:n], row, 0.0, OP.add, OP.min)
-        return ("sc", k), T.sc[:, 2 * C * k + 15:2 * C * k + C:16], T.sc[:, 2 * C * k + C + 15:2 * C * k + 2 * C:16]
+        op("v", rreg + [("k16", 0) if n <= C else "k16"], [("sc", k)], n * CYC / 2, V.tensor_tensor_scan, T.sc[:, 2 * C * k:2 * C * k + n], T.k16[:, 0:n], row, 0.0, OP.add, OP.min)
+        return ("sc", k), T.sc[:, 2 * C * k + 15:2 * C * k + n:16]
 
-    def rowlist(row, rreg, lst):
-        cv, got, _ = pick(row, rreg)
-        op("v", [cv, ("cols", 0)], [lst], 0, V.tensor_scalar, sl(lst), got, T.cols[:, 0:1], None, OP.add)
+    def listed(buf, o0, lst, parts=1):
+        n = C // parts
+        for k in range(parts):
+            cv, got = pick(T[buf][:, o0 + n * k:o0 + n * k + n], halves(buf, o0) if n == C else [halves(buf, o0)[k]], n)
+            op("v", [cv, ("cols", 0)], [lst if n == C else (lst, k)], 0, V.tensor_scalar, run(lst, n * k, n * k + n), got, T.cols[:, 0:1], None, OP.add)
 
     def small(out, in0, o, in1):
         op("v", [in0, in1], [out], 0, V.tensor_tensor, sl(out), sl(in0), sl(in1), o)
 
     def ts(out, in0, s1, o0, s2=None, o1=None):
-        if o1 is None:
-            op("v", [in0], [out], 0, V.tensor_scalar, sl(out), sl(in0), s1, None, o0)
-        else:
-            op("v", [in0], [out], 0, V.tensor_scalar, sl(out), sl(in0), s1, s2, o0, o1)
+        reads = [in0] + [s for s in (s1, s2) if isinstance(s, tuple)]
+        s1, s2 = [T.cols[:, s[1]:s[1] + 1] if isinstance(s, tuple) else s for s in (s1, s2)]
+        op("v", reads, [out], 0, V.tensor_scalar, sl(out), sl(in0), s1, s2, *([o0] if o1 is None else [o0, o1]))
 
     def vcopy(out, in_):
         op("v", [in_], [out], 0, V.tensor_copy, sl(out), sl(in_))
 
     def quant(q, s, x, a=0, n=C, part=None, xreg=None):
-        op("v", xreg or [x], [(q, part), (s, part)], 0.015 + 0.0011 * n, V.quantize_mx, T[q][:, a:a + n], T[s][:, a:a + n], T[x][:, 4 * a:4 * a + 4 * n])
+        op("v", xreg or [x], [(q, part), (s, part)], 0.015 + 1.1 * n * CYC, V.quantize_mx, T[q][:, a:a + n], T[s][:, a:a + n], T[x][:, 4 * a:4 * a + 4 * n])
 
     def mm(bank, lq, lqs, a, rq, rs, b=0, n=C, part=None):
-        op("t", [lq, lqs, (rq, part), (rs, part)], [bank], (n + 16) * 0.00125, M.matmul_mx, T[bank[0]][:, 512 * bank[1]:512 * bank[1] + n],
+        op("t", [lq, lqs, (rq, part), (rs, part)], [bank], (n + 16) * PE, M.matmul_mx, T[bank[0]][:, 512 * bank[1]:512 * bank[1] + n],
            T[lq][:, a:a + 128], T[lqs][:, a:a + 128], T[rq][:, b:b + n], T[rs][:, b:b + n], True, True)
 
     def bank(b, n=C):
@@ -220,34 +212,29 @@ def rank_program(g, core, T, topo):
 
     dma("s", "dpl", sl("pli"), T.pl[:, :], [], ["pli"], 12)
     dma("s", "dql", sl("qli"), T.ql[:, :], [], ["qli"], 12)
-    dma("s", "du_", sl("ut"), T.u[:, :], [], ["ut"], 200)
-    later = [dma("s", "dx", sl("x0"), T.x[:, :], [], ["x0"], XLOAD)]
-    for sem, out, in_, name in (("dml", sl("mli"), T.ml, "mli"), ("dwc", T.wq[:, :].bitcast(dt.uint8), T.wc, "wq"), ("dws", sl("wsc"), T.ws, "wsc"), ("dv", sl("vt"), T.v, "vt")):
-        dma("s", sem, out, in_[:, :], [], [name], 800, later)
+    dma("a", "dml", sl("mli"), T.ml[:, :], [], ["mli"], 12)
+    dma("s", "du_", sl("ut"), T.u[:, :], [], ["ut"], 128)
+    later = [dma("s", "dx", sl("x0"), T.x[:, :], [], ["x0"], 384)]
+    for sem, out, in_, name, kib in (("dwc", T.wq[:, :].bitcast(dt.uint8), T.wc, "wq", 256), ("dws", sl("wsc"), T.ws, "wsc", 64), ("dv", sl("vt"), T.v, "vt", 128)):
+        dma("s", sem, out, in_[:, :], [], [name], kib, later)
 
-    def iota(n, pattern, base, cm, cols, view=None):
-        kw = {} if SCRATCH[n][2] == "int32" else {"allow_small_or_imprecise_dtypes": True}
-        op("p", [], [n], 0.13 + 2 * cols * CYC, P.iota, view or sl(n), pattern, base, cm, **kw)
+    def iota(view, reg, pattern, base, cm, cols, after=()):
+        kw = {} if reg in ("pi", "c24i", "u8i") else {"allow_small_or_imprecise_dtypes": True}
+        op("p", [], [reg], 0.13 + 2 * cols * CYC, P.iota, view, pattern, base, cm, after=after, **kw)
 
-    iota("pi", [[1, 1]], 0, 1, 1, T.pi[:, 0:1])
-    iota("j16", [[1, 16]], 0, 0, 16)
-    iota("c24i", [[16, 24]], 0, 0, 24)
-    iota("iot", [[1, C]], -H, 0, C)
+    iota(T.pi[:, 0:1], "pi", [[1, 1]], 0, 1, 1)
+    iota(sl("j16"), "j16", [[1, 16]], 0, 0, 16)
+    iota(sl("c24i"), "c24i", [[16, 24]], 0, 0, 24)
+    iota(sl("iot"), "iot", [[1, C]], -H, 0, C)
     loads = len(calls)
-    iota("u8i", [[16, 8]], 0, 0, 8)
-    for k in range(2):
-        copy_a(sl("idc", k), ["iot"], [("idc", k)], sl("iot"), scale=1024.0, bias=1024.0 * H + 511 * k - 1)
-    iota("ones", [[0, 512]], 1, 0, 512)
-    op("v", [], ["unit"], C * CYC, V.memset, sl("unit"), 2.0 ** -8)
+    iota(sl("u8i"), "u8i", [[16, 8]], 0, 0, 8)
+    op("v", [], ["unit"], C * CYC, V.memset, sl("unit"), 1.0)
     for b in range(4):
-        op("p", ["ones"], [("et", b)], 0.17 + 1024 * CYC, P.affine_select, sl("et", b, 512), sl("ones"), [[-1, 512]], OP.is_equal, 0.0, b, 4)
+        op("p", ["unit"], [("et", b)], 0.17 + 1024 * CYC, P.affine_select, sl("et", b, 512), T.unit[:, 0:512], [[-1, 512]], OP.is_equal, 0.0, b, 4)
         quant("eq", "es", "et", 128 * b, 128, b, [("et", b)])
 
     def col(i, in0, reg, s1, o0, s2=None, o1=None):
-        if o1 is None:
-            op("v", [reg], [("cols", i)], 0, V.tensor_scalar, T.cols[:, i:i + 1], in0, s1, None, o0)
-        else:
-            op("v", [reg], [("cols", i)], 0, V.tensor_scalar, T.cols[:, i:i + 1], in0, s1, s2, o0, o1)
+        op("v", [reg], [("cols", i)], 0, V.tensor_scalar, T.cols[:, i:i + 1], in0, s1, s2, *([o0] if o1 is None else [o0, o1]))
 
     op("v", ["pi"], ["qi"], 0, V.tensor_scalar, T.qi[:, 0:1], T.pi[:, 0:1], 15, None, OP.bitwise_and)
     col(5, T.qi[:, 0:1], "qi", 0, OP.add)
@@ -255,38 +242,37 @@ def rank_program(g, core, T, topo):
     col(6, T.qi[:, 0:1], "qi", 15, OP.is_lt, 1024.0, OP.mult)
     col(0, T.cols[:, 6:7], ("cols", 6), float(H), OP.add)
     col(1, T.cols[:, 6:7], ("cols", 6), 512.0, OP.mult)
-    col(2, T.cols[:, 1:2], ("cols", 1), -352.0, OP.add)
-    col(3, T.cols[:, 6:7], ("cols", 6), 511.0 + H, OP.add)
-    col(8, T.cols[:, 1:2], ("cols", 1), -127.5, OP.add)
-    col(9, T.qi[:, 0:1], "qi", 8, OP.is_lt, 256.0, OP.mult)
-    col(10, T.qi[:, 0:1], "qi", 8, OP.is_ge, 256.0, OP.mult)
+    col(2, T.cols[:, 6:7], ("cols", 6), 512.0, OP.mult, -447.0, OP.add)
+    col(3, T.cols[:, 6:7], ("cols", 6), 512.0, OP.mult, 767.5 - SIDE, OP.add)
+    col(8, T.cols[:, 0:1], ("cols", 0), 2.0, OP.mult, 1.0, OP.add)
+    col(9, T.qi[:, 0:1], "qi", 8, OP.is_lt, 1.0, OP.add)
+    col(13, T.qi[:, 0:1], "qi", 8, OP.is_ge, -2.0 ** 90, OP.mult)
+    col(10, T.qi[:, 0:1], "qi", 8, OP.is_ge, 1.0, OP.mult)
+    col(14, T.qi[:, 0:1], "qi", 8, OP.is_ge, 2.0 ** -100, OP.mult)
     op("v", ["pi"], ["q32"], 0, V.tensor_scalar, T.q32[:, 0:1], T.pi[:, 0:1], 31, None, OP.bitwise_and)
-    col(11, T.q32[:, 0:1], "q32", 16, OP.is_lt, 512.0, OP.mult)
-    col(12, T.q32[:, 0:1], "q32", 16, OP.is_ge, -512.0, OP.mult)
+    col(11, T.q32[:, 0:1], "q32", 16, OP.is_lt, 512.0 / U, OP.mult)
+    col(12, T.q32[:, 0:1], "q32", 16, OP.is_ge, -512.0 / U, OP.mult)
     for n in ("hs", "gs"):
         for a in (0, C + 16):
             op("v", [], [(n, "end%d" % a)], 0, V.memset, T[n][:, a:a + 16], 0.0)
     for k, (a, w, ns) in enumerate(TABLES):
-        dma("s", "did%d" % k, T.pw2[:, a:a + C], sl("iot"), ["iot"], halves("pw2", a), 400)
-    for a in range(C, 7 * 512, 512):
-        copy_a(T.pw2[:, a:a + 512 - C], ["iot"], [("pw2", a)], T.iot[:, 0:512 - C], n=128)
-    op("v", [], [("sums", 3)], H * CYC, V.memset, T.sums[:, 3:4 * C:4], 0.0)
+        dma("s", "did%d" % k, T.pw2[:, a:a + C], sl("iot"), ["iot"], halves("pw2", a), 96)
     op("v", [], [("lrow", 0)], 0, V.memset, T.lrow[:, 0:1], 0.0)
     op("v", [], [("cols", 7)], 0, V.memset, T.cols[:, 7:8], 2.0 ** -100)
-    op("v", ["j16", ("cols", 5)], ["f1"], 0, V.tensor_scalar, T.wf[:, AT["f1"][1]:AT["f1"][1] + 16], sl("j16"), T.cols[:, 5:6], 2048.0, OP.is_equal, OP.mult)
-    op("v", ["j16", ("cols", 4)], ["f2"], 0, V.tensor_scalar, T.wf[:, AT["f2"][1]:AT["f2"][1] + 16], sl("j16"), T.cols[:, 4:5], -1024.0, OP.is_equal, OP.mult)
-    op("v", ["f1", "f2"], ["kseed"], 0, V.tensor_tensor, T.kseed[:, 0:16], T.wf[:, AT["f1"][1]:AT["f1"][1] + 16], T.wf[:, AT["f2"][1]:AT["f2"][1] + 16], OP.add)
-    op("v", ["c24i", ("cols", 5)], ["cw"], 0, V.tensor_scalar, sl("cw"), sl("c24i"), T.cols[:, 5:6], None, OP.add)
+    op("v", ["j16", ("cols", 5)], ["k1"], 0, V.tensor_scalar, run("k1", 0, 256), sl("j16"), T.cols[:, 5:6], 2048.0, OP.is_equal, OP.mult)
+    op("v", ["j16", ("cols", 4)], ["k2"], 0, V.tensor_scalar, run("k2", 0, 256), sl("j16"), T.cols[:, 4:5], -1024.0, OP.is_equal, OP.mult)
+    op("v", ["k1", "k2"], ["kseed"], 0, V.tensor_tensor, T.kseed[:, 0:16], run("k1", 0, 256), run("k2", 0, 256), OP.add)
+    ts("cw", "c24i", ("cols", 5), OP.add)
     op("v", ["c24i", ("cols", 5)], ["rl"], 0, V.tensor_scalar, T.rl[:, 0:24], sl("c24i"), 0.0, T.cols[:, 5:6], OP.mult, OP.add)
     seed = T.kseed[:, 0:16].indirect(T.rl[:, 0:24])
     op("v", ["kseed", "rl"], [("k16", 0)], 0.05 + C * GATHER, V.tensor_copy, T.k16[:, 0:C], seed)
-    op("a", ["kseed", "rl"], ["k16f"], 0.065 + C * GATHER, A.activation, sl("k16f"), seed, AF.Copy, scale=512.0)
-    op("v", [("k16", 0)], [("k16", 1)], H * CYC, V.tensor_copy, T.k16[:, C:2 * C], T.k16[:, 0:C])
+    op("a", ["kseed", "rl"], [("k16", 1)], 0.065 + C * GATHER, A.activation, T.k16[:, C:2 * C], seed, AF.Copy)
+    op("v", [("k16", 0)], ["k16f"], H * CYC, V.tensor_scalar, sl("k16f"), T.k16[:, 0:C], 512.0, None, OP.mult)
 
     op("v", ["u8i"], ["uoff"], 0, V.tensor_copy, sl("uoff"), T.u8i[:, 0:8])
     quant("uq", "us", "ut", n=128)
     op("v", ["uq", "uoff"], ["up"], 0.05 + 128 * GATHER, V.tensor_copy, T.up[:, :].bitcast(dt.uint32), T.uq[:, :].bitcast(dt.uint32).indirect(T.uoff[:, :]))
-    op("v", ["us", "uoff"], ["ups"], 0.05 + 128 * GATHER, V.tensor_copy, sl("ups"), T.us[:, :].indirect(T.uoff[:, :]))
+    op("a", ["us", "uoff"], ["ups"], 0.065 + 128 * GATHER, A.activation, sl("ups"), T.us[:, :].indirect(T.uoff[:, :]), AF.Copy)
     quant("vq", "vs", "vt", n=128)
 
     vcopy("pw", "pli")
@@ -295,66 +281,65 @@ def rank_program(g, core, T, topo):
     gath("av", "qrow", "iot", "qw")
     gath("av", "pw2", "qrow", "pw", o0=ROW[1])
     gath("a", "prow", "iot", "pw")
-    copy_a(sl("ip", 0), ["iot"], [("ip", 0)], sl("iot"))
-    copy_a(sl("ip", 1), ["prow"], [("ip", 1)], sl("prow"))
-    dma("s", "did4", power("p")[0], sl("prow"), ["prow"], power("p")[1], 400)
+    dma("s", "did4", power("p")[0], sl("prow"), ["prow"], power("p")[1], 96)
+    dma("s", "did3", sl("ip", 1), sl("prow"), ["prow"], [("ip", 1)], 96)
     small("pmc", "pli", OP.subtract, "cw")
     small("mn", "pli", OP.min, "cw")
     ts("gt", "pmc", 0.0, OP.is_lt, float(C), OP.mult)
     small("idf", "mn", OP.add, "gt")
     vcopy("idl", "idf")
-    gath("a", "key0", "idc", "idl", bias=float(H))
-    copy_a(sl("key1"), ["key0"], ["key1"], sl("key0"), bias=-1.0)
     gath("a", "murow", "iot", "muw")
-    gath("a", "mpr", "murow", "pw")
-    rowlist(sl("mpr"), ["mpr"], "mupf")
+    op("v", ["iot"], [("dl", 0)], H * CYC, V.tensor_scalar, T.dl[:, 0:2 * C:2], sl("iot"), 0.0, None, OP.mult)
+    fused(T.dl[:, 1:2 * C:2], [("dl", 1)], sl("murow"), ["murow"], "pw", OP.subtract, sl("prow"), ["prow"])
+    cv, got = pick(T.dl[:, 1:2 * C:2], [("dl", 1)])
+    op("v", [cv, ("cols", 6)], ["f3"], 0, V.tensor_scalar, sl("f3"), got, T.cols[:, 6:7], None, OP.add)
+    small("mupf", "f3", OP.add, "pli")
     vcopy("mupw", "mupf")
     small("lo_", "mupf", OP.min, "pli")
     small("hi_", "mupf", OP.max, "pli")
     vcopy("lpw", "lo_")
     vcopy("hpw", "hi_")
     gath("a", "pmr", "prow", "mupw")
-    rowlist(sl("pmr"), ["pmr"], "pmpf")
-    vcopy("pmpw", "pmpf")
-    small("ww2", "pmpf", OP.subtract, "cw")
-    op("v", ["ww2", ("cols", 6)], ["wk"], 0, V.tensor_scalar, sl("wk"), sl("ww2"), T.cols[:, 6:7], None, OP.mult)
-    small("wk", "wk", OP.add, "cw")
+    listed("pmr", 0, "pmpw")
+
+    def behind(sends):
+        for a in range(C, 7 * 512, 512):
+            iota(T.pw2[:, a:a + 512 - C], ("pw2", a), [[0, 512 - C]], 0, 0, 512 - C, sends)
+        op("p", ["prow"], [("fq", 1)], 0.17 + 2 * C * CYC, P.affine_select, T.fq[:, 1:2 * C:2], sl("prow"), [[0, C]], OP.is_gt, 0.0, 1, 0, after=sends)
+        iota(sl("ip", 0), ("ip", 0), [[1, C]], -H, 0, C, sends)
+        iota(sl("idc"), "idc", [[SIDE, 2], [1024, C]], -1, 0, 2 * C, sends)
+        gath("a", "key0", "idc", "idl", bias=float(H))
+        copy_a(sl("key1"), ["key0"], ["key1"], sl("key0"), bias=-1.0)
 
     def times(how, to, n, lst):
         gath(how, "pw2", "pw2", lst, o0=ROW[to], wreg=power(n)[1], wcols=(ROW[n], ROW[n] + C))
 
     def powers(s):
-        a = "a%d" % s
-        rowlist(*power(1), a)
-        gath("a", "hh", "prow", a)
-        gath("a", "hh", "hh", "pmpw", o0=C, wreg=halves("hh"), wcols=(0, C))
-        cv, stay, swap = pick(sl("hh"), ["hh"], 2 * C)
-        op("v", [cv], ["hd_"], 0, V.tensor_tensor, sl("hd_"), swap, stay, OP.subtract)
-        op("v", ["hd_", ("cols", 6), ("cols", 0)], ["h2"], 0, V.tensor_scalar, sl("h2"), sl("hd_"), T.cols[:, 6:7], T.cols[:, 0:1], OP.mult, OP.add)
-        op("v", [cv, "h2"], ["hk"], 0, V.tensor_tensor, sl("hk"), stay, sl("h2"), OP.add)
+        a, how = "a%d" % s, "a" if s == 1 else "aa"
+        listed("pw2", ROW[1], a, len(how))
         for n in STEPS[:6]:
-            times("aav" if n == 32 else "a", 2 * n, n, a if n == 1 else "l%d" % n)
-            rowlist(*power(2 * n), "l%d" % (2 * n))
+            times(how, 2 * n, n, a if n == 1 else "l%d" % n)
+            listed("pw2", ROW[2 * n], "l%d" % (2 * n), len(how))
 
     def walk(s, cur, hd, pair, spare, last=None):
         for i, n in enumerate(STEPS):
             lst = "a%d" % s if n == 1 else "l%d" % n
-            nxt, o = pair[cur == pair[0]], AT[lst][1]
-            for k, (a, e) in enumerate(((0, W1 if last else WCUT), (W1 if last else WCUT, C))):
+            nxt = pair[cur == pair[0]]
+            for k, (a, e) in enumerate(((0, H), (H, C))):
                 near = spare if i or not hd else hd
                 if near == spare and last:
-                    op("v", [(cur, k) if i else cur], [(spare, k)], (e - a) * CYC / 2, V.tensor_scalar, T[spare][:, a:e], T[cur][:, a:e], float(-n), None, OP.add)
+                    op("v", [(cur, k) if i else cur], [(spare, k)], H * CYC / 2, V.tensor_scalar, T[spare][:, a:e], T[cur][:, a:e], -n * U, None, OP.add)
                 elif near == spare:
-                    copy_a(T[spare][:, a:e], [(cur, k) if i else cur], [(spare, k)], T[cur][:, a:e], n=e - a, bias=float(-n))
+                    copy_a(T[spare][:, a:e], [(cur, k)], [(spare, k)], T[cur][:, a:e], n=H, bias=float(-n))
                 out, reg = (T[last][:, 16 + a:16 + e], (last, k)) if last and i == 7 else (T[nxt][:, a:e], (nxt, k))
-                op("v", [cur, lst, (near, k) if near == spare else near], [reg], 0.05 + (e - a) * GATHER, V.tensor_tensor, out,
-                   sl(cur).indirect(T.wl[:, o + a // 16:o + e // 16]), T[near][:, a:e], OP.min)
+                op("v", [cur, (lst, k), (near, k) if near == spare else near], [reg], 0.05 + H * GATHER, V.tensor_tensor, out, sl(cur).indirect(run(lst, a, e)), T[near][:, a:e], OP.min)
             cur = nxt
         return cur
 
     def first_mirror():
-        for n, c in (("hm", 10), ("hf", 9)):
-            op("v", [("cols", c)], [n, ("pb", 0)], C * CYC, V.tensor_scalar, sl(n), bank(("pb", 0)), 0.0, T.cols[:, c:c + 1], OP.is_ge, OP.mult)
+        mm(("pb", 1), "up", "ups", 0, "tq0", "ts0")
+        copy_a(sl("hm"), [("cols", 10), ("cols", 14)], ["hm", ("pb", 1)], bank(("pb", 1)), func=AF.Sign, scale=T.cols[:, 10:11], bias=T.cols[:, 14:15])
+        op("v", [("cols", 9), ("cols", 13)], ["hf", ("pb", 0)], C * CYC, V.tensor_scalar, sl("hf"), bank(("pb", 0)), T.cols[:, 13:14], T.cols[:, 9:10], OP.is_ge, OP.mult)
         fused(sl("h0"), ["h0"], sl("hm"), ["hm"], "pw", OP.add, sl("hf"), ["hf"])
         walk(1, "h0", None, ("h0", "h1"), "hdb", "hs")
         for to, n, lst in ((3, 1, "l2"), (5, 1, "l4"), (6, 2, "l4"), (7, 3, "l4"), (24, 8, "l16"), (40, 8, "l32"), (48, 16, "l32"), (56, 24, "l32"),
@@ -367,8 +352,8 @@ def rank_program(g, core, T, topo):
         for out, k, t, a in (("ep", 0, "1", 0), ("eq0", 1, "1", 16), ("eq0", 0, "2", 16), ("ep", 1, "2", 32)):
             o = AT[out][1]
             op("v", ["th" + t, "tg" + t], [(out, k)], 0, V.tensor_tensor, T.wf[:, o + k:o + 24:2], T["th" + t][:, a:a + 353:32], T["tg" + t][:, a + 8:a + 361:32], OP.subtract)
-        for out, src, c in (("ep2", "ep", 11), ("eq2", "eq0", 12)):
-            op("v", [src, ("cols", c)], [out], 0, V.tensor_scalar, sl(out), sl(src), T.cols[:, c:c + 1], None, OP.mult)
+        ts("ep2", "ep", ("cols", 11), OP.mult)
+        ts("eq2", "eq0", ("cols", 12), OP.mult)
         small("ev", "ep2", OP.subtract, "eq2")
         small("ne", "eq2", OP.subtract, "ep2")
         small("ei", "ev", OP.max, "ne")
@@ -380,91 +365,109 @@ def rank_program(g, core, T, topo):
         vcopy("ix", "if0")
         for k in (1, 2):
             ts("d%di" % k, "ei", 3 * k, OP.logical_shift_right, 7 * 512, OP.bitwise_and)
-            op("v", ["d%di" % k, ("cols", 0)], ["d%df" % k], 0, V.tensor_scalar, sl("d%df" % k), sl("d%di" % k), 0.75, T.cols[:, 0:1], OP.mult, OP.add)
+            ts("d%df" % k, "d%di" % k, 0.75, OP.mult, ("cols", 0), OP.add)
         ts("nw", "ng", 3.0 * C, OP.mult)
         small("d2f", "d2f", OP.add, "nw")
         for k, (a, w, ns) in enumerate(TABLES):
             gath("av", "lv", "pw2", "ix", wreg=[r for i in range(len(ns)) for r in halves("pw2", a + w * i)] + [("pw2", i) for i in range(C, 7 * 512, 512)], wcols=(a, a + w * (len(ns) - 1) + C))
             if k == 2:
-                return rowlist(sl("lv"), ["lv"], "m1")
-            cv, got, _ = pick(sl("lv"), ["lv"])
-            op("v", [cv, "d%df" % (k + 1)], ["if0"], 0, V.tensor_tensor, sl("if0"), got, sl("d%df" % (k + 1)), OP.add)
-            vcopy("ix", "if0")
+                return listed("lv", 0, "m1", 2)
+            for j in range(2):
+                f, d, x = [run(n, H * j, H * j + H) for n in ("if0", "d%df" % (k + 1), "ix")]
+                cv, got = pick(sl("lv", j, H), [halves("lv")[j]], H)
+                op("v", [cv, "d%df" % (k + 1)], [("if0", j)], 0, V.tensor_tensor, f, got, d, OP.add)
+                op("v", [("if0", j)], [("ix", j)], 0, V.tensor_copy, x, f)
 
     def lay_out(s):
-        a = "a%d" % s
         cur = walk(s, "key0", "key1", ("ka", "kb"), "khd")
         op("v", [cur, "k16f"], ["scf"], C * CYC, V.tensor_tensor_scan, sl("scf"), sl("k16f"), sl(cur), 0.0, OP.add, OP.min)
         op("v", ["scf", ("cols", 1)], ["kw"], 0, V.tensor_scalar, sl("kw"), T.scf[:, 15:C:16], T.cols[:, 1:2], None, OP.add)
         op("v", ["scf", ("cols", 2)], ["lol"], 0, V.tensor_scalar, sl("lol"), T.scf[:, 15:C:16], T.cols[:, 2:3], 2.0 ** -10, OP.add, OP.mult)
+        op("v", ["scf", ("cols", 3)], ["el"], 0, V.tensor_scalar, sl("el"), T.scf[:, 15:C:16], T.cols[:, 3:4], 2.0 ** -9, OP.add, OP.mult)
         ts("di", "kw", 1023, OP.bitwise_and)
-        fused(sl("drow"), ["drow"], sl(cur), [cur], a, OP.subtract, sl("idc", 0), ["idc"])
-        copy_a(T.lrow[:, 1:C + 1], ["drow"], [("lrow", 1)], sl("drow"), func=AF.Relu)
-        now, last = T.lrow[:, 1:C + 1], T.lrow[:, 0:C]
-        for k, (d0, d1) in enumerate(((last, last), (now, last), (now, now))):
-            op("v", ["lrow"], [("sums", k)], H * CYC, V.tensor_tensor_scan, T.sums[:, k:4 * C:4], d0, d1, -float(H), OP.add, OP.add)
-        op("v", ["scf", ("cols", 8)], ["el"], 0, V.tensor_scalar, sl("el"), T.scf[:, 15:C:16], T.cols[:, 8:9], 2.0 ** -8, OP.add, OP.mult)
-        gath("a", "le", "sums", "el")
+        fused(sl("drow"), ["drow"], sl(cur), [cur], "a%d" % s, OP.subtract, sl("idc", 0), ["idc"])
+        op("v", ["drow"], [("lrow", 1)], H * CYC, V.tensor_scalar, T.lrow[:, 1:C + 1], sl("drow"), 0.0, None, OP.max)
+        for k, (d0, d1) in enumerate(((T.lrow[:, 0:C + 1], T.lrow[:, 0:C + 1]), (T.lrow[:, 1:C + 1], T.lrow[:, 0:C]))):
+            op("v", ["lrow"], [("sums", k)], H * CYC, V.tensor_tensor_scan, T.sums[:, k:2 * C + 1:2], d0, d1, -float(H), OP.add, OP.add)
+        gath("a", "le", "sums", "el", wcols=(0, 2 * C + 1))
         gath("a", "le", "drow", "lol", o0=C)
-        ts("v0", "di", 511.0, OP.is_ge, float(C), OP.mult)
+        ts("v0", "di", float(SIDE), OP.is_ge, float(C), OP.mult)
         small("v1", "v0", OP.add, "cw")
         vcopy("vl", "v1")
         gath("a", "vrow", "ip", "vl")
-        op("v", ["di", ("cols", 3)], ["sg"], 0, V.tensor_scalar, sl("sg"), sl("di"), -1.0, T.cols[:, 3:4], OP.mult, OP.add)
-        op("v", ["di", ("cols", 0)], ["nz"], 0, V.tensor_scalar, sl("nz"), sl("di"), T.cols[:, 0:1], None, OP.add)
-        small("a0", "nz", OP.min, "sg")
-        cl, lens, _ = pick(sl("le", 1), halves("le", C))
+        ts("sg", "di", -1.0, OP.mult, float(SIDE), OP.add)
+        small("a0", "di", OP.min, "sg")
+        cl, lens = pick(sl("le", 1), halves("le", C))
         op("v", [cl, ("cols", 6)], ["lw"], 0, V.tensor_scalar, sl("lw"), lens, T.cols[:, 6:7], None, OP.add)
-        ce, ends, _ = pick(sl("le", 0), halves("le"))
+        ce, ends = pick(sl("le", 0), halves("le"))
         op("v", [ce, "a0"], ["sp"], 0, V.tensor_tensor, sl("sp"), ends, sl("a0"), OP.add)
-        vcopy("spl", "sp")
+        ts("spl", "sp", ("cols", 0), OP.add)
         op("v", ["vrow", "spl"], halves("order"), 0.05 + C * SCATTER, V.tensor_copy, sl("order", 0).indirect(sl("spl")), sl("vrow"))
-        rowlist(sl("order", 0), halves("order"), "opl")
+        listed("order", 0, "opl")
         gath("a", "order", "prow", "opl", o0=C)
         small("w1", "v0", OP.max, "lw")
         small("pos2", "sp", OP.add, "w1")
         small("pos1", "pos2", OP.subtract, "lw")
-        op("v", ["pos1", "pos2"], ["p1l", "p2l"], 0, V.tensor_copy, two("p2l"), two("pos2"))
+        op("v", ["pos1", "pos2", ("cols", 0)], ["p1l", "p2l"], 0, V.tensor_scalar, run("p2l", 0, 2 * C), run("pos2", 0, 2 * C), T.cols[:, 0:1], None, OP.add)
         return cl, lens
 
     def mirror(mw, cl, lens):
-        op("v", ["ssb", "opl"], halves("mk"), 0.05 + C * GATHER, V.tensor_scalar, sl("mk", 0), sl("ssb").indirect(sl("opl")), 0.0, -0.5, OP.is_ge, OP.add)
-        gath("a", "mk", "markp", "opl", o0=C, scale=0.5)
-        op("v", ["mk", "unit"], ["sf"], C * CYC, V.tensor_tensor_scan, sl("sf"), sl("unit"), sl("mk"), 0.5, OP.add, OP.min)
-        op("v", ["mk", "unit"], ["sr"], C * CYC, V.tensor_tensor_scan, T.sr[:, ::-1], sl("unit"), T.mk[:, ::-1], 0.5, OP.add, OP.min)
-        gath("a", "fr", "sf", "p2l", scale=256.0, bias=128.0)
-        gath("v", "fr", "sr", "p1l", o0=C, scale=256.0, bias=128.0)
-        cv, before, behind = pick(sl("fr"), ["fr"], 2 * C)
-        op("v", [cv, cl], ["clf"], 0, V.tensor_tensor, sl("clf"), before, lens, OP.min)
-        op("v", [cv, cl], ["clr"], 0, V.tensor_tensor, sl("clr"), behind, lens, OP.min)
+        op("a", ["ssb", "pw", ("cols", 7)], ["markp"], 0.065 + C * GATHER, A.activation, sl("markp"), sl("ssb").indirect(sl("pw")), AF.Sign, bias=T.cols[:, 7:8])
+        op("v", ["ssb", "opl"], halves("mk"), 0.05 + C * GATHER, V.tensor_scalar, sl("mk", 0), sl("ssb").indirect(sl("opl")), 0.0, 256.0, OP.is_ge, OP.mult)
+        gath("a", "mk", "markp", "opl", o0=C, scale=128.0, bias=128.0)
+        op("v", ["mk", "unit"], ["sf"], C * CYC, V.tensor_tensor_scan, sl("sf"), sl("unit"), sl("mk"), 256.0, OP.add, OP.min)
+        op("v", ["mk", "unit"], ["sr"], C * CYC, V.tensor_tensor_scan, T.sr[:, ::-1], sl("unit"), T.mk[:, ::-1], 256.0, OP.add, OP.min)
+        gath("a", "fr", "sf", "p2l")
+        gath("v", "fr", "sr", "p1l", o0=C)
+        cv, _ = pick(sl("fr"), ["fr"], 2 * C)
+        for k, n in enumerate(("clf", "clr")):
+            o = 2 * C * cv[1] + C * k
+            op("v", [cv, cl], [n], 0, V.tensor_tensor, sl(n), T.sc[:, o + 15:o + C:16], lens, OP.min)
         small("e0", "clr", OP.subtract, "clf")
         small("g0", "clr", OP.is_lt, "clf")
         small("y0", "e0", OP.add, "pos1")
         small("gl", "g0", OP.mult, "lw")
         small("tg", "y0", OP.add, "gl")
-        vcopy("tl", "tg")
-        gath("av" if mw == "m3" else "v", "mrow", "order", "tl")
-        rowlist(sl("mrow"), ["mrow"], mw)
+        ts("tl", "tg", ("cols", 0), OP.add)
+        how = "av" if mw == "m3" else "v"
+        gath(how, "mrow", "order", "tl")
+        listed("mrow", 0, mw, len(how))
 
-    def conjugate(mw):
-        if mw != "m2":
-            gath("v" if mw == "m3" else "av", "smr", "ssb", mw)
-        else:
+    def conjugate(s):
+        a, mw = "a%d" % s, "m%d" % s
+        gath("a", "hh", "prow", a, wreg=["prow"] + ["opl"] * (s > 1))
+        gath("a", "hh", "hh", "pmpw", o0=C, wreg=halves("hh"), wcols=(0, C))
+        cv, both = pick(sl("hh"), ["hh"], 2 * C)
+        op("v", [cv, ("cols", 8)], ["f2", "f4"], 0, V.tensor_scalar, run("f2", 0, 2 * C), both, 2.0, T.cols[:, 8:9], OP.mult, OP.add)
+        small("hd_", "f4", OP.subtract, "f2")
+        ts("h2", "hd_", ("cols", 6), OP.mult)
+        small("hk", "f2", OP.add, "h2")
+        how = "v" if s == 3 else "av"
+        if s == 2:
             gath("a", "ssp", "ssb", "pw")
             gath("a", "laid", "ssb", "opl")
             gath("a", "laid", "ssp", "opl", o0=C)
             gath("a", "smr", "laid", "tl")
-        how = "v" if mw == "m3" else "av"
+        else:
+            gath(how, "smr", "ssb", mw)
         gath(how, "shp", "smr", "hpw")
-        fused(sl("flag"), ["flag"], sl("smr"), ["smr"], "lpw", OP.is_gt, sl("shp"), ["shp"])
-        cv, got, _ = pick(sl("flag"), ["flag"])
-        op("v", [cv, "ww2"], ["f1"], 0, V.tensor_tensor, sl("f1"), got, sl("ww2"), OP.mult)
-        op("v", [cv, "hd_"], ["f3"], 0, V.tensor_tensor, sl("f3"), got, sl("hd_"), OP.mult)
-        op("v", ["f1", "f3", "wk", "hk"], ["f2", "f4"], 0.1, V.tensor_tensor, two("f2"), two("f1"), two("wk"), OP.add)
-        op("v", ["f2", "f4"], ["piw", "uw"], 0, V.tensor_copy, two("piw"), two("f2"))
-        how = "a" if mw == "m3" else "av"
-        gath(how, "pprow", "prow", "piw")
-        gath(how, "pw2", "pprow", "uw", o0=ROW[1])
+        n = C // len(how)
+        for k in range(len(how)):
+            f3, f1, hd, hk, u, lo = [run(x, n * k, n * k + n) for x in ("f3", "f1", "hd_", "hk", "uw", "lpw")]
+            flags, pairs = T.fq[:, 2 * n * k:2 * n * k + 2 * n:2], slice(2 * n * k, 2 * n * k + 2 * n)
+            part = {x: x if n == C else (x, k) for x in ("f3", "f1", "uw", "tau")}
+            freg = halves("fq") if n == C else [halves("fq")[k]]
+            op("v", ["smr", "lpw"] + (halves("shp") if n == C else [halves("shp")[k]]), freg, 0.05 + n * GATHER, V.tensor_tensor, flags, sl("smr").indirect(lo), T.shp[:, n * k:n * k + n], OP.is_gt)
+            cv, got = pick(flags, freg, n)
+            op("v", ["dl", ("fq", 1)] + freg, [part["tau"]], n * CYC, V.tensor_tensor_scan, T.tau[:, pairs], T.dl[:, pairs], T.fq[:, pairs], 0.0, OP.mult, OP.add)
+            op("v", [cv, "hd_"], [part["f3"]], 0, V.tensor_tensor, f3, got, hd, OP.mult)
+            op("v", [part["f3"], "hk"], [part["f1"]], 0, V.tensor_tensor, f1, f3, hk, OP.add)
+            op("v", [part["f1"]], [part["uw"]], 0, V.tensor_copy, u, f1)
+        gath("a" if s == 3 else "av", "pw2", "tau", "uw", o0=ROW[1])
+
+    def z_piece(out, part, rm, b, a, e):
+        op("v", [("fp", b), rm] + halves("fa", C * b), [(out, part)], 0.05 + (e - a) * GATHER, V.tensor_tensor, T[out][:, 4 * a + b:4 * e:4],
+           sl("fp", b).indirect(run(rm, a, e)), T.fa[:, C * b + a:C * b + e], OP.add)
 
     steps = T.tables["STEP"] if "STEP" in T.tables else [1, 2, 3]
     for s in (1, 2, 3):
@@ -473,35 +476,32 @@ def rank_program(g, core, T, topo):
         tq, tsn, lq, lp = "tq%d" % (s - 1), "ts%d" % (s - 1), "lq%d" % s, "lp%d" % s
         mw, rm, ra, zq, zs = "m%d" % s, "rm%d" % s, "ra%d" % s, "zq%d" % s, "zs%d" % s
         powers(s)
-        arrive("aa%d" % s, ne, [ra], [send(dst, "aa%d" % s, sl(ra), sl("a%d" % s), ["a%d" % s], s == 1)], FLIGHT + 0.8)
+        arrive("aa%d" % s, ne, [ra], [send(dst, "aa%d" % s, sl(ra), sl("a%d" % s), ["a%d" % s], s == 1)], FLIGHT + LIST)
         quant(tq, tsn, "x0" if s == 1 else "xn")
         mm(("pb", 0), "up", "ups", 0, tq, tsn)
         both = [send(dst, "at%d" % s, T[lq][:, :].bitcast(dt.uint8), T[tq][:, :].bitcast(dt.uint8), [tq]), send(dst, "at%d" % s, sl(lp), sl(tsn), [tsn])]
-        arrive("at%d" % s, 2 * ne, [lq, lp], both, FLIGHT + TILE)
+        arrive("at%d" % s, 2 * ne, [lq, lp], both, FLIGHT + TILE + (COLD if s == 1 else 0.0))
         if s == 1:
+            behind(both)
             first_mirror()
         copy_a(sl("ssb"), [], ["ssb", ("pb", 0)], bank(("pb", 0)))
         if s > 1:
-            op("a", ["ssb", "pw", ("cols", 7)], ["markp"], 0.065 + C * GATHER, A.activation, sl("markp"), sl("ssb").indirect(sl("pw")), AF.Sign, bias=T.cols[:, 7:8])
             mirror(mw, *lay_out(s))
         for b in range(4):
             mm(("pa", b), "eq", "es", 128 * b, tq, tsn)
-            if s == 3:
+            if s == 3 and b not in SHARED:
                 copy_a(sl("fo", b), [], [("fo", b), ("pa", b)], bank(("pa", b)))
         for b in (1, 2, 3, 0):
             mm(("pb", b), "eq", "es", 128 * b, lq, lp)
             copy_a(sl("fp", b), [], [("fp", b), ("pb", b)], bank(("pb", b)), scale=0.5)
             gath("a", "fa", "fp", ra, o0=C * b, wreg=[("fp", b)], wcols=(C * b, C * b + C))
-        arrive("am%d" % s, ne, [rm], [send(dst, "am%d" % s, sl(rm), sl(mw), [mw])], FLIGHT + (0.8 if s < 3 else 0.1))
-        conjugate(mw)
+        arrive("am%d" % s, ne, [rm], [send(dst, "am%d" % s, sl(rm), sl(mw), [mw])], FLIGHT + (LIST if s < 3 else LAST))
+        conjugate(s)
         if s == 3:
             break
-        o = AT[rm][1]
-        for b in range(4):
-            for a in range(0, C, PIECE):
-                e = a + PIECE
-                op("v", [("fp", b), rm] + halves("fa", C * b), [("z", (b, a))], 0.05 + PIECE * GATHER, V.tensor_tensor, T.z[:, 4 * a + b:4 * e:4],
-                   sl("fp", b).indirect(T.wr[:, o + a // 16:o + e // 16]), T.fa[:, C * b + a:C * b + e], OP.add)
+        for a in range(0, C, PIECE):
+            for b in range(4):
+                z_piece("z", (b, a), rm, b, a, a + PIECE)
         quant(zq, zs, "z")
         for b in range(4):
             mm(("pb", b), "wq", "wsc", 128 * b, zq, zs)
@@ -510,31 +510,35 @@ def rank_program(g, core, T, topo):
             op("v", halves("mg", C * b), [("xn", b), ("pa", b)], C * CYC, V.tensor_tensor, T.xn[:, b:4 * C:4], bank(("pa", b)), sl("mg", b), OP.add)
     gath("a", "qr3", "pw2", "pw", wreg=power(1)[1], wcols=(ROW[1], ROW[1] + C), bias=float(H))
     dma("s", "dqo", T.qo[:, :], T.qr3[0:128:16, :], ["qr3"], [], 12)
-    o = AT["rm3"][1]
-    for k, (a, e) in enumerate(((0, CUT), (CUT, C))):
+    for k, (a, e) in enumerate(RUNS):
         for b in (1, 2, 3, 0):
-            op("v", [("fp", b), "rm3"] + halves("fa", C * b), [("ze", (b, k))], 0.05 + (e - a) * GATHER, V.tensor_tensor, T.ze[:, 4 * a + b:4 * e:4],
-               sl("fp", b).indirect(T.wr[:, o + a // 16:o + e // 16]), T.fa[:, C * b + a:C * b + e], OP.add)
+            z_piece("ze", (b, k), "rm3", b, a, e)
         quant("zq3", "zs3", "ze", a, e - a, k, [("ze", (b, k)) for b in range(4)])
         for b in range(4):
-            at = ("pa" if k else "pb", b)
+            at, out = ("pa" if k and b not in SHARED else "pb", b), T.rl3[:, C * b + a:C * b + e]
             mm(at, "wq", "wsc", 128 * b, "zq3", "zs3", a, e - a, k)
-            copy_a(T.rl3[:, C * b + a:C * b + e], [], [("rl3", (b, k)), at], bank(at, e - a), n=e - a, scale=0.03125)
-    o = AT["m3"][1]
-    for k, (a, e) in enumerate(((0, CUT), (CUT, C))):
+            if k:
+                op("v", [], [("rl3", (b, k)), at], (e - a) * CYC, V.tensor_scalar, out, bank(at, e - a), 0.03125, None, OP.mult)
+            else:
+                copy_a(out, [], [("rl3", (b, k)), at], bank(at, e - a), n=e - a, scale=0.03125)
+    for k, (a, e) in enumerate(RUNS):
         for b in range(4):
-            op("v", [("rl3", (b, 0)), ("rl3", (b, 1)), "m3", ("fo", b)], [("xe", 4 * k + b)], 0.05 + (e - a) * GATHER, V.tensor_tensor, T.xe[:, 4 * a + b:4 * e:4],
-               sl("rl3", b).indirect(T.wl[:, o + a // 16:o + e // 16]), T.fo[:, C * b + a:C * b + e], OP.add)
+            src, both, out = sl("rl3", b).indirect(run("m3", a, e)), [("rl3", (b, 0)), ("rl3", (b, 1)), "m3"], T.xe[:, 4 * a + b:4 * e:4]
+            if b in SHARED:
+                op("a", both, [("mg", (b, k))], 0.065 + (e - a) * GATHER, A.activation, T.mg[:, C * b + a:C * b + e], src, AF.Copy)
+                op("v", [("mg", (b, k))], [("xe", 4 * k + b), ("pa", b)], (e - a) * CYC, V.tensor_tensor, out, T.pa[:, 512 * b + a:512 * b + e], T.mg[:, C * b + a:C * b + e], OP.add)
+            else:
+                op("v", both + [("fo", b)], [("xe", 4 * k + b)], 0.05 + (e - a) * GATHER, V.tensor_tensor, out, src, T.fo[:, C * b + a:C * b + e], OP.add)
         quant("tq3", "ts3", "xe", a, e - a, k, [("xe", 4 * k + b) for b in range(4)])
         mm(("pb", k), "vq", "vs", 0, "tq3", "ts3", a, e - a, k)
         copy_a(T.ysb[:, a:e], [], [("ysb", k), ("pb", k)], bank(("pb", k), e - a), n=e - a)
-        dma("a" if k else "s", "dy%d" % k, T.y[:, a:e], T.ysb[:, a:e], [("ysb", k)], [], 500 - 400 * k)
-        dma("s", "doc%d" % k, T.oc[:, 4 * a:4 * e], T.tq3[:, a:e].bitcast(dt.uint8), [("tq3", k)], [], 500 - 400 * k)
+        dma("a" if k else "s", "dy%d" % k, T.y[:, a:e], T.ysb[:, a:e], [("ysb", k)], [], (e - a) / 2)
+        dma("s", "doc%d" % k, T.oc[:, 4 * a:4 * e], T.tq3[:, a:e].bitcast(dt.uint8), [("tq3", k)], [], (e - a) / 2)
     for k in range(4):
-        dma("s", "dos%d" % k, T.osc[4 * k:4 * k + 4, 0:C], T.ts3[32 * k:32 * k + 4, 0:C], ["ts3"], [], 2)
+        dma("as"[k % 2], "dos%d" % k, T.osc[4 * k:4 * k + 4, 0:C], T.ts3[32 * k:32 * k + 4, 0:C], ["ts3"], [], 2)
 
-    def gap(d, c):
-        return d["late"] + (0.0 if c["q"] == "n" else SAME if d["q"] == c["q"] else CROSS)
+    def gap(d, c, k=0):
+        return d["lates"][k] + (0.0 if c["q"] in "nd" else SAME[k] if d["q"] == c["q"] else CROSS[k])
 
     users = [[] for _ in calls]
     for i, c in enumerate(calls):
@@ -547,7 +551,7 @@ def rank_program(g, core, T, topo):
         c["in"] = [(calls[d], gap(calls[d], c), calls[d]["q"] != c["q"]) for d in c["deps"]]
 
     def arrange(ahead, margin, give):
-        free = {q: 0.0 for q in "vatpsn"}
+        free = {q: 0.0 for q in "vatpsnd"}
         left = [len(c["deps"]) for c in calls]
         ready = [i for i, n in enumerate(left) if n == 0]
         order = []
@@ -584,17 +588,84 @@ def rank_program(g, core, T, topo):
                 left[u] -= 1
                 if left[u] == 0:
                     ready.append(u)
-        return max(c["end"] + c["late"] for c in calls), order
+        return order
 
-    order = [] if ORDER else min(arrange(*rule) for rule in RULES)[1]
+    def polish(cur, rounds):
+        n, qs, deps, weigh = len(calls), [c["q"] for c in calls], [c["deps"] for c in calls], (1.5, 1.0)
+        sets = [([c["holds"][k] for c in calls], [c["lates"][k] for c in calls], [[(d, gap(calls[d], c, k)) for d in c["deps"]] for c in calls],
+                 [[(u, gap(calls[i], calls[u], k)) for u in users[i]] for i in range(n)]) for k in (1, 2)]
+
+        def sweep(seq, hold, edges, floor, known, free):
+            for i in seq:
+                t = max(free.get(qs[i], 0.0), floor[i])
+                for d, w in edges[i]:
+                    if known[d] + w > t:
+                        t = known[d] + w
+                known[i] = t = t + hold[i]
+                if qs[i] != "n":
+                    free[qs[i]] = t
+            return known
+
+        def moved(seg, up):
+            one, other = (seg[-1], seg[0]) if up else (seg[0], seg[-1])
+            along, seen = {one}, set()
+            for x in (seg[::-1] if up else seg):
+                if x in along or qs[x] in seen:
+                    along.add(x)
+                    along.update(deps[x] if up else users[x])
+                    if qs[x] not in (qs[one], "n"):
+                        seen.add(qs[x])
+            return None if other in along else sorted(seg, key=lambda x: (x in along) != up)
+
+        zero, barred, seed, best = [0.0] * n, {}, 1, None
+        for step in range(rounds + 1):
+            ends = [sweep(cur, h, fin, zero, [0.0] * n, {}) for h, _, fin, _ in sets]
+            tails = [sweep(cur[::-1], h, out, late, [0.0] * n, {}) for h, late, _, out in sets]
+            score = sum(w * max(t) for w, t in zip(weigh, tails))
+            if best is None or score < best[0]:
+                best = (score, cur)
+            hold, en, tl = sets[step % 2][0], ends[step % 2], tails[step % 2]
+            place, span = {i: j for j, i in enumerate(cur)}, max(tl)
+            line = {q: [i for i in cur if qs[i] == q] for q in "vatpsd"}
+            moves = []
+            for s in line.values():
+                for j in range(1, len(s)):
+                    u, v = s[j - 1], s[j]
+                    if en[v] - hold[v] + tl[v] > span - 1e-6 and en[v] - hold[v] - en[u] < 1e-9:
+                        moves += [(s[j - r], v, True) for r in range(1, min(REACH, j) + 1)] + [(u, s[j + r], False) for r in range(1, min(REACH, len(s) - j))]
+            rated = []
+            for u, v, up in moves:
+                seed = (seed * 1103515245 + 12345) % 2 ** 31
+                seg = moved(cur[place[u]:place[v] + 1], up) if u >= loads and seed % len(moves) < 60 and barred.get((u, v), -1) <= step else None
+                if seg is None:
+                    continue
+                guess, edge = 0.0, {}
+                for q, s in line.items():
+                    mine = [x for x in seg if qs[x] == q]
+                    if mine:
+                        edge[q] = (s.index(min(mine, key=place.get)) - 1, s.index(max(mine, key=place.get)) + 1)
+                for j, (h, late, fin, out) in enumerate(sets):
+                    e2 = sweep(seg, h, fin, zero, list(ends[j]), {q: ends[j][line[q][a]] for q, (a, _) in edge.items() if a >= 0})
+                    t2 = sweep(seg[::-1], h, out, late, list(tails[j]), {q: tails[j][line[q][b]] for q, (_, b) in edge.items() if b < len(line[q])})
+                    guess += weigh[j] * max(e2[x] - h[x] + t2[x] for x in seg)
+                rated.append((guess, seed, seg, u, v))
+            if not rated:
+                barred = {}
+                continue
+            _, _, seg, u, v = min(rated)
+            cur = cur[:place[u]] + seg + cur[place[v] + 1:]
+            barred[(v, u)] = step + 5 + seed % 11
+        return best
+
+    if not ORDER:
+        ORDER.extend(polish(min(polish(arrange(*rule), ROUNDS[0]) for rule in RULES)[1], ROUNDS[1])[1])
 
     know = {q: {} for q in queue}
-    ORDER.extend(order)
     for k, i in enumerate(ORDER):
         c = calls[i]
         c["end"] = k
         q = c["q"]
-        if q == "n":
+        if q in "nd":
             c["tok"], c["then"] = c["emit"](), {}
             continue
         need = {}

@@ -1,14 +1,15 @@
+import math
 import numpy as np
 from concourse.mybir import dt, AluOpType as OP, ActivationFunctionType as AF
 
 C = 384
 H = C // 2
 U = 2.0 ** -7
-SIDE = 703
 STEPS = (1, 2, 4, 8, 16, 32, 64, 64)
-RUNS = ((0, 256), (256, C))
+SIDE = 703
+WHOLE, HALVES, RUNS, THIRDS = ((0, C),), ((0, H), (H, C)), ((0, 256), (256, C)), ((0, 128), (128, 256), (256, C))
+SENT, ALONG, LAST = RUNS, WHOLE, THIRDS
 SHARED = (2, 3)
-PIECE = 128
 SCRATCH = {}
 AT = {}
 
@@ -27,51 +28,58 @@ def _wrapped(buf, names, dtype):
 
 TABLES = ((0, 512, tuple(range(8))), (3968, C, tuple(range(0, 64, 8))), (7040, C, (0, 64, 128, "p", "p64", "p128")))
 ROW = {n: a + w * i for a, w, ns in TABLES for i, n in enumerate(ns) if n}
+MORE = ((3, 1, 2), (5, 1, 4), (6, 2, 4), (7, 3, 4), (24, 8, 16), (40, 8, 32), (48, 16, 32), (56, 24, 32), (128, 64, 64), ("p64", "p", 64), ("p128", "p64", 64))
 SLOTS = 16
 _sb("pw2", 9344, "bfloat16")
-_sb("iot prow qrow murow pmr drow mrow vrow markp k16f hf hm h0 h1 hdb th1 tg1", C, "bfloat16")
+_sb("iot prow qrow murow pmr hf hm h0 h1 hd hd2 th1 tg1 drow mrow vrow markp k16f", C, "bfloat16")
 _sb("hs gs th2 tg2", C + 32, "bfloat16")
 _sb("lrow", C + 16, "bfloat16")
 _sb("hh fq tau ip order mk sf sr unit", 2 * C, "bfloat16")
 _sb("sums", 2 * C + 16, "bfloat16")
-_sb("lv", C, "float16")
-_sb("dl k16 fr le", 2 * C, "float16")
-_sb("sc", SLOTS * 2 * C, "float16")
+_sb("lv k16", C, "float16")
+_sb("dl fr le", 2 * C, "float16")
+_sb("sc", SLOTS * C, "float16")
+_sb("pf", 3 * C + 32, "float16")
 _sb("kseed", 32, "bfloat16")
-_sb("ssb ssp smr shp ysb qr3 scf key0 key1 ka kb khd", C, "float32")
+_sb("ssb ssp smr shp ysb qr3 scf key0 key1 ka kb kd kd2", C, "float32")
 _sb("idc laid", 2 * C, "float32")
-_sb("rsb rl3 mg", 4 * C, "float32")
-_sb("x0 xn xe z ze fo fp fa", 4 * C, "bfloat16")
+_sb("rsb mg", 4 * C, "float32")
+_sb("x0 xn z fo fp fa", 4 * C, "bfloat16")
 _sb("ut vt", 512, "bfloat16")
-_sb("et", 2048, "bfloat16")
+_sb("et", 516, "bfloat16")
 _sb("eq wq", 512, "float8_e4m3fn_x4")
-_sb("es wsc", 512, "uint8")
+_sb("es ws_", 512, "uint8")
 _sb("uq vq up", 128, "float8_e4m3fn_x4")
 _sb("us vs ups", 128, "uint8")
 _sb("tq0 tq1 tq2 tq3 lq1 lq2 lq3 zq1 zq2 zq3", C, "float8_e4m3fn_x4")
-_sb("ts0 ts1 ts2 ts3 lp1 lp2 lp3 zs1 zs2 zs3", C, "uint8")
-_sb("pli qli mli c24i", 24, "int32")
+_sb("ts0 ts1 ts2 ts3 ls1 ls2 ls3 zs1 zs2 zs3", C, "uint8")
+_sb("mli c24i", 24, "int32")
+_wrapped("pq", "pli qli", "int32")
+_sb("rpq", 48, "int32")
 _sb("pi qi q32 u8i", 8, "int32")
 _sb("j16 cols", 16, "float32")
 _sb("uoff", 8, "uint16")
-_sb("rl", 48, "uint16")
+_sb("rl", 24, "uint16")
+_sb("c0 co m0 m1f mo", 72, "float32")
+_sb("e0 e1 eo", 96, "float32")
 _wrapped("wi", "kw di ei d0i d1i d2i", "int32")
-_wrapped("wf", "cw pmc mupf lo_ hi_ mn gt idf k1 k2 hk f1 f3 f2 f4 hd_ h2 sg a0 v0 v1 sp lw w1 pos2 pos1 clf clr e0 g0 y0 gl tg "
-         "ep eq0 ep2 eq2 ev ne ng nw cur if0 d1f d2f", "float32")
-_wrapped("wl", "pw qw muw lpw hpw mupw pmpw idl uw lol vl spl p2l p1l el opl tl ix l2 l4 l8 l16 l32 l64 a1 a2 a3 m1 m2 m3", "uint16")
-_wrapped("wr", "ra1 ra2 ra3 rm1 rm2 rm3", "uint16")
+_wrapped("wf", "cw mupf lo_ hi_ k1 k2 f3 ng nw if0 d1f d2f pmc mn gt idf sg a0 v0 v1 sp w1 pos2", "float32")
+_wrapped("wl", "pw qw muw lpw hpw mupw pmpw uw ix idl lol vl spl p2l p1l el opl tl rp rq ra1 l2 l4 l8 l16 l32 l64 a1 a2 a3 m1 m2 m3", "uint16")
+_wrapped("wr", "ra2 ra3 rm1 rm2 rm3", "uint16")
 _sb("pa pb", 2048, "float32", "psum")
-DMAS = ["dpl", "dql", "dml", "dx", "du_", "dv", "dwc", "dws", "doc0", "doc1", "dos0", "dos1", "dos2", "dos3", "dy0", "dy1", "dqo"] + ["did%d" % k for k in range(5)]
-SEMAPHORES = ["sv", "sa", "st", "sp", "ls"] + ["%s%d" % (k, s) for s in (1, 2, 3) for k in ("at", "aa", "am")] + DMAS
+DMAS = "dpl dql dml dx0 dx1 du_ dv dwc dws doc0 doc1 doc2 dos0 dos1 dos2 dos3 dy0 dy1 dy2 dqo did0 did1 did2 did3 did4".split()
+SEMAPHORES = ["sv", "sa", "st", "sp", "ls"] + ["%s%d" % (k, s) for s in (1, 2, 3) for k in ("at0", "at1", "at2", "ap", "aa", "am")] + DMAS
+WIDE = {"bfloat16": 2, "float16": 2, "uint16": 2, "uint8": 1}
 
-CYC, GATHER, SCATTER, LEAST, PE = [np.array(v) for v in ((0.00095, 0.00083, 0.0012), (0.0015, 0.0013, 0.0023), (0.0036, 0.0032, 0.006), (0.065, 0.054, 0.075), (0.00125, 0.00125, 0.0016))]
-SAME, CROSS = (0.18, 0.15, 0.18), (0.24, 0.21, 0.24)
-LOAD, RATE, ISSUE, FLIGHT, LIST, LAST = 1.5, 185.0, 0.5, 1.4, 0.8, np.array((0.1, 0.6, 0.6))
-TILE, COLD = np.array((3.5, 4.0, 6.0)), 6.0
-RULES = [(ahead, margin, {"v": v, "a": a}) for ahead in (0.03, 0.06, 0.1) for margin in (0.1, 0.2) for v, a in ((2.0, 0.1), (10.0, 0.5))]
-EARLY, FIRST = 22.0, {"v": 4.0, "a": 0.3}
-ROUNDS, REACH = (150, 1500), 5
-ORDER = []
+FIX = np.array((1.0, 1.0, 1.4))
+CYC = 0.00083 * FIX
+GATHER, SCATTER, PE = CYC * (1.56, 1.15, 1.85), CYC * (3.8, 2.0, 5.0), np.array((0.00125, 0.0014, 0.00166))
+SAME, CROSS, WEIGH = (0.18, 0.14, 0.18), (0.24, 0.25, 0.24), (1.0, 0.4, 1.1)
+LOAD, RATE, START, ISSUE, FLIGHT, LIST = 1.5, 185.0, 0.2, 0.5, np.array((1.8, 2.0, 2.0)), np.array((0.8, 1.0, 0.8))
+TILE, COLD = np.array((5.0, 5.6, 5.0)), np.array((10.3, 10.0, 13.5))
+RULES = [(ahead, margin, {"v": v, "a": a}) for ahead in (0.03, 0.1) for margin in (0.1, 0.2) for v, a in ((2.0, 0.1), (10.0, 0.5))]
+PASSES, TRIES, WIDTH, HEAT, SOFT, DRAG = 26, 2000, 100, 0.05, 0.25, 0.2
+ORDER, MASKS = [], {}
 
 
 def rank_program(g, core, T, topo):
@@ -84,503 +92,533 @@ def rank_program(g, core, T, topo):
     calls = []
     writer, readers = {}, {}
 
-    def meets(name, part, table):
-        d = table.get(name, {})
-        return [d[k] for k in d if part is None or k is None or k == part]
+    def v(n, a=0, e=None, s=1):
+        if n in AT:
+            return (AT[n][0], AT[n][1], AT[n][1] + 24, 1, None)
+        return (n, a, SCRATCH[n][1][1] if e is None else e, s, None)
+
+    def row(n, i=0, a=0, e=C):
+        return v(n, C * i + a, C * i + e)
+
+    def run(n, a=0, e=C):
+        return (AT[n][0], AT[n][1] + a // 16, AT[n][1] + e // 16, 1, None)
+
+    def along(win, lst):
+        return win[:4] + (lst,)
+
+    def cut(w, a, e):
+        return (w[0], w[1] + a * w[3], min(w[2], w[1] + e * w[3]), w[3], None)
+
+    def ap(w):
+        if not isinstance(w, tuple):
+            return w
+        x = T[w[0]][:, w[1]:w[2]:w[3]] if w[3] > 0 else T[w[0]][:, w[2] - 1:w[1] - 1 if w[1] else None:-1]
+        return x.indirect(ap(w[4])) if w[4] else x
+
+    def size(w):
+        return 16 * size(w[4]) if w[4] else len(range(w[1], w[2], abs(w[3])))
+
+    def touched(ws):
+        out = []
+        for w in ws:
+            if isinstance(w, tuple):
+                n, a, e, s, lst = w
+                if SCRATCH[n][0] == "psum":
+                    a, e, s = a // 512 * 512, -(-e // 512) * 512, 1
+                if (a, e, s) not in MASKS:
+                    MASKS[a, e, s] = sum(1 << i for i in range(a, e, abs(s)))
+                out += [(n, MASKS[a, e, s])] + touched([lst])
+        return out
 
     def add(q, reads, writes, hold, late, emit, after=()):
-        reads = [x if isinstance(x, tuple) else (x, None) for x in reads]
-        writes = [x if isinstance(x, tuple) else (x, None) for x in writes]
-        deps = set(after)
-        for n, p in reads + writes:
-            deps.update(meets(n, p, writer))
-        for n, p in writes:
-            for rs in meets(n, p, readers):
-                deps.update(rs)
-        me = len(calls)
-        hold, late = [[float(x) for x in v + np.zeros(3)] for v in (hold, late)]
-        calls.append({"q": q, "deps": sorted(deps), "hold": hold[0], "late": late[0], "holds": hold, "lates": late, "emit": emit})
-        for n, p in reads:
-            readers.setdefault(n, {}).setdefault(p, []).append(me)
-        for n, p in writes:
-            w, r = writer.setdefault(n, {}), readers.setdefault(n, {})
-            if p is None:
-                w.clear()
-                r.clear()
-            r[p] = []
-            w[p] = me
+        writes, reads = touched(writes), touched(reads)
+        deps, turns, me = set(after), set(), len(calls)
+        for n, m in reads + writes:
+            deps.update(c for k, c in writer.get(n, []) if k & m)
+        for n, m in writes:
+            deps.update(c for k, c in readers.get(n, []) if k & m)
+        for n, m in reads:
+            if SCRATCH[n][0] == "psum":
+                turns.update([c for k, c in readers.get(n, []) if k & m][-1:])
+        hold = {k: [float(x) for x in h + np.zeros(3)] for k, h in hold.items()}
+        calls.append({"q": q, "deps": sorted(deps | turns), "turns": turns - deps, "holds": hold, "lates": [float(x) for x in late + np.zeros(3)], "emit": emit})
+        for n, m in writes:
+            writer[n] = [(k & ~m, c) for k, c in writer.get(n, []) if k & ~m] + [(m, me)]
+            readers[n] = [(k & ~m, c) for k, c in readers.get(n, []) if k & ~m]
+        for n, m in reads:
+            readers.setdefault(n, []).append((m, me))
         return me
 
     count = {"sv": 0, "sa": 0, "st": 0, "sp": 0}
+    line = []
 
-    def op(q, reads, writes, hold, call, *args, after=(), **kw):
-        def emit():
-            count[own[q]] += 1
-            call(*args, **kw).then_inc(T.sem[own[q]], 1)
-            return own[q], count[own[q]]
-        return add(q, reads, writes, np.maximum(hold, LEAST), 0.0, emit, after)
+    def op(q, out, ins, forms):
+        def emit(k):
+            _, call, args, kw = forms[k]
+            count[own[k]] += 1
+            call(*[ap(x) for x in args], **{n: ap(x) for n, x in kw.items()}).then_inc(T.sem[own[k]], 1)
+            return own[k], count[own[k]]
+        behind = line[:1] if q == "p" else []
+        me = add(q, ins + [w[4] for w in out], [w[:4] + (None,) for w in out], {k: np.maximum(f[0], 64 * CYC) for k, f in forms.items()}, 0.0, emit, behind)
+        calls[me]["turns"].update(behind)
 
     def dma(q, sem, out, in_, reads, writes, kib, after=()):
-        def emit():
+        def emit(k):
             count[sem] = 16
             queue[q].dma_start(out, in_).then_inc(T.sem[sem], 16)
             return sem, 16
-        first = add(q, reads, writes, 0.1, LOAD, emit, after)
-        return add("d", reads, writes, kib / RATE, 0.0, lambda: (sem, 16), [first])
+        first = add(q, reads, writes, {q: START}, LOAD, emit, after)
+        return add("d", reads, writes, {"d": kib / RATE}, 0.0, lambda k: (sem, 16), [first])
 
     sent = [0]
 
-    def send(dst, sem, out, in_, reads, first=False):
-        def emit():
+    def send(dst, sem, out, in_):
+        codes, ne = SCRATCH[in_[0]][2].startswith("float8"), len(topo.engines(core, dst))
+
+        def emit(k):
             rid, pid, _ = topo.addr(dst)
-            g.remote_dma(out, in_, T.sem[sem], T.sem.ls, pid, rid, topo.mask(core, dst))
-            sent[0] += len(topo.engines(core, dst))
-        return add("p", reads, [], ISSUE + (FLIGHT if first else 0.0), 0.0, emit)
+            g.remote_dma(*[ap(w).bitcast(dt.uint8) if codes else ap(w) for w in (out, in_)], T.sem[sem], T.sem.ls, pid, rid, topo.mask(core, dst))
+            sent[0] += ne
 
-    def arrive(sem, n, names, sends, late):
-        def emit():
-            count[sem] = n
-            return sem, n
-        return add("n", [], names, 0.0, late, emit, sends)
+        def landed(k):
+            count[sem] = ne
+            return sem, ne
+        call = add("p", [in_], [], {"p": ISSUE + (0.0 if line else COLD)}, FLIGHT, emit, line[:1])
+        calls[call]["turns"].update(line[:1])
+        line[:] = [call, add("n", [], [out], {"n": np.maximum(LIST, TILE * size(in_) * (4 if codes else 1) / (5 * C))}, 0.0, landed, [call] + line[1:])]
 
-    def sl(n, i=None, w=C):
-        if n in AT:
-            buf, o = AT[n]
-            return T[buf][:, o:o + 24]
-        return T[n][:, :] if i is None else T[n][:, w * i:w * i + w]
+    def pace(out, *ins):
+        if out[4] or ins and ins[0][4]:
+            return 0.05 * FIX + size(out) * (SCATTER if out[4] else GATHER)
+        return size(out) * CYC * (0.5 if all(WIDE.get(SCRATCH[w[0]][2]) == 2 for w in (out,) + ins) else 1.0)
 
-    def run(n, a, e):
-        buf, o = AT[n]
-        return T[buf][:, o + a // 16:o + e // 16]
+    def named(x):
+        return v(x) if isinstance(x, str) else x
 
-    def gath(how, out, win, lst, o0=0, wreg=None, wcols=None, **kw):
-        w = T[win][:, wcols[0]:wcols[1]] if wcols else sl(win)
-        n = C // len(how)
-        for k, q in enumerate(how[::-1]):
-            dst, src = T[out][:, o0 + n * k:o0 + n * k + n], w.indirect(run(lst, n * k, n * k + n))
-            reads, regs = (wreg or [win]) + [lst if n == C else (lst, k)], halves(out, o0) if n == C else [halves(out, o0)[k]]
-            if q == "a":
-                op("a", reads, regs, 0.065 + n * GATHER, A.activation, dst, src, AF.Copy, **kw)
-            else:
-                op("v", reads, regs, 0.05 + n * GATHER, V.tensor_copy, dst, src)
+    def tt(out, a, o, b):
+        out, a, b = named(out), named(a), named(b)
+        t = pace(out, a) if a[4] else size(out) * CYC * (1 if "psum" in (SCRATCH[a[0]][0], SCRATCH[b[0]][0]) else 2)
+        op("v", [out], [a, b], {"v": (t, V.tensor_tensor, (out, a, b, o), {})})
 
-    def halves(n, o0=0):
-        return [(n, (o0, 0)), (n, (o0, 1))]
+    def scalars(out, a, s1, o0, s2=None, o1=None):
+        return (pace(out, a), V.tensor_scalar, (out, a, s1, s2, o0) + (() if o1 is None else (o1,)), {})
 
-    def fused(out, oreg, win, wreg, lst, o, in1, ireg):
-        op("v", wreg + [lst] + ireg, oreg, 0.05 + C * GATHER, V.tensor_tensor, out, win.indirect(sl(lst)), in1, o)
+    def ts(out, a, s1, o0, s2=None, o1=None):
+        op("v", [named(out)], [named(a), s1, s2], {"v": scalars(named(out), named(a), s1, o0, s2, o1)})
 
-    def copy_a(out, reads, writes, in_, n=C, func=AF.Copy, **kw):
-        op("a", reads, writes, n * CYC, A.activation, out, in_, func, **kw)
+    def copy(out, a):
+        out, a = named(out), named(a)
+        op("v", [out], [a], {"v": (pace(out, a), V.tensor_copy, (out, a), {})})
+
+    def fill(out, value):
+        op("v", [out], [], {"v": (pace(out), V.memset, (out, value), {})})
+
+    def scan(out, d0, d1, o0, o1, first=0.0):
+        op("v", [out], [d0, d1], {"v": (pace(out, d0, d1), V.tensor_tensor_scan, (out, d0, d1, first, o0, o1), {})})
+
+    def act(out, a, func, **kw):
+        return (0.065 * FIX + size(out) * GATHER if a[4] else 0.02 + size(out) * CYC, A.activation, (out, a, func), kw)
+
+    def move(q, out, a, scale=None, bias=None):
+        out, a = named(out), named(a)
+        kw = {n: x for n, x in (("scale", scale), ("bias", bias)) if x}
+        steps = [y for x, o in ((scale, OP.mult), (bias, OP.add)) if x for y in (x, o)]
+        op(q, [out], [a], {"a": act(out, a, AF.Copy, **kw), "v": scalars(out, a, *steps) if kw else (pace(out, a), V.tensor_copy, (out, a), {})})
+
+    def gather(out, win, lst, runs=WHOLE, how="va", **kw):
+        for q, (a, e) in zip(how[-len(runs):], runs):
+            move(q, cut(named(out), a, e), along(named(win), run(lst, a, e)), **kw)
+
+    def col(i):
+        return v("cols", i, i + 1)
 
     turn = [0]
 
-    def pick(row, rreg, n=C):
+    def pick(w):
         turn[0] = k = (turn[0] + 1) % SLOTS
-        op("v", rreg + [("k16", 0) if n <= C else "k16"], [("sc", k)], n * CYC / 2, V.tensor_tensor_scan, T.sc[:, 2 * C * k:2 * C * k + n], T.k16[:, 0:n], row, 0.0, OP.add, OP.min)
-        return ("sc", k), T.sc[:, 2 * C * k + 15:2 * C * k + n:16]
+        o, n = C * k, size(w)
+        scan(v("sc", o, o + n), v("k16", 0, n), w, OP.add, OP.min)
+        return v("sc", o + 15, o + n, 16)
 
-    def listed(buf, o0, lst, parts=1):
-        n = C // parts
-        for k in range(parts):
-            cv, got = pick(T[buf][:, o0 + n * k:o0 + n * k + n], halves(buf, o0) if n == C else [halves(buf, o0)[k]], n)
-            op("v", [cv, ("cols", 0)], [lst if n == C else (lst, k)], 0, V.tensor_scalar, run(lst, n * k, n * k + n), got, T.cols[:, 0:1], None, OP.add)
+    def listed(w, lst, runs=WHOLE):
+        for a, e in runs:
+            ts(run(lst, a, e), pick(cut(w, a, e)), col(0), OP.add)
 
-    def small(out, in0, o, in1):
-        op("v", [in0, in1], [out], 0, V.tensor_tensor, sl(out), sl(in0), sl(in1), o)
+    def pack(out, plane, x):
+        op("v", [out, plane], [x], {"v": (0.012 * FIX + 1.06 * size(out) * CYC, V.quantize_mx, (out, plane, x), {})})
 
-    def ts(out, in0, s1, o0, s2=None, o1=None):
-        reads = [in0] + [s for s in (s1, s2) if isinstance(s, tuple)]
-        s1, s2 = [T.cols[:, s[1]:s[1] + 1] if isinstance(s, tuple) else s for s in (s1, s2)]
-        op("v", reads, [out], 0, V.tensor_scalar, sl(out), sl(in0), s1, s2, *([o0] if o1 is None else [o0, o1]))
+    def quant(q, x, a=0, e=C):
+        pack(v(q, a, e), v(q.replace("q", "s"), a, e), v(x, 4 * a, 4 * e))
 
-    def vcopy(out, in_):
-        op("v", [in_], [out], 0, V.tensor_copy, sl(out), sl(in_))
+    def bank(n, b, e=C):
+        return v(n, 512 * b, 512 * b + e)
 
-    def quant(q, s, x, a=0, n=C, part=None, xreg=None):
-        op("v", xreg or [x], [(q, part), (s, part)], 0.015 + 1.1 * n * CYC, V.quantize_mx, T[q][:, a:a + n], T[s][:, a:a + n], T[x][:, 4 * a:4 * a + 4 * n])
-
-    def mm(bank, lq, lqs, a, rq, rs, b=0, n=C, part=None):
-        op("t", [lq, lqs, (rq, part), (rs, part)], [bank], (n + 16) * PE, M.matmul_mx, T[bank[0]][:, 512 * bank[1]:512 * bank[1] + n],
-           T[lq][:, a:a + 128], T[lqs][:, a:a + 128], T[rq][:, b:b + n], T[rs][:, b:b + n], True, True)
-
-    def bank(b, n=C):
-        return T[b[0]][:, 512 * b[1]:512 * b[1] + n]
+    def mm(out, lq, ls, b, rq, a=0, e=C):
+        sides = [v(lq, 128 * b, 128 * b + 128), v(ls, 128 * b, 128 * b + 128), v(rq, a, e), v(rq.replace("q", "s"), a, e)]
+        op("t", [out], sides, {"t": ((e - a + 16) * PE, M.matmul_mx, [out] + sides + [True, True], {})})
 
     def power(n):
-        return T.pw2[:, ROW[n]:ROW[n] + C], halves("pw2", ROW[n])
+        return v("pw2", ROW[n], ROW[n] + C)
 
-    dma("s", "dpl", sl("pli"), T.pl[:, :], [], ["pli"], 12)
-    dma("s", "dql", sl("qli"), T.ql[:, :], [], ["qli"], 12)
-    dma("a", "dml", sl("mli"), T.ml[:, :], [], ["mli"], 12)
-    dma("s", "du_", sl("ut"), T.u[:, :], [], ["ut"], 128)
-    later = [dma("s", "dx", sl("x0"), T.x[:, :], [], ["x0"], 384)]
-    for sem, out, in_, name, kib in (("dwc", T.wq[:, :].bitcast(dt.uint8), T.wc, "wq", 256), ("dws", sl("wsc"), T.ws, "wsc", 64), ("dv", sl("vt"), T.v, "vt", 128)):
-        dma("s", sem, out, in_[:, :], [], [name], kib, later)
+    dma("s", "dpl", ap(v("pli")), T.pl[:, :], [], [v("pli")], 12)
+    dma("s", "dql", ap(v("qli")), T.ql[:, :], [], [v("qli")], 12)
+    dma("a", "dml", T.mli[:, :], T.ml[:, :], [], [v("mli")], 12)
+    dma("s", "du_", T.ut[:, :], T.u[:, :], [], [v("ut")], 128)
+    later = [dma("s", "dx%d" % k, T.x0[:, 4 * a:4 * e], T.x[:, 4 * a:4 * e], [], [v("x0", 4 * a, 4 * e)], e - a) for k, (a, e) in enumerate(RUNS)][-1:]
+    for sem, out, in_, name, kib in (("dwc", T.wq[:, :].bitcast(dt.uint8), T.wc, "wq", 256), ("dws", T.ws_[:, :], T.ws, "ws_", 64), ("dv", T.vt[:, :], T.v, "vt", 128)):
+        dma("s", sem, out, in_[:, :], [], [v(name)], kib, later)
 
-    def iota(view, reg, pattern, base, cm, cols, after=()):
-        kw = {} if reg in ("pi", "c24i", "u8i") else {"allow_small_or_imprecise_dtypes": True}
-        op("p", [], [reg], 0.13 + 2 * cols * CYC, P.iota, view, pattern, base, cm, after=after, **kw)
+    def iota(out, pattern, base, cm=0):
+        kw = {} if SCRATCH[out[0]][2] == "int32" else {"allow_small_or_imprecise_dtypes": True}
+        op("p", [out], [], {"p": (0.13 * FIX + 2 * size(out) * CYC, P.iota, (out, pattern, base, cm), kw)})
 
-    iota(T.pi[:, 0:1], "pi", [[1, 1]], 0, 1, 1)
-    iota(sl("j16"), "j16", [[1, 16]], 0, 0, 16)
-    iota(sl("c24i"), "c24i", [[16, 24]], 0, 0, 24)
-    iota(sl("iot"), "iot", [[1, C]], -H, 0, C)
+    def select(out, a, pattern, o, base, cm):
+        op("p", [out], [a], {"p": (0.17 * FIX + 2 * size(out) * CYC, P.affine_select, (out, a, pattern, o, 0.0, base, cm), {})})
+
+    iota(v("pi", 0, 1), [[1, 1]], 0, 1)
+    iota(v("j16"), [[1, 16]], 0)
+    iota(v("c24i"), [[16, 24]], 0)
+    iota(v("iot"), [[1, C]], -H)
     loads = len(calls)
-    iota(sl("u8i"), "u8i", [[16, 8]], 0, 0, 8)
-    op("v", [], ["unit"], C * CYC, V.memset, sl("unit"), 1.0)
-    for b in range(4):
-        op("p", ["unit"], [("et", b)], 0.17 + 1024 * CYC, P.affine_select, sl("et", b, 512), T.unit[:, 0:512], [[-1, 512]], OP.is_equal, 0.0, b, 4)
-        quant("eq", "es", "et", 128 * b, 128, b, [("et", b)])
+    iota(v("u8i"), [[16, 8]], 0)
+    fill(v("unit", 0, 516), 1.0)
 
-    def col(i, in0, reg, s1, o0, s2=None, o1=None):
-        op("v", [reg], [("cols", i)], 0, V.tensor_scalar, T.cols[:, i:i + 1], in0, s1, s2, *([o0] if o1 is None else [o0, o1]))
-
-    op("v", ["pi"], ["qi"], 0, V.tensor_scalar, T.qi[:, 0:1], T.pi[:, 0:1], 15, None, OP.bitwise_and)
-    col(5, T.qi[:, 0:1], "qi", 0, OP.add)
-    col(4, T.qi[:, 0:1], "qi", 1, OP.add)
-    col(6, T.qi[:, 0:1], "qi", 15, OP.is_lt, 1024.0, OP.mult)
-    col(0, T.cols[:, 6:7], ("cols", 6), float(H), OP.add)
-    col(1, T.cols[:, 6:7], ("cols", 6), 512.0, OP.mult)
-    col(2, T.cols[:, 6:7], ("cols", 6), 512.0, OP.mult, -447.0, OP.add)
-    col(3, T.cols[:, 6:7], ("cols", 6), 512.0, OP.mult, 767.5 - SIDE, OP.add)
-    col(8, T.cols[:, 0:1], ("cols", 0), 2.0, OP.mult, 1.0, OP.add)
-    col(9, T.qi[:, 0:1], "qi", 8, OP.is_lt, 1.0, OP.add)
-    col(13, T.qi[:, 0:1], "qi", 8, OP.is_ge, -2.0 ** 90, OP.mult)
-    col(10, T.qi[:, 0:1], "qi", 8, OP.is_ge, 1.0, OP.mult)
-    col(14, T.qi[:, 0:1], "qi", 8, OP.is_ge, 2.0 ** -100, OP.mult)
-    op("v", ["pi"], ["q32"], 0, V.tensor_scalar, T.q32[:, 0:1], T.pi[:, 0:1], 31, None, OP.bitwise_and)
-    col(11, T.q32[:, 0:1], "q32", 16, OP.is_lt, 512.0 / U, OP.mult)
-    col(12, T.q32[:, 0:1], "q32", 16, OP.is_ge, -512.0 / U, OP.mult)
+    place, block = v("qi", 0, 1), v("q32", 0, 1)
+    ts(place, v("pi", 0, 1), 15, OP.bitwise_and)
+    ts(col(5), place, 0, OP.add)
+    ts(col(4), place, 1, OP.add)
+    ts(col(6), place, 15, OP.is_lt, 1024.0, OP.mult)
+    ts(col(0), col(6), float(H), OP.add)
+    ts(col(1), col(6), 512.0, OP.mult)
+    ts(col(2), col(6), 512.0, OP.mult, -447.0, OP.add)
+    ts(col(3), col(6), 512.0, OP.mult, 767.5 - SIDE, OP.add)
+    fill(col(7), 2.0 ** -100)
+    ts(col(8), col(0), 2.0, OP.mult, 1.0, OP.add)
+    ts(col(9), place, 8, OP.is_lt, 1.0, OP.add)
+    ts(col(13), place, 8, OP.is_ge, -2.0 ** 90, OP.mult)
+    ts(col(10), place, 8, OP.is_ge, 1.0, OP.mult)
+    ts(col(14), place, 8, OP.is_ge, 2.0 ** -100, OP.mult)
+    ts(block, v("pi", 0, 1), 31, OP.bitwise_and)
+    ts(col(11), block, 16, OP.is_lt, 2.0 ** 20, OP.mult)
+    ts(col(12), block, 16, OP.is_ge, 512.0 / U - 2.0 ** -4, OP.mult)
+    for k, (a, w, ns) in enumerate(TABLES):
+        dma("s", "did%d" % k, T.pw2[:, a:a + C], T.iot[:, :], [v("iot")], [v("pw2", a, a + C)], 96)
+    ts(run("k1", 0, 256), "j16", col(5), OP.is_equal, 2048.0, OP.mult)
+    ts(run("k2", 0, 256), "j16", col(4), OP.is_equal, -1024.0, OP.mult)
+    tt(v("kseed", 0, 16), run("k1", 0, 256), OP.add, run("k2", 0, 256))
+    ts("cw", "c24i", col(5), OP.add)
+    ts("rl", "c24i", 0.0, OP.mult, col(5), OP.add)
+    move("v", "k16", along(v("kseed", 0, 16), v("rl")))
     for n in ("hs", "gs"):
         for a in (0, C + 16):
-            op("v", [], [(n, "end%d" % a)], 0, V.memset, T[n][:, a:a + 16], 0.0)
-    for k, (a, w, ns) in enumerate(TABLES):
-        dma("s", "did%d" % k, T.pw2[:, a:a + C], sl("iot"), ["iot"], halves("pw2", a), 96)
-    op("v", [], [("lrow", 0)], 0, V.memset, T.lrow[:, 0:1], 0.0)
-    op("v", [], [("cols", 7)], 0, V.memset, T.cols[:, 7:8], 2.0 ** -100)
-    op("v", ["j16", ("cols", 5)], ["k1"], 0, V.tensor_scalar, run("k1", 0, 256), sl("j16"), T.cols[:, 5:6], 2048.0, OP.is_equal, OP.mult)
-    op("v", ["j16", ("cols", 4)], ["k2"], 0, V.tensor_scalar, run("k2", 0, 256), sl("j16"), T.cols[:, 4:5], -1024.0, OP.is_equal, OP.mult)
-    op("v", ["k1", "k2"], ["kseed"], 0, V.tensor_tensor, T.kseed[:, 0:16], run("k1", 0, 256), run("k2", 0, 256), OP.add)
-    ts("cw", "c24i", ("cols", 5), OP.add)
-    op("v", ["c24i", ("cols", 5)], ["rl"], 0, V.tensor_scalar, T.rl[:, 0:24], sl("c24i"), 0.0, T.cols[:, 5:6], OP.mult, OP.add)
-    seed = T.kseed[:, 0:16].indirect(T.rl[:, 0:24])
-    op("v", ["kseed", "rl"], [("k16", 0)], 0.05 + C * GATHER, V.tensor_copy, T.k16[:, 0:C], seed)
-    op("a", ["kseed", "rl"], [("k16", 1)], 0.065 + C * GATHER, A.activation, T.k16[:, C:2 * C], seed, AF.Copy)
-    op("v", [("k16", 0)], ["k16f"], H * CYC, V.tensor_scalar, sl("k16f"), T.k16[:, 0:C], 512.0, None, OP.mult)
+            move("a", v(n, a, a + 16), v("unit", 0, 16))
+    for a in range(C, 7 * 512, 512):
+        move("a", v("pw2", a, a + 512 - C), v("unit", 0, 512 - C))
+    move("a", v("e0", 3, 96, 4), v("unit", 0, 24), scale=-1.0)
+    move("a", v("e0", 0, 96, 4), v("unit", 0, 24), bias=-1.0)
+    ts(v("e0", 1, 96, 8), v("e0", 0, 96, 8), col(11), OP.add)
+    ts(v("e0", 2, 96, 8), v("e0", 0, 96, 8), 2.0 ** -4, OP.add, col(12), OP.add)
+    ts(v("e0", 5, 96, 8), v("e0", 1, 96, 8), -1.0, OP.mult, 2.0 ** 20, OP.add)
+    ts(v("e0", 6, 96, 8), v("e0", 2, 96, 8), -1.0, OP.mult, 512.0 / U + 2.0 ** -4, OP.add)
+    copy(v("e1", 2, 96, 4), "cw")
+    iota(v("c0"), [[0, 24], [2, 3]], 0)
+    ts(v("pf", 61, 3 * C + 32, 48), v("c0", 1, 72, 3), col(6), OP.mult)
 
-    op("v", ["u8i"], ["uoff"], 0, V.tensor_copy, sl("uoff"), T.u8i[:, 0:8])
-    quant("uq", "us", "ut", n=128)
-    op("v", ["uq", "uoff"], ["up"], 0.05 + 128 * GATHER, V.tensor_copy, T.up[:, :].bitcast(dt.uint32), T.uq[:, :].bitcast(dt.uint32).indirect(T.uoff[:, :]))
-    op("a", ["us", "uoff"], ["ups"], 0.065 + 128 * GATHER, A.activation, sl("ups"), T.us[:, :].indirect(T.uoff[:, :]), AF.Copy)
-    quant("vq", "vs", "vt", n=128)
+    copy("uoff", "u8i")
+    quant("uq", "ut", 0, 128)
+    words = [T.up[:, :].bitcast(dt.uint32), T.uq[:, :].bitcast(dt.uint32).indirect(T.uoff[:, :])]
+    op("v", [v("up")], [v("uq"), v("uoff")], {"v": (0.05 * FIX + 128 * GATHER, V.tensor_copy, words, {})})
+    move("a", "ups", along(v("us"), v("uoff")))
+    quant("vq", "vt", 0, 128)
 
-    vcopy("pw", "pli")
-    vcopy("qw", "qli")
-    vcopy("muw", "mli")
-    gath("av", "qrow", "iot", "qw")
-    gath("av", "pw2", "qrow", "pw", o0=ROW[1])
-    gath("a", "prow", "iot", "pw")
-    dma("s", "did4", power("p")[0], sl("prow"), ["prow"], power("p")[1], 96)
-    dma("s", "did3", sl("ip", 1), sl("prow"), ["prow"], [("ip", 1)], 96)
-    small("pmc", "pli", OP.subtract, "cw")
-    small("mn", "pli", OP.min, "cw")
+    copy("pw", "pli")
+    copy("qw", "qli")
+    copy("muw", "mli")
+    gather("qrow", "iot", "qw", HALVES)
+    gather(power(1), "qrow", "pw", HALVES)
+    gather("prow", "iot", "pw")
+    dma("s", "did3", ap(power("p")), T.prow[:, :], [v("prow")], [power("p")], 96)
+    tt(v("e1", 3, 96, 4), "pli", OP.add, "cw")
+    gather("murow", "iot", "muw")
+    fill(v("dl", 0, 2 * C, 2), 0.0)
+    tt(v("dl", 1, 2 * C, 2), along(v("murow"), v("pw")), OP.subtract, "prow")
+    ts("f3", pick(v("dl", 1, 2 * C, 2)), col(6), OP.add)
+    tt("mupf", "f3", OP.add, "pli")
+    copy("mupw", "mupf")
+    tt("lo_", "mupf", OP.min, "pli")
+    tt("hi_", "mupf", OP.max, "pli")
+    copy(run("lpw", 0, 2 * C), run("lo_", 0, 2 * C))
+    gather("pmr", "prow", "mupw")
+    listed(v("pmr"), "pmpw")
+    tt("pmc", "pli", OP.subtract, "cw")
+    tt("mn", "pli", OP.min, "cw")
     ts("gt", "pmc", 0.0, OP.is_lt, float(C), OP.mult)
-    small("idf", "mn", OP.add, "gt")
-    vcopy("idl", "idf")
-    gath("a", "murow", "iot", "muw")
-    op("v", ["iot"], [("dl", 0)], H * CYC, V.tensor_scalar, T.dl[:, 0:2 * C:2], sl("iot"), 0.0, None, OP.mult)
-    fused(T.dl[:, 1:2 * C:2], [("dl", 1)], sl("murow"), ["murow"], "pw", OP.subtract, sl("prow"), ["prow"])
-    cv, got = pick(T.dl[:, 1:2 * C:2], [("dl", 1)])
-    op("v", [cv, ("cols", 6)], ["f3"], 0, V.tensor_scalar, sl("f3"), got, T.cols[:, 6:7], None, OP.add)
-    small("mupf", "f3", OP.add, "pli")
-    vcopy("mupw", "mupf")
-    small("lo_", "mupf", OP.min, "pli")
-    small("hi_", "mupf", OP.max, "pli")
-    vcopy("lpw", "lo_")
-    vcopy("hpw", "hi_")
-    gath("a", "pmr", "prow", "mupw")
-    listed("pmr", 0, "pmpw")
+    tt("idf", "mn", OP.add, "gt")
+    copy("idl", "idf")
+    move("a", "k16f", "k16", scale=512.0)
+    dma("s", "did4", ap(row("ip", 1)), T.prow[:, :], [v("prow")], [row("ip", 1)], 96)
 
-    def behind(sends):
-        for a in range(C, 7 * 512, 512):
-            iota(T.pw2[:, a:a + 512 - C], ("pw2", a), [[0, 512 - C]], 0, 0, 512 - C, sends)
-        op("p", ["prow"], [("fq", 1)], 0.17 + 2 * C * CYC, P.affine_select, T.fq[:, 1:2 * C:2], sl("prow"), [[0, C]], OP.is_gt, 0.0, 1, 0, after=sends)
-        iota(sl("ip", 0), ("ip", 0), [[1, C]], -H, 0, C, sends)
-        iota(sl("idc"), "idc", [[SIDE, 2], [1024, C]], -1, 0, 2 * C, sends)
-        gath("a", "key0", "idc", "idl", bias=float(H))
-        copy_a(sl("key1"), ["key0"], ["key1"], sl("key0"), bias=-1.0)
-
-    def times(how, to, n, lst):
-        gath(how, "pw2", "pw2", lst, o0=ROW[to], wreg=power(n)[1], wcols=(ROW[n], ROW[n] + C))
+    def behind_first_writes():
+        select(v("et"), v("unit", 0, 516), [[-1, 516]], OP.is_equal, 3, 4)
+        for b in range(4):
+            pack(v("eq", 128 * b, 128 * b + 128), v("es", 128 * b, 128 * b + 128), v("et", 3 - b, 515 - b))
+        select(v("fq", 1, 2 * C, 2), v("prow"), [[0, C]], OP.is_gt, 1, 0)
+        iota(v("idc"), [[SIDE, 2], [1024, C]], -1)
+        gather("key0", "idc", "idl", bias=float(H))
+        move("a", "key1", "key0", bias=-1.0)
+        iota(row("ip"), [[1, C]], -H)
+        iota(v("m0"), [[0, 72]], 0)
+        iota(v("lrow", 0, 16), [[0, 16]], 0)
 
     def powers(s):
-        a, how = "a%d" % s, "a" if s == 1 else "aa"
-        listed("pw2", ROW[1], a, len(how))
+        lists = {n: "l%d" % n if n > 1 else "a%d" % s for n in STEPS}
+        runs = WHOLE if s == 1 else HALVES
+        listed(power(1), lists[1], runs)
         for n in STEPS[:6]:
-            times(how, 2 * n, n, a if n == 1 else "l%d" % n)
-            listed("pw2", ROW[2 * n], "l%d" % (2 * n), len(how))
+            gather(power(2 * n), power(n), lists[n], runs, "aa")
+            listed(power(2 * n), lists[2 * n], runs)
+        for to, n, by in MORE if s == 1 else ():
+            gather(power(to), power(n), lists[by])
+        return lists
 
-    def walk(s, cur, hd, pair, spare, last=None):
+    def walk(lists, cur, near, pair, spare, last, unit, runs, q):
         for i, n in enumerate(STEPS):
-            lst = "a%d" % s if n == 1 else "l%d" % n
-            nxt = pair[cur == pair[0]]
-            for k, (a, e) in enumerate(((0, H), (H, C))):
-                near = spare if i or not hd else hd
-                if near == spare and last:
-                    op("v", [(cur, k) if i else cur], [(spare, k)], H * CYC / 2, V.tensor_scalar, T[spare][:, a:e], T[cur][:, a:e], -n * U, None, OP.add)
-                elif near == spare:
-                    copy_a(T[spare][:, a:e], [(cur, k)], [(spare, k)], T[cur][:, a:e], n=H, bias=float(-n))
-                out, reg = (T[last][:, 16 + a:16 + e], (last, k)) if last and i == 7 else (T[nxt][:, a:e], (nxt, k))
-                op("v", [cur, (lst, k), (near, k) if near == spare else near], [reg], 0.05 + H * GATHER, V.tensor_tensor, out, sl(cur).indirect(run(lst, a, e)), T[near][:, a:e], OP.min)
+            nxt = last if i == 7 else v(pair[i % 2])
+            for a, e in runs:
+                if i < 7 and (i or not near):
+                    move(q, v(spare, a, e), cut(cur, a, e), bias=-n * unit)
+                if i == 6:
+                    move(q, v(spare + "2", a, e), cut(cur, a, e), bias=-2 * n * unit)
+            for a, e in runs:
+                tt(cut(nxt, a, e), along(cur, run(lists[n], a, e)), OP.min, v(spare + "2" if i == 7 else spare if i or not near else near, a, e))
             cur = nxt
-        return cur
 
-    def first_mirror():
-        mm(("pb", 1), "up", "ups", 0, "tq0", "ts0")
-        copy_a(sl("hm"), [("cols", 10), ("cols", 14)], ["hm", ("pb", 1)], bank(("pb", 1)), func=AF.Sign, scale=T.cols[:, 10:11], bias=T.cols[:, 14:15])
-        op("v", [("cols", 9), ("cols", 13)], ["hf", ("pb", 0)], C * CYC, V.tensor_scalar, sl("hf"), bank(("pb", 0)), T.cols[:, 13:14], T.cols[:, 9:10], OP.is_ge, OP.mult)
-        fused(sl("h0"), ["h0"], sl("hm"), ["hm"], "pw", OP.add, sl("hf"), ["hf"])
-        walk(1, "h0", None, ("h0", "h1"), "hdb", "hs")
-        for to, n, lst in ((3, 1, "l2"), (5, 1, "l4"), (6, 2, "l4"), (7, 3, "l4"), (24, 8, "l16"), (40, 8, "l32"), (48, 16, "l32"), (56, 24, "l32"),
-                           (128, 64, "l64"), ("p64", "p", "l64"), ("p128", "p64", "l64")):
-            times("a", to, n, lst)
-        gath("av", "gs", "hs", "pw", o0=16, wcols=(16, 16 + C))
+    def first_mirror(s, lists):
+        for k, (a, e) in enumerate(RUNS):
+            one, two = bank("pb", 2 * k + 1, e - a), bank("pb", 2 * k, e - a)
+            mm(one, "up", "ups", 0, "tq%d" % (s - 1), a, e)
+            mm(two, "up", "ups", 0, "tq%d" % (s - 1), a, e)
+            op("a", [v("hm", a, e)], [one, col(10), col(14)], {"a": act(v("hm", a, e), one, AF.Sign, scale=col(10), bias=col(14))})
+            ts(v("hf", a, e), two, col(13), OP.is_ge, col(9), OP.mult)
+            move("a", v("ssb", a, e), one)
+        for a, e in RUNS:
+            tt(v("h0", a, e), along(v("hm"), run("pw", a, e)), OP.add, v("hf", a, e))
+        walk(lists, v("h0"), None, ("h1", "h0"), "hd", v("hs", 16, 16 + C), U, RUNS, "v")
+        gather(v("gs", 16, 16 + C), v("hs", 16, 16 + C), "pw", HALVES)
         for n in ("h", "g"):
-            op("v", [n + "s"], ["t%s1" % n], H * CYC, V.transpose, sl("t%s1" % n), T[n + "s"][:, 16:16 + C])
-            op("v", [n + "s"], ["t%s2" % n], H * CYC, V.transpose, sl("t%s2" % n), sl(n + "s"))
-        for out, k, t, a in (("ep", 0, "1", 0), ("eq0", 1, "1", 16), ("eq0", 0, "2", 16), ("ep", 1, "2", 32)):
-            o = AT[out][1]
-            op("v", ["th" + t, "tg" + t], [(out, k)], 0, V.tensor_tensor, T.wf[:, o + k:o + 24:2], T["th" + t][:, a:a + 353:32], T["tg" + t][:, a + 8:a + 361:32], OP.subtract)
-        ts("ep2", "ep", ("cols", 11), OP.mult)
-        ts("eq2", "eq0", ("cols", 12), OP.mult)
-        small("ev", "ep2", OP.subtract, "eq2")
-        small("ne", "eq2", OP.subtract, "ep2")
-        small("ei", "ev", OP.max, "ne")
-        small("ng", "ep2", OP.is_lt, "eq2")
-        small("nw", "ng", OP.mult, "pmc")
-        small("cur", "nw", OP.add, "cw")
-        ts("d0i", "ei", 7 * 512, OP.bitwise_and)
-        small("if0", "d0i", OP.add, "cur")
-        vcopy("ix", "if0")
+            for out, a in ((v("t%s1" % n), v(n + "s", 16, 16 + C)), (v("t%s2" % n), v(n + "s"))):
+                op("v", [out], [a], {"v": (pace(out, a), V.transpose, (out, a), {})})
+        for o, t, a in ((0, "1", 0), (1, "2", 16)):
+            tt(v("e1", o, 96, 4), v("th" + t, a, a + 369, 16), OP.subtract, v("tg" + t, a + 8, a + 377, 16))
+        scan(v("eo"), v("e0"), v("e1"), OP.mult, OP.add)
+        tt("ei", v("eo", 2, 96, 4), OP.max, v("eo", 3, 96, 4))
+        tt("ng", v("eo", 2, 96, 4), OP.is_lt, v("eo", 3, 96, 4))
+        ts("d0i", "ei", 8 * 512 - 1, OP.bitwise_and)
+        copy("ix", "d0i")
         for k in (1, 2):
             ts("d%di" % k, "ei", 3 * k, OP.logical_shift_right, 7 * 512, OP.bitwise_and)
-            ts("d%df" % k, "d%di" % k, 0.75, OP.mult, ("cols", 0), OP.add)
+        ts(run("d1f", 0, 2 * C), run("d1i", 0, 2 * C), 0.75, OP.mult, col(0), OP.add)
         ts("nw", "ng", 3.0 * C, OP.mult)
-        small("d2f", "d2f", OP.add, "nw")
+        tt("d2f", "d2f", OP.add, "nw")
         for k, (a, w, ns) in enumerate(TABLES):
-            gath("av", "lv", "pw2", "ix", wreg=[r for i in range(len(ns)) for r in halves("pw2", a + w * i)] + [("pw2", i) for i in range(C, 7 * 512, 512)], wcols=(a, a + w * (len(ns) - 1) + C))
+            gather("lv", v("pw2", a, a + w * (len(ns) - 1) + C), "ix", HALVES)
             if k == 2:
-                return listed("lv", 0, "m1", 2)
-            for j in range(2):
-                f, d, x = [run(n, H * j, H * j + H) for n in ("if0", "d%df" % (k + 1), "ix")]
-                cv, got = pick(sl("lv", j, H), [halves("lv")[j]], H)
-                op("v", [cv, "d%df" % (k + 1)], [("if0", j)], 0, V.tensor_tensor, f, got, d, OP.add)
-                op("v", [("if0", j)], [("ix", j)], 0, V.tensor_copy, x, f)
+                return listed(v("lv"), "m%d" % s, HALVES)
+            for a, e in HALVES:
+                tt(run("if0", a, e), pick(v("lv", a, e)), OP.add, run("d%df" % (k + 1), a, e))
+                copy(run("ix", a, e), run("if0", a, e))
 
-    def lay_out(s):
-        cur = walk(s, "key0", "key1", ("ka", "kb"), "khd")
-        op("v", [cur, "k16f"], ["scf"], C * CYC, V.tensor_tensor_scan, sl("scf"), sl("k16f"), sl(cur), 0.0, OP.add, OP.min)
-        op("v", ["scf", ("cols", 1)], ["kw"], 0, V.tensor_scalar, sl("kw"), T.scf[:, 15:C:16], T.cols[:, 1:2], None, OP.add)
-        op("v", ["scf", ("cols", 2)], ["lol"], 0, V.tensor_scalar, sl("lol"), T.scf[:, 15:C:16], T.cols[:, 2:3], 2.0 ** -10, OP.add, OP.mult)
-        op("v", ["scf", ("cols", 3)], ["el"], 0, V.tensor_scalar, sl("el"), T.scf[:, 15:C:16], T.cols[:, 3:4], 2.0 ** -9, OP.add, OP.mult)
+    def later_mirror(s, lists):
+        keys = v("kb")
+        walk(lists, v("key0"), "key1", ("ka", "kb"), "kd", keys, 1.0, HALVES, "a")
+        for a, e in HALVES:
+            scan(v("scf", a, e), v("k16f", a, e), cut(keys, a, e), OP.add, OP.min)
+        got = v("scf", 15, C, 16)
+        ts("kw", got, col(1), OP.add)
+        ts("lol", got, col(2), OP.add, 2.0 ** -10, OP.mult)
+        ts("el", got, col(3), OP.add, 2.0 ** -9, OP.mult)
         ts("di", "kw", 1023, OP.bitwise_and)
-        fused(sl("drow"), ["drow"], sl(cur), [cur], "a%d" % s, OP.subtract, sl("idc", 0), ["idc"])
-        op("v", ["drow"], [("lrow", 1)], H * CYC, V.tensor_scalar, T.lrow[:, 1:C + 1], sl("drow"), 0.0, None, OP.max)
-        for k, (d0, d1) in enumerate(((T.lrow[:, 0:C + 1], T.lrow[:, 0:C + 1]), (T.lrow[:, 1:C + 1], T.lrow[:, 0:C]))):
-            op("v", ["lrow"], [("sums", k)], H * CYC, V.tensor_tensor_scan, T.sums[:, k:2 * C + 1:2], d0, d1, -float(H), OP.add, OP.add)
-        gath("a", "le", "sums", "el", wcols=(0, 2 * C + 1))
-        gath("a", "le", "drow", "lol", o0=C)
+        tt("drow", along(keys, v(lists[1])), OP.subtract, row("idc"))
+        op("v", [v("lrow", 1, C + 1)], [v("drow")], {"v": scalars(v("lrow", 1, C + 1), v("drow"), 0.0, OP.max), "a": act(v("lrow", 1, C + 1), v("drow"), AF.Relu)})
+        scan(v("sums", 0, 2 * C + 1, 2), v("lrow", 0, C + 1), v("lrow", 0, C + 1), OP.add, OP.add, -float(H))
+        scan(v("sums", 1, 2 * C + 1, 2), v("lrow", 1, C + 1), v("lrow", 0, C), OP.add, OP.add, -float(H))
+        gather(row("le"), v("sums", 0, 2 * C + 1), "el")
+        gather(row("le", 1), "drow", "lol")
         ts("v0", "di", float(SIDE), OP.is_ge, float(C), OP.mult)
-        small("v1", "v0", OP.add, "cw")
-        vcopy("vl", "v1")
-        gath("a", "vrow", "ip", "vl")
+        tt("v1", "v0", OP.add, "cw")
+        copy("vl", "v1")
+        gather("vrow", "ip", "vl")
         ts("sg", "di", -1.0, OP.mult, float(SIDE), OP.add)
-        small("a0", "di", OP.min, "sg")
-        cl, lens = pick(sl("le", 1), halves("le", C))
-        op("v", [cl, ("cols", 6)], ["lw"], 0, V.tensor_scalar, sl("lw"), lens, T.cols[:, 6:7], None, OP.add)
-        ce, ends = pick(sl("le", 0), halves("le"))
-        op("v", [ce, "a0"], ["sp"], 0, V.tensor_tensor, sl("sp"), ends, sl("a0"), OP.add)
-        ts("spl", "sp", ("cols", 0), OP.add)
-        op("v", ["vrow", "spl"], halves("order"), 0.05 + C * SCATTER, V.tensor_copy, sl("order", 0).indirect(sl("spl")), sl("vrow"))
-        listed("order", 0, "opl")
-        gath("a", "order", "prow", "opl", o0=C)
-        small("w1", "v0", OP.max, "lw")
-        small("pos2", "sp", OP.add, "w1")
-        small("pos1", "pos2", OP.subtract, "lw")
-        op("v", ["pos1", "pos2", ("cols", 0)], ["p1l", "p2l"], 0, V.tensor_scalar, run("p2l", 0, 2 * C), run("pos2", 0, 2 * C), T.cols[:, 0:1], None, OP.add)
-        return cl, lens
-
-    def mirror(mw, cl, lens):
-        op("a", ["ssb", "pw", ("cols", 7)], ["markp"], 0.065 + C * GATHER, A.activation, sl("markp"), sl("ssb").indirect(sl("pw")), AF.Sign, bias=T.cols[:, 7:8])
-        op("v", ["ssb", "opl"], halves("mk"), 0.05 + C * GATHER, V.tensor_scalar, sl("mk", 0), sl("ssb").indirect(sl("opl")), 0.0, 256.0, OP.is_ge, OP.mult)
-        gath("a", "mk", "markp", "opl", o0=C, scale=128.0, bias=128.0)
-        op("v", ["mk", "unit"], ["sf"], C * CYC, V.tensor_tensor_scan, sl("sf"), sl("unit"), sl("mk"), 256.0, OP.add, OP.min)
-        op("v", ["mk", "unit"], ["sr"], C * CYC, V.tensor_tensor_scan, T.sr[:, ::-1], sl("unit"), T.mk[:, ::-1], 256.0, OP.add, OP.min)
-        gath("a", "fr", "sf", "p2l")
-        gath("v", "fr", "sr", "p1l", o0=C)
-        cv, _ = pick(sl("fr"), ["fr"], 2 * C)
-        for k, n in enumerate(("clf", "clr")):
-            o = 2 * C * cv[1] + C * k
-            op("v", [cv, cl], [n], 0, V.tensor_tensor, sl(n), T.sc[:, o + 15:o + C:16], lens, OP.min)
-        small("e0", "clr", OP.subtract, "clf")
-        small("g0", "clr", OP.is_lt, "clf")
-        small("y0", "e0", OP.add, "pos1")
-        small("gl", "g0", OP.mult, "lw")
-        small("tg", "y0", OP.add, "gl")
-        ts("tl", "tg", ("cols", 0), OP.add)
-        how = "av" if mw == "m3" else "v"
-        gath(how, "mrow", "order", "tl")
-        listed("mrow", 0, mw, len(how))
+        tt("a0", "di", OP.min, "sg")
+        lens, lw, pos1 = pick(row("le", 1)), v("m1f", 0, 72, 3), v("m1f", 2, 72, 3)
+        ts(lw, lens, col(6), OP.add)
+        tt("sp", pick(row("le")), OP.add, "a0")
+        ts("spl", "sp", col(0), OP.add)
+        copy(along(row("order"), v("spl")), "vrow")
+        listed(row("order"), "opl")
+        gather(row("order", 1), "prow", "opl")
+        tt("w1", "v0", OP.max, lw)
+        tt("pos2", "sp", OP.add, "w1")
+        tt(pos1, "pos2", OP.subtract, lw)
+        ts("p2l", "pos2", col(0), OP.add)
+        ts("p1l", pos1, col(0), OP.add)
+        for k, (a, e) in enumerate(SENT):
+            mm(bank("pb", k, e - a), "up", "ups", 0, "tq%d" % (s - 1), a, e)
+            move("a", v("ssb", a, e), bank("pb", k, e - a))
+        if s == 2:
+            gather("ssp", "ssb", "pw")
+            gather(row("laid"), "ssb", "opl")
+            gather(row("laid", 1), "ssp", "opl")
+        through = v("ssp") if s == 2 else along(v("ssb"), v("pw"))
+        op("a", [v("markp")], [through, col(7)], {"a": act(v("markp"), through, AF.Sign, bias=col(7))})
+        ts(row("mk"), along(v("ssb"), v("opl")), 0.0, OP.is_ge, 256.0, OP.mult)
+        gather(row("mk", 1), "markp", "opl", scale=128.0, bias=128.0)
+        for a in (0, C):
+            scan(v("sf", a, a + C), row("unit"), v("mk", a, a + C), OP.add, OP.min, 256.0)
+            scan(v("sr", a, a + C, -1), row("unit"), v("mk", a, a + C, -1), OP.add, OP.min, 256.0)
+        gather(row("fr"), "sf", "p2l")
+        gather(row("fr", 1), "sr", "p1l", how="v")
+        back, ahead = pick(row("fr")), pick(row("fr", 1))
+        tt(v("m1f", 1, 72, 3), ahead, OP.subtract, back)
+        tt(v("m0", 1, 72, 3), ahead, OP.is_lt, back)
+        tt(v("m0", 2, 72, 3), ahead, OP.is_lt, lens)
+        scan(v("mo"), v("m0"), v("m1f"), OP.mult, OP.add)
+        ts("tl", v("mo", 2, 72, 3), col(0), OP.add)
+        gather("mrow", "order", "tl", HALVES)
+        listed(v("mrow"), "m%d" % s, HALVES)
 
     def conjugate(s):
-        a, mw = "a%d" % s, "m%d" % s
-        gath("a", "hh", "prow", a, wreg=["prow"] + ["opl"] * (s > 1))
-        gath("a", "hh", "hh", "pmpw", o0=C, wreg=halves("hh"), wcols=(0, C))
-        cv, both = pick(sl("hh"), ["hh"], 2 * C)
-        op("v", [cv, ("cols", 8)], ["f2", "f4"], 0, V.tensor_scalar, run("f2", 0, 2 * C), both, 2.0, T.cols[:, 8:9], OP.mult, OP.add)
-        small("hd_", "f4", OP.subtract, "f2")
-        ts("h2", "hd_", ("cols", 6), OP.mult)
-        small("hk", "f2", OP.add, "h2")
-        how = "v" if s == 3 else "av"
-        if s == 2:
-            gath("a", "ssp", "ssb", "pw")
-            gath("a", "laid", "ssb", "opl")
-            gath("a", "laid", "ssp", "opl", o0=C)
-            gath("a", "smr", "laid", "tl")
-        else:
-            gath(how, "smr", "ssb", mw)
-        gath(how, "shp", "smr", "hpw")
-        n = C // len(how)
-        for k in range(len(how)):
-            f3, f1, hd, hk, u, lo = [run(x, n * k, n * k + n) for x in ("f3", "f1", "hd_", "hk", "uw", "lpw")]
-            flags, pairs = T.fq[:, 2 * n * k:2 * n * k + 2 * n:2], slice(2 * n * k, 2 * n * k + 2 * n)
-            part = {x: x if n == C else (x, k) for x in ("f3", "f1", "uw", "tau")}
-            freg = halves("fq") if n == C else [halves("fq")[k]]
-            op("v", ["smr", "lpw"] + (halves("shp") if n == C else [halves("shp")[k]]), freg, 0.05 + n * GATHER, V.tensor_tensor, flags, sl("smr").indirect(lo), T.shp[:, n * k:n * k + n], OP.is_gt)
-            cv, got = pick(flags, freg, n)
-            op("v", ["dl", ("fq", 1)] + freg, [part["tau"]], n * CYC, V.tensor_tensor_scan, T.tau[:, pairs], T.dl[:, pairs], T.fq[:, pairs], 0.0, OP.mult, OP.add)
-            op("v", [cv, "hd_"], [part["f3"]], 0, V.tensor_tensor, f3, got, hd, OP.mult)
-            op("v", [part["f3"], "hk"], [part["f1"]], 0, V.tensor_tensor, f1, f3, hk, OP.add)
-            op("v", [part["f1"]], [part["uw"]], 0, V.tensor_copy, u, f1)
-        gath("a" if s == 3 else "av", "pw2", "tau", "uw", o0=ROW[1])
+        gather(row("hh"), "prow", "a%d" % s)
+        gather(row("hh", 1), row("hh"), "pmpw")
+        stay, swap = pick(row("hh")), pick(row("hh", 1))
+        ts(v("pf", 77, 3 * C + 32, 48), stay, 2.0, OP.mult, col(8), OP.add)
+        tt(v("c0", 2, 72, 3), swap, OP.subtract, stay)
+        runs = HALVES if s < 3 else WHOLE
+        gather("smr", *(("laid", "tl") if s == 2 else ("ssb", "m%d" % s)), runs)
+        gather("shp", "smr", "hpw", runs)
+        for a, e in runs:
+            flags = v("fq", 2 * a, 2 * e, 2)
+            tt(flags, along(v("smr"), run("lpw", a, e)), OP.is_gt, v("shp", a, e))
+            scan(v("pf", 3 * a, 3 * e, 3), v("k16", 0, e - a), flags, OP.add, OP.min)
+            scan(v("tau", 2 * a, 2 * e), v("dl", 2 * a, 2 * e), v("fq", 2 * a, 2 * e), OP.mult, OP.add)
+            b, f = 3 * a // 16, 3 * e // 16
+            scan(v("co", b, f), v("c0", b, f), v("pf", 45 + 16 * b, 30 + 16 * f, 16), OP.mult, OP.add)
+            copy(run("uw", a, e), v("co", b + 2, f, 3))
+        gather(power(1), "tau", "uw", runs)
 
-    def z_piece(out, part, rm, b, a, e):
-        op("v", [("fp", b), rm] + halves("fa", C * b), [(out, part)], 0.05 + (e - a) * GATHER, V.tensor_tensor, T[out][:, 4 * a + b:4 * e:4],
-           sl("fp", b).indirect(run(rm, a, e)), T.fa[:, C * b + a:C * b + e], OP.add)
+    def state(s):
+        runs, shared = (LAST, SHARED) if s == 3 else (WHOLE, range(4))
+        for k, (a, e) in enumerate(runs):
+            for b in range(4):
+                tt(v("z", 4 * a + b, 4 * e, 4), along(row("fp", b), run("rm%d" % s, a, e)), OP.add, row("fa", b, a, e))
+            quant("zq%d" % s, "z", a, e)
+            for b in range(4):
+                at = bank("pa" if k % 2 and b not in shared else "pb", b, e - a)
+                mm(at, "wq", "ws_", b, "zq%d" % s, a, e)
+                move("v" if k else "a", row("rsb", b, a, e), at, scale=0.03125)
+        for a, e in runs:
+            for b in range(4):
+                src = along(row("rsb", b), run("m%d" % s, a, e))
+                if b in shared:
+                    move("a", row("mg", b, a, e), src)
+                    for i, j in ((a, e),) if s == 3 else SENT:
+                        tt(v("xn", 4 * i + b, 4 * j, 4), v("pa", 512 * b + i, 512 * b + j), OP.add, row("mg", b, i, j))
+                else:
+                    tt(v("xn", 4 * a + b, 4 * e, 4), src, OP.add, row("fo", b, a, e))
+            for i, j in ((a, e),) if s == 3 else SENT:
+                quant("tq%d" % s, "xn", i, j)
 
     steps = T.tables["STEP"] if "STEP" in T.tables else [1, 2, 3]
+    for a, e in RUNS:
+        quant("tq0", "x0", a, e)
     for s in (1, 2, 3):
         dst = T.cores[rank ^ steps[s - 1]]
-        ne = len(topo.engines(core, dst))
-        tq, tsn, lq, lp = "tq%d" % (s - 1), "ts%d" % (s - 1), "lq%d" % s, "lp%d" % s
-        mw, rm, ra, zq, zs = "m%d" % s, "rm%d" % s, "ra%d" % s, "zq%d" % s, "zs%d" % s
-        powers(s)
-        arrive("aa%d" % s, ne, [ra], [send(dst, "aa%d" % s, sl(ra), sl("a%d" % s), ["a%d" % s], s == 1)], FLIGHT + LIST)
-        quant(tq, tsn, "x0" if s == 1 else "xn")
-        mm(("pb", 0), "up", "ups", 0, tq, tsn)
-        both = [send(dst, "at%d" % s, T[lq][:, :].bitcast(dt.uint8), T[tq][:, :].bitcast(dt.uint8), [tq]), send(dst, "at%d" % s, sl(lp), sl(tsn), [tsn])]
-        arrive("at%d" % s, 2 * ne, [lq, lp], both, FLIGHT + TILE + (COLD if s == 1 else 0.0))
+        tq, tp, lq, lp = "tq%d" % (s - 1), "ts%d" % (s - 1), "lq%d" % s, "ls%d" % s
+        lists = powers(s)
         if s == 1:
-            behind(both)
-            first_mirror()
-        copy_a(sl("ssb"), [], ["ssb", ("pb", 0)], bank(("pb", 0)))
-        if s > 1:
-            mirror(mw, *lay_out(s))
+            send(dst, "aa1", v("rpq"), v("pq"))
+            copy(run("rp", 0, 2 * C), "rpq")
+            gather("drow", "iot", "rq")
+            gather("vrow", "drow", "rp")
+            listed(v("vrow"), "ra1")
+        else:
+            send(dst, "aa%d" % s, v("ra%d" % s), v("a%d" % s))
+        for k, (a, e) in enumerate(SENT):
+            send(dst, "at%d%d" % (k, s), v(lq, a, e), v(tq, a, e))
+            if k == 0:
+                send(dst, "ap%d" % s, v(lp), v(tp))
+        if s == 1:
+            behind_first_writes()
+        (first_mirror if s == 1 else later_mirror)(s, lists)
         for b in range(4):
-            mm(("pa", b), "eq", "es", 128 * b, tq, tsn)
+            mm(bank("pa", b), "eq", "es", b, tq)
             if s == 3 and b not in SHARED:
-                copy_a(sl("fo", b), [], [("fo", b), ("pa", b)], bank(("pa", b)))
-        for b in (1, 2, 3, 0):
-            mm(("pb", b), "eq", "es", 128 * b, lq, lp)
-            copy_a(sl("fp", b), [], [("fp", b), ("pb", b)], bank(("pb", b)), scale=0.5)
-            gath("a", "fa", "fp", ra, o0=C * b, wreg=[("fp", b)], wcols=(C * b, C * b + C))
-        arrive("am%d" % s, ne, [rm], [send(dst, "am%d" % s, sl(rm), sl(mw), [mw])], FLIGHT + (LIST if s < 3 else LAST))
+                move("a", row("fo", b), bank("pa", b))
+        for b in range(4):
+            for a, e in SENT:
+                mm(bank("pb", b, e - a), "eq", "es", b, lq, a, e)
+                move("a", row("fp", b, a, e), bank("pb", b, e - a), scale=0.5)
+            gather(row("fa", b), row("fp", b), "ra%d" % s, ALONG, "aa")
+        send(dst, "am%d" % s, v("rm%d" % s), v("m%d" % s))
         conjugate(s)
-        if s == 3:
-            break
-        for a in range(0, C, PIECE):
-            for b in range(4):
-                z_piece("z", (b, a), rm, b, a, a + PIECE)
-        quant(zq, zs, "z")
-        for b in range(4):
-            mm(("pb", b), "wq", "wsc", 128 * b, zq, zs)
-            copy_a(sl("rsb", b), [], [("rsb", b), ("pb", b)], bank(("pb", b)), scale=0.03125)
-            gath("a", "mg", "rsb", mw, o0=C * b, wreg=[("rsb", b)], wcols=(C * b, C * b + C))
-            op("v", halves("mg", C * b), [("xn", b), ("pa", b)], C * CYC, V.tensor_tensor, T.xn[:, b:4 * C:4], bank(("pa", b)), sl("mg", b), OP.add)
-    gath("a", "qr3", "pw2", "pw", wreg=power(1)[1], wcols=(ROW[1], ROW[1] + C), bias=float(H))
-    dma("s", "dqo", T.qo[:, :], T.qr3[0:128:16, :], ["qr3"], [], 12)
-    for k, (a, e) in enumerate(RUNS):
-        for b in (1, 2, 3, 0):
-            z_piece("ze", (b, k), "rm3", b, a, e)
-        quant("zq3", "zs3", "ze", a, e - a, k, [("ze", (b, k)) for b in range(4)])
-        for b in range(4):
-            at, out = ("pa" if k and b not in SHARED else "pb", b), T.rl3[:, C * b + a:C * b + e]
-            mm(at, "wq", "wsc", 128 * b, "zq3", "zs3", a, e - a, k)
-            if k:
-                op("v", [], [("rl3", (b, k)), at], (e - a) * CYC, V.tensor_scalar, out, bank(at, e - a), 0.03125, None, OP.mult)
-            else:
-                copy_a(out, [], [("rl3", (b, k)), at], bank(at, e - a), n=e - a, scale=0.03125)
-    for k, (a, e) in enumerate(RUNS):
-        for b in range(4):
-            src, both, out = sl("rl3", b).indirect(run("m3", a, e)), [("rl3", (b, 0)), ("rl3", (b, 1)), "m3"], T.xe[:, 4 * a + b:4 * e:4]
-            if b in SHARED:
-                op("a", both, [("mg", (b, k))], 0.065 + (e - a) * GATHER, A.activation, T.mg[:, C * b + a:C * b + e], src, AF.Copy)
-                op("v", [("mg", (b, k))], [("xe", 4 * k + b), ("pa", b)], (e - a) * CYC, V.tensor_tensor, out, T.pa[:, 512 * b + a:512 * b + e], T.mg[:, C * b + a:C * b + e], OP.add)
-            else:
-                op("v", both + [("fo", b)], [("xe", 4 * k + b)], 0.05 + (e - a) * GATHER, V.tensor_tensor, out, src, T.fo[:, C * b + a:C * b + e], OP.add)
-        quant("tq3", "ts3", "xe", a, e - a, k, [("xe", 4 * k + b) for b in range(4)])
-        mm(("pb", k), "vq", "vs", 0, "tq3", "ts3", a, e - a, k)
-        copy_a(T.ysb[:, a:e], [], [("ysb", k), ("pb", k)], bank(("pb", k), e - a), n=e - a)
-        dma("a" if k else "s", "dy%d" % k, T.y[:, a:e], T.ysb[:, a:e], [("ysb", k)], [], (e - a) / 2)
-        dma("s", "doc%d" % k, T.oc[:, 4 * a:4 * e], T.tq3[:, a:e].bitcast(dt.uint8), [("tq3", k)], [], (e - a) / 2)
+        state(s)
+    gather("qr3", power(1), "pw", bias=float(H))
+    dma("s", "dqo", T.qo[:, :], T.qr3[0:128:16, :], [v("qr3")], [], 12)
+    for k, (a, e) in enumerate(LAST):
+        mm(bank("pb", k, e - a), "vq", "vs", 0, "tq3", a, e)
+        move("a", v("ysb", a, e), bank("pb", k, e - a))
+        dma("a" if e == C else "s", "dy%d" % k, T.y[:, a:e], T.ysb[:, a:e], [v("ysb", a, e)], [], (e - a) / 2)
+        dma("s", "doc%d" % k, T.oc[:, 4 * a:4 * e], T.tq3[:, a:e].bitcast(dt.uint8), [v("tq3", a, e)], [], (e - a) / 2)
     for k in range(4):
-        dma("as"[k % 2], "dos%d" % k, T.osc[4 * k:4 * k + 4, 0:C], T.ts3[32 * k:32 * k + 4, 0:C], ["ts3"], [], 2)
+        dma("as"[k % 2], "dos%d" % k, T.osc[4 * k:4 * k + 4, 0:C], T.ts3[32 * k:32 * k + 4, 0:C], [v("ts3")], [], 2)
 
-    def gap(d, c, k=0):
-        return d["lates"][k] + (0.0 if c["q"] in "nd" else SAME[k] if d["q"] == c["q"] else CROSS[k])
-
+    n, deps = len(calls), [c["deps"] for c in calls]
+    holds, lates = [c["holds"] for c in calls], [c["lates"] for c in calls]
     users = [[] for _ in calls]
-    for i, c in enumerate(calls):
-        for d in c["deps"]:
+    for i in range(n):
+        for d in deps[i]:
             users[d].append(i)
-    for i in reversed(range(len(calls))):
-        c = calls[i]
-        c["way"] = c["hold"] + max([gap(c, calls[u]) + calls[u]["way"] for u in users[i]] + [c["late"]])
-    for c in calls:
-        c["in"] = [(calls[d], gap(calls[d], c), calls[d]["q"] != c["q"]) for d in c["deps"]]
+
+    def gap(d, i, qd, qi, k):
+        if qd == qi and d in calls[i]["turns"]:
+            return 0.0
+        return lates[d][k] + (0.0 if qi in "nd" else SAME[k] if qd == qi else CROSS[k])
 
     def arrange(ahead, margin, give):
-        free = {q: 0.0 for q in "vatpsnd"}
-        left = [len(c["deps"]) for c in calls]
-        ready = [i for i, n in enumerate(left) if n == 0]
-        order = []
-        todo = list(range(len(calls)))
+        qs = [c["q"] for c in calls]
+        hold = [holds[i][qs[i]][0] for i in range(n)]
+        into = [[(d, gap(d, i, qs[d], qs[i], 0), qs[d] != qs[i]) for d in deps[i]] for i in range(n)]
+        way, can, end = [0.0] * n, [0.0] * n, [0.0] * n
+        for i in reversed(range(n)):
+            way[i] = hold[i] + max([gap(i, u, qs[i], qs[u], 0) + way[u] for u in users[i]] + [lates[i][0]])
+        free = dict.fromkeys("vatpsnd", 0.0)
+        left = [len(d) for d in deps]
+        ready = [i for i in range(n) if left[i] == 0]
+        order, todo = [], list(range(n))
         while ready:
-            for i in todo:
-                c = calls[i]
-                c["can"] = max([free[c["q"]]] + [d["end"] + t for d, t, _ in c["in"]])
-                c["end"] = c["can"] + c["hold"]
-            bound = max(calls[i]["can"] + calls[i]["way"] for i in todo)
-            soon = calls[min(ready, key=lambda i: calls[i]["can"])]
-            q, now = soon["q"], soon["can"]
-            mine = [calls[i] for i in todo if calls[i]["q"] == q and calls[i]["can"] < now + 1.5]
+            near = todo[:300]
+            for i in near:
+                can[i] = max([free[qs[i]]] + [end[d] + t for d, t, _ in into[i]])
+                end[i] = can[i] + hold[i]
+            bound = max(can[i] + way[i] for i in near)
+            soon = min((i for i in ready if i <= near[-1]), key=lambda i: can[i])
+            q, now = qs[soon], can[soon]
+            mine = [i for i in near if qs[i] == q and can[i] < now + 1.5]
 
             def fits(c):
-                sure = max([0.0] + [d["end"] + t + margin for d, t, other in c["in"] if other])
-                if sure > now and any(u["way"] > c["way"] and u["can"] < sure + c["hold"] for u in mine):
+                sure = max([0.0] + [end[d] + t + margin for d, t, other in into[c] if other])
+                if sure > now and any(way[u] > way[c] and can[u] < sure + hold[c] for u in mine):
                     return False
-                held = [u for u in mine if u["way"] > c["way"] and u["can"] < c["end"]]
-                return all(c["end"] + u["way"] - bound <= (FIRST if now < EARLY else give).get(q, 1.0) * (u["can"] - c["can"]) for u in held)
+                return all(end[c] + way[u] - bound <= give.get(q, 1.0) * (can[u] - can[c]) for u in mine if way[u] > way[c] and can[u] < end[c])
 
-            good = [i for i in ready if calls[i]["q"] == q and calls[i]["can"] <= now + ahead and fits(calls[i])]
+            good = [i for i in ready if i <= near[-1] and qs[i] == q and can[i] <= now + ahead and fits(i)]
             if todo[0] < loads:
-                good, q = todo[:1], calls[todo[0]]["q"]
+                good, q = todo[:1], qs[todo[0]]
             if not good:
                 free[q] = now + ahead
                 continue
-            i = max(good, key=lambda i: calls[i]["way"])
-            free[q] = calls[i]["end"]
+            i = max(good, key=lambda i: way[i])
+            free[q] = end[i]
             order.append(i)
             ready.remove(i)
             todo.remove(i)
@@ -588,100 +626,144 @@ def rank_program(g, core, T, topo):
                 left[u] -= 1
                 if left[u] == 0:
                     ready.append(u)
-        return order
+        return max(end), order, qs
 
-    def polish(cur, rounds):
-        n, qs, deps, weigh = len(calls), [c["q"] for c in calls], [c["deps"] for c in calls], (1.5, 1.0)
-        sets = [([c["holds"][k] for c in calls], [c["lates"][k] for c in calls], [[(d, gap(calls[d], c, k)) for d in c["deps"]] for c in calls],
-                 [[(u, gap(calls[i], calls[u], k)) for u in users[i]] for i in range(n)]) for k in (1, 2)]
+    def anneal(order, qs):
+        rng, ks = np.random.default_rng(1), range(len(WEIGH))
+        hold, into = [[0.0] * n for k in ks], [[None] * n for k in ks]
 
-        def sweep(seq, hold, edges, floor, known, free):
+        def tie(x):
+            for k in ks:
+                hold[k][x] = holds[x][qs[x]][k]
+                for i in [x] + users[x]:
+                    into[k][i] = [(d, gap(d, i, qs[d], qs[i], k)) for d in deps[i]]
+
+        def heads(seq, k, end, free):
+            h, fin = hold[k], into[k]
             for i in seq:
-                t = max(free.get(qs[i], 0.0), floor[i])
-                for d, w in edges[i]:
-                    if known[d] + w > t:
-                        t = known[d] + w
-                known[i] = t = t + hold[i]
-                if qs[i] != "n":
-                    free[qs[i]] = t
-            return known
+                q = qs[i]
+                t = free[q]
+                for d, w in fin[i]:
+                    w += end[d]
+                    if w > t:
+                        t = w
+                end[i] = free[q] = t + h[i]
+                free["n"] = 0.0
+            return end
 
-        def moved(seg, up):
-            one, other = (seg[-1], seg[0]) if up else (seg[0], seg[-1])
-            along, seen = {one}, set()
-            for x in (seg[::-1] if up else seg):
-                if x in along or qs[x] in seen:
-                    along.add(x)
-                    along.update(deps[x] if up else users[x])
-                    if qs[x] not in (qs[one], "n"):
-                        seen.add(qs[x])
-            return None if other in along else sorted(seg, key=lambda x: (x in along) != up)
+        for i in range(n):
+            tie(i)
+        for rnd in range(PASSES):
+            heat = HEAT * (1 - rnd / PASSES) + 0.005
+            a, b = loads, loads + WIDTH // 2 + int(rng.integers(WIDTH // 2))
+            while a < n - WIDTH // 2:
+                seg, inside = order[a:b], set(order[a:b])
+                ends, frees, exits, nexts = [], [], [], []
+                for k in ks:
+                    frees.append(dict.fromkeys("vatpsdn", 0.0))
+                    ends.append(heads(order[:a], k, [0.0] * n, frees[k]))
+                    tail, back = [0.0] * n, dict.fromkeys("vatpsdn", 0.0)
+                    for i in reversed(order[b:]):
+                        tail[i] = back[qs[i]] = max([back[qs[i]], lates[i][k]] + [tail[u] + gap(i, u, qs[i], qs[u], k) for u in users[i]]) + hold[k][i]
+                        back["n"] = 0.0
+                    exits.append([(i, {q: max([lates[i][k]] + [tail[u] + gap(i, u, q, qs[u], k) for u in users[i] if u not in inside]) for q in holds[i]})
+                                  for i in seg if not users[i] or any(u not in inside for u in users[i])])
+                    nexts.append(back)
 
-        zero, barred, seed, best = [0.0] * n, {}, 1, None
-        for step in range(rounds + 1):
-            ends = [sweep(cur, h, fin, zero, [0.0] * n, {}) for h, _, fin, _ in sets]
-            tails = [sweep(cur[::-1], h, out, late, [0.0] * n, {}) for h, late, _, out in sets]
-            score = sum(w * max(t) for w, t in zip(weigh, tails))
-            if best is None or score < best[0]:
-                best = (score, cur)
-            hold, en, tl = sets[step % 2][0], ends[step % 2], tails[step % 2]
-            place, span = {i: j for j, i in enumerate(cur)}, max(tl)
-            line = {q: [i for i in cur if qs[i] == q] for q in "vatpsd"}
-            moves = []
-            for s in line.values():
-                for j in range(1, len(s)):
-                    u, v = s[j - 1], s[j]
-                    if en[v] - hold[v] + tl[v] > span - 1e-6 and en[v] - hold[v] - en[u] < 1e-9:
-                        moves += [(s[j - r], v, True) for r in range(1, min(REACH, j) + 1)] + [(u, s[j + r], False) for r in range(1, min(REACH, len(s) - j))]
-            rated = []
-            for u, v, up in moves:
-                seed = (seed * 1103515245 + 12345) % 2 ** 31
-                seg = moved(cur[place[u]:place[v] + 1], up) if u >= loads and seed % len(moves) < 60 and barred.get((u, v), -1) <= step else None
-                if seg is None:
-                    continue
-                guess, edge = 0.0, {}
-                for q, s in line.items():
-                    mine = [x for x in seg if qs[x] == q]
-                    if mine:
-                        edge[q] = (s.index(min(mine, key=place.get)) - 1, s.index(max(mine, key=place.get)) + 1)
-                for j, (h, late, fin, out) in enumerate(sets):
-                    e2 = sweep(seg, h, fin, zero, list(ends[j]), {q: ends[j][line[q][a]] for q, (a, _) in edge.items() if a >= 0})
-                    t2 = sweep(seg[::-1], h, out, late, list(tails[j]), {q: tails[j][line[q][b]] for q, (_, b) in edge.items() if b < len(line[q])})
-                    guess += weigh[j] * max(e2[x] - h[x] + t2[x] for x in seg)
-                rated.append((guess, seed, seg, u, v))
-            if not rated:
-                barred = {}
-                continue
-            _, _, seg, u, v = min(rated)
-            cur = cur[:place[u]] + seg + cur[place[v] + 1:]
-            barred[(v, u)] = step + 5 + seed % 11
-        return best
+                def rate(seq, j, most):
+                    total, last = [], {qs[i]: i for i in seq[:j] if qs[i] != "n"}
+                    for k in ks:
+                        if sum(total) > most[k]:
+                            return None
+                        free, end = dict(frees[k]), ends[k]
+                        for q, i in last.items():
+                            free[q] = end[i]
+                        heads(seq[j:], k, end, free)
+                        xs = [end[i] + e[qs[i]] for i, e in exits[k]] + [free[q] + nexts[k][q] for q in "vatpsd"]
+                        top = max(xs)
+                        total.append(WEIGH[k] * (top + SOFT * math.log(sum([math.exp((x - top) / SOFT) for x in xs if x > top - 4 * SOFT]))))
+                    return total
+
+                parts = rate(seg, 0, [1e9 for k in ks])
+                best = (sum(parts), seg, [qs[i] for i in seg])
+                for r0, r1, r2, r3, r4 in rng.random((TRIES, 5)).tolist():
+                    j = int(r0 * len(seg))
+                    x = seg[j]
+                    q, up = qs[x], r4 < 0.5
+                    if len(holds[x]) > 1 and r1 < 0.25:
+                        qs[x] = "a" if q == "v" else "v"
+                        tie(x)
+                        new, i = seg, j
+                    elif r1 > 1 - DRAG:
+                        i = max(0, j - 2 - int(r2 * 30)) if up else min(len(seg) - 1, j + 2 + int(r2 * 30))
+                        part, bound = seg[i:j + 1][::-1] if up else seg[j:i + 1], {x}
+                        for y in part:
+                            if y in bound:
+                                bound.update(deps[y] if up else users[y])
+                        part = [y for y in part if y not in bound] + [y for y in part if y in bound]
+                        new = seg[:i] + part[::-1] + seg[j + 1:] if up else seg[:j] + part + seg[i + 1:]
+                    else:
+                        step, stop, spots = -1 if up else 1, deps[x] if up else users[x], []
+                        i = j + step
+                        while 0 <= i < len(seg) and seg[i] not in stop:
+                            if qs[seg[i]] == q:
+                                spots.append(i)
+                            i += step
+                        if not spots or q == "n":
+                            continue
+                        i = spots[int(r2 * r2 * len(spots))]
+                        new = seg[:j] + seg[j + 1:]
+                        new.insert(i, x)
+                    j = min(i, j)
+                    keep = [[end[i] for i in new[j:]] for end in ends]
+                    more = -heat * math.log(r3 + 1e-12)
+                    score = rate(new, j, [sum(parts[:k]) + more + 0.15 for k in ks])
+                    if score and sum(score) < sum(parts) + more:
+                        parts, seg = score, sorted(new, key=lambda i: ends[0][i] - hold[0][i])
+                        if sum(parts) < best[0]:
+                            best = (sum(parts), seg, [qs[i] for i in seg])
+                        continue
+                    for end, was in zip(ends, keep):
+                        for i, e in zip(new[j:], was):
+                            end[i] = e
+                    if qs[x] != q:
+                        qs[x] = q
+                        tie(x)
+                order[a:b] = best[1]
+                for i, q in zip(best[1], best[2]):
+                    if qs[i] != q:
+                        qs[i] = q
+                        tie(i)
+                a, b = b - WIDTH // 2, b + WIDTH // 2
+            end = heads(order, 0, [0.0] * n, dict.fromkeys("vatpsdn", 0.0))
+            order[loads:] = sorted(order[loads:], key=lambda i: end[i] - hold[0][i])
+        return order, qs
 
     if not ORDER:
-        ORDER.extend(polish(min(polish(arrange(*rule), ROUNDS[0]) for rule in RULES)[1], ROUNDS[1])[1])
+        ORDER.extend(anneal(*min(arrange(*rule) for rule in RULES)[1:]))
 
     know = {q: {} for q in queue}
-    for k, i in enumerate(ORDER):
-        c = calls[i]
+    order, qs = ORDER
+    for k, i in enumerate(order):
+        c, q = calls[i], qs[i]
         c["end"] = k
-        q = c["q"]
         if q in "nd":
-            c["tok"], c["then"] = c["emit"](), {}
+            c["tok"], c["then"] = c["emit"](q), {}
             continue
         need = {}
-        for d in c["deps"]:
+        for d in deps[i]:
             tok = calls[d]["tok"]
-            if tok and need.get(tok[0], (0,))[0] < tok[1]:
+            if tok and not (qs[d] == q and d in c["turns"]) and need.get(tok[0], (0,))[0] < tok[1]:
                 need[tok[0]] = (tok[1], d)
         for sem in sorted(need, key=lambda k: -calls[need[k][1]]["end"]):
-            n, d = need[sem]
-            if know[q].get(sem, 0) < n:
-                queue[q].wait_ge(T.sem[sem], n)
-                know[q][sem] = n
-                for k, v in calls[d]["then"].items():
-                    know[q][k] = max(know[q].get(k, 0), v)
+            m, d = need[sem]
+            if know[q].get(sem, 0) < m:
+                queue[q].wait_ge(T.sem[sem], m)
+                know[q][sem] = m
+                for x, y in calls[d]["then"].items():
+                    know[q][x] = max(know[q].get(x, 0), y)
         c["then"] = dict(know[q])
-        c["tok"] = c["emit"]()
+        c["tok"] = c["emit"](q)
     for sem in sorted(count):
         if know["p"].get(sem, 0) < count[sem]:
             g.wait_ge(T.sem[sem], count[sem])

import math
import numpy as np
from concourse.mybir import dt, AluOpType as OP, ActivationFunctionType as AF

C = 384
H = C // 2
U = 2.0 ** -7
STEPS = (1, 2, 4, 8, 16, 32, 64, 64)
SIDE = 703
WHOLE, HALVES, RUNS, THIRDS = ((0, C),), ((0, H), (H, C)), ((0, 256), (256, C)), ((0, 128), (128, 256), (256, C))
SENT, ALONG, LAST = RUNS, WHOLE, THIRDS
SHARED = (2, 3)
SCRATCH = {}
AT = {}


def _sb(names, width, dtype, where="sbuf"):
    for n in names.split():
        SCRATCH[n] = (where, [128, width], dtype)


def _wrapped(buf, names, dtype):
    names = names.split()
    for i, n in enumerate(names):
        AT[n] = (buf, 24 * i)
    _sb(buf, 24 * len(names), dtype)


TABLES = ((0, 512, tuple(range(8))), (3968, C, tuple(range(0, 64, 8))), (7040, C, (0, 64, 128, "p", "p64", "p128")))
ROW = {n: a + w * i for a, w, ns in TABLES for i, n in enumerate(ns) if n}
MORE = ((3, 1, 2), (5, 1, 4), (6, 2, 4), (7, 3, 4), (24, 8, 16), (40, 8, 32), (48, 16, 32), (56, 24, 32), (128, 64, 64), ("p64", "p", 64), ("p128", "p64", 64))
SLOTS = 16
_sb("pw2", 9344, "bfloat16")
_sb("iot prow qrow murow pmr hf hm h0 h1 hd hd2 th1 tg1 drow mrow vrow markp k16f", C, "bfloat16")
_sb("hs gs th2 tg2", C + 32, "bfloat16")
_sb("lrow", C + 16, "bfloat16")
_sb("hh fq tau ip order mk sf sr unit", 2 * C, "bfloat16")
_sb("sums", 2 * C + 16, "bfloat16")
_sb("lv k16", C, "float16")
_sb("dl fr le", 2 * C, "float16")
_sb("sc", SLOTS * C, "float16")
_sb("pf", 3 * C + 32, "float16")
_sb("kseed", 32, "bfloat16")
_sb("ssb ssp smr shp ysb qr3 scf key0 key1 ka kb kd kd2", C, "float32")
_sb("idc laid", 2 * C, "float32")
_sb("rsb mg", 4 * C, "float32")
_sb("x0 xn z fo fp fa", 4 * C, "bfloat16")
_sb("ut vt", 512, "bfloat16")
_sb("et", 516, "bfloat16")
_sb("eq wq", 512, "float8_e4m3fn_x4")
_sb("es ws_", 512, "uint8")
_sb("uq vq up", 128, "float8_e4m3fn_x4")
_sb("us vs ups", 128, "uint8")
_sb("tq0 tq1 tq2 tq3 lq1 lq2 lq3 zq1 zq2 zq3", C, "float8_e4m3fn_x4")
_sb("ts0 ts1 ts2 ts3 ls1 ls2 ls3 zs1 zs2 zs3", C, "uint8")
_sb("mli c24i", 24, "int32")
_wrapped("pq", "pli qli", "int32")
_sb("rpq", 48, "int32")
_sb("pi qi q32 u8i", 8, "int32")
_sb("j16 cols", 16, "float32")
_sb("uoff", 8, "uint16")
_sb("rl", 24, "uint16")
_sb("c0 co m0 m1f mo", 72, "float32")
_sb("e0 e1 eo", 96, "float32")
_wrapped("wi", "kw di ei d0i d1i d2i", "int32")
_wrapped("wf", "cw mupf lo_ hi_ k1 k2 f3 ng nw if0 d1f d2f pmc mn gt idf sg a0 v0 v1 sp w1 pos2", "float32")
_wrapped("wl", "pw qw muw lpw hpw mupw pmpw uw ix idl lol vl spl p2l p1l el opl tl rp rq ra1 l2 l4 l8 l16 l32 l64 a1 a2 a3 m1 m2 m3", "uint16")
_wrapped("wr", "ra2 ra3 rm1 rm2 rm3", "uint16")
_sb("pa pb", 2048, "float32", "psum")
DMAS = "dpl dql dml dx0 dx1 du_ dv dwc dws doc0 doc1 doc2 dos0 dos1 dos2 dos3 dy0 dy1 dy2 dqo did0 did1 did2 did3 did4".split()
SEMAPHORES = ["sv", "sa", "st", "sp", "ls"] + ["%s%d" % (k, s) for s in (1, 2, 3) for k in ("at0", "at1", "at2", "ap", "aa", "am")] + DMAS
WIDE = {"bfloat16": 2, "float16": 2, "uint16": 2, "uint8": 1}

FIX = np.array((1.0, 1.0, 1.4))
CYC = 0.00083 * FIX
GATHER, SCATTER, PE = CYC * (1.56, 1.15, 1.85), CYC * (3.8, 2.0, 5.0), np.array((0.00125, 0.0014, 0.00166))
SAME, CROSS, WEIGH = (0.18, 0.14, 0.18), (0.24, 0.25, 0.24), (1.0, 0.4, 1.1)
LOAD, RATE, START, ISSUE, FLIGHT, LIST = 1.5, 185.0, 0.2, 0.5, np.array((1.8, 2.0, 2.0)), np.array((0.8, 1.0, 0.8))
TILE, COLD = np.array((5.0, 5.6, 5.0)), np.array((10.3, 10.0, 13.5))
RULES = [(ahead, margin, {"v": v, "a": a}) for ahead in (0.03, 0.1) for margin in (0.1, 0.2) for v, a in ((2.0, 0.1), (10.0, 0.5))]
PASSES, TRIES, WIDTH, HEAT, SOFT, DRAG = 26, 2000, 100, 0.05, 0.25, 0.2
ORDER, MASKS = [], {}


def rank_program(g, core, T, topo):
    rank = T.rank_of(core)
    if rank is None:
        return
    V, A, P, M = g.vector, g.scalar, g, g.tensor
    queue = {"v": V, "a": A, "t": M, "p": P, "s": g.sync}
    own = {"v": "sv", "a": "sa", "t": "st", "p": "sp"}
    calls = []
    writer, readers = {}, {}

    def v(n, a=0, e=None, s=1):
        if n in AT:
            return (AT[n][0], AT[n][1], AT[n][1] + 24, 1, None)
        return (n, a, SCRATCH[n][1][1] if e is None else e, s, None)

    def row(n, i=0, a=0, e=C):
        return v(n, C * i + a, C * i + e)

    def run(n, a=0, e=C):
        return (AT[n][0], AT[n][1] + a // 16, AT[n][1] + e // 16, 1, None)

    def along(win, lst):
        return win[:4] + (lst,)

    def cut(w, a, e):
        return (w[0], w[1] + a * w[3], min(w[2], w[1] + e * w[3]), w[3], None)

    def ap(w):
        if not isinstance(w, tuple):
            return w
        x = T[w[0]][:, w[1]:w[2]:w[3]] if w[3] > 0 else T[w[0]][:, w[2] - 1:w[1] - 1 if w[1] else None:-1]
        return x.indirect(ap(w[4])) if w[4] else x

    def size(w):
        return 16 * size(w[4]) if w[4] else len(range(w[1], w[2], abs(w[3])))

    def touched(ws):
        out = []
        for w in ws:
            if isinstance(w, tuple):
                n, a, e, s, lst = w
                if SCRATCH[n][0] == "psum":
                    a, e, s = a // 512 * 512, -(-e // 512) * 512, 1
                if (a, e, s) not in MASKS:
                    MASKS[a, e, s] = sum(1 << i for i in range(a, e, abs(s)))
                out += [(n, MASKS[a, e, s])] + touched([lst])
        return out

    def add(q, reads, writes, hold, late, emit, after=()):
        writes, reads = touched(writes), touched(reads)
        deps, turns, me = set(after), set(), len(calls)
        for n, m in reads + writes:
            deps.update(c for k, c in writer.get(n, []) if k & m)
        for n, m in writes:
            deps.update(c for k, c in readers.get(n, []) if k & m)
        for n, m in reads:
            if SCRATCH[n][0] == "psum":
                turns.update([c for k, c in readers.get(n, []) if k & m][-1:])
        hold = {k: [float(x) for x in h + np.zeros(3)] for k, h in hold.items()}
        calls.append({"q": q, "deps": sorted(deps | turns), "turns": turns - deps, "holds": hold, "lates": [float(x) for x in late + np.zeros(3)], "emit": emit})
        for n, m in writes:
            writer[n] = [(k & ~m, c) for k, c in writer.get(n, []) if k & ~m] + [(m, me)]
            readers[n] = [(k & ~m, c) for k, c in readers.get(n, []) if k & ~m]
        for n, m in reads:
            readers.setdefault(n, []).append((m, me))
        return me

    count = {"sv": 0, "sa": 0, "st": 0, "sp": 0}
    line = []

    def op(q, out, ins, forms):
        def emit(k):
            _, call, args, kw = forms[k]
            count[own[k]] += 1
            call(*[ap(x) for x in args], **{n: ap(x) for n, x in kw.items()}).then_inc(T.sem[own[k]], 1)
            return own[k], count[own[k]]
        behind = line[:1] if q == "p" else []
        me = add(q, ins + [w[4] for w in out], [w[:4] + (None,) for w in out], {k: np.maximum(f[0], 64 * CYC) for k, f in forms.items()}, 0.0, emit, behind)
        calls[me]["turns"].update(behind)

    def dma(q, sem, out, in_, reads, writes, kib, after=()):
        def emit(k):
            count[sem] = 16
            queue[q].dma_start(out, in_).then_inc(T.sem[sem], 16)
            return sem, 16
        first = add(q, reads, writes, {q: START}, LOAD, emit, after)
        return add("d", reads, writes, {"d": kib / RATE}, 0.0, lambda k: (sem, 16), [first])

    sent = [0]

    def send(dst, sem, out, in_):
        codes, ne = SCRATCH[in_[0]][2].startswith("float8"), len(topo.engines(core, dst))

        def emit(k):
            rid, pid, _ = topo.addr(dst)
            g.remote_dma(*[ap(w).bitcast(dt.uint8) if codes else ap(w) for w in (out, in_)], T.sem[sem], T.sem.ls, pid, rid, topo.mask(core, dst))
            sent[0] += ne

        def landed(k):
            count[sem] = ne
            return sem, ne
        call = add("p", [in_], [], {"p": ISSUE + (0.0 if line else COLD)}, FLIGHT, emit, line[:1])
        calls[call]["turns"].update(line[:1])
        line[:] = [call, add("n", [], [out], {"n": np.maximum(LIST, TILE * size(in_) * (4 if codes else 1) / (5 * C))}, 0.0, landed, [call] + line[1:])]

    def pace(out, *ins):
        if out[4] or ins and ins[0][4]:
            return 0.05 * FIX + size(out) * (SCATTER if out[4] else GATHER)
        return size(out) * CYC * (0.5 if all(WIDE.get(SCRATCH[w[0]][2]) == 2 for w in (out,) + ins) else 1.0)

    def named(x):
        return v(x) if isinstance(x, str) else x

    def tt(out, a, o, b):
        out, a, b = named(out), named(a), named(b)
        t = pace(out, a) if a[4] else size(out) * CYC * (1 if "psum" in (SCRATCH[a[0]][0], SCRATCH[b[0]][0]) else 2)
        op("v", [out], [a, b], {"v": (t, V.tensor_tensor, (out, a, b, o), {})})

    def scalars(out, a, s1, o0, s2=None, o1=None):
        return (pace(out, a), V.tensor_scalar, (out, a, s1, s2, o0) + (() if o1 is None else (o1,)), {})

    def ts(out, a, s1, o0, s2=None, o1=None):
        op("v", [named(out)], [named(a), s1, s2], {"v": scalars(named(out), named(a), s1, o0, s2, o1)})

    def copy(out, a):
        out, a = named(out), named(a)
        op("v", [out], [a], {"v": (pace(out, a), V.tensor_copy, (out, a), {})})

    def fill(out, value):
        op("v", [out], [], {"v": (pace(out), V.memset, (out, value), {})})

    def scan(out, d0, d1, o0, o1, first=0.0):
        op("v", [out], [d0, d1], {"v": (pace(out, d0, d1), V.tensor_tensor_scan, (out, d0, d1, first, o0, o1), {})})

    def act(out, a, func, **kw):
        return (0.065 * FIX + size(out) * GATHER if a[4] else 0.02 + size(out) * CYC, A.activation, (out, a, func), kw)

    def move(q, out, a, scale=None, bias=None):
        out, a = named(out), named(a)
        kw = {n: x for n, x in (("scale", scale), ("bias", bias)) if x}
        steps = [y for x, o in ((scale, OP.mult), (bias, OP.add)) if x for y in (x, o)]
        op(q, [out], [a], {"a": act(out, a, AF.Copy, **kw), "v": scalars(out, a, *steps) if kw else (pace(out, a), V.tensor_copy, (out, a), {})})

    def gather(out, win, lst, runs=WHOLE, how="va", **kw):
        for q, (a, e) in zip(how[-len(runs):], runs):
            move(q, cut(named(out), a, e), along(named(win), run(lst, a, e)), **kw)

    def col(i):
        return v("cols", i, i + 1)

    turn = [0]

    def pick(w):
        turn[0] = k = (turn[0] + 1) % SLOTS
        o, n = C * k, size(w)
        scan(v("sc", o, o + n), v("k16", 0, n), w, OP.add, OP.min)
        return v("sc", o + 15, o + n, 16)

    def listed(w, lst, runs=WHOLE):
        for a, e in runs:
            ts(run(lst, a, e), pick(cut(w, a, e)), col(0), OP.add)

    def pack(out, plane, x):
        op("v", [out, plane], [x], {"v": (0.012 * FIX + 1.06 * size(out) * CYC, V.quantize_mx, (out, plane, x), {})})

    def quant(q, x, a=0, e=C):
        pack(v(q, a, e), v(q.replace("q", "s"), a, e), v(x, 4 * a, 4 * e))

    def bank(n, b, e=C):
        return v(n, 512 * b, 512 * b + e)

    def mm(out, lq, ls, b, rq, a=0, e=C):
        sides = [v(lq, 128 * b, 128 * b + 128), v(ls, 128 * b, 128 * b + 128), v(rq, a, e), v(rq.replace("q", "s"), a, e)]
        op("t", [out], sides, {"t": ((e - a + 16) * PE, M.matmul_mx, [out] + sides + [True, True], {})})

    def power(n):
        return v("pw2", ROW[n], ROW[n] + C)

    dma("s", "dpl", ap(v("pli")), T.pl[:, :], [], [v("pli")], 12)
    dma("s", "dql", ap(v("qli")), T.ql[:, :], [], [v("qli")], 12)
    dma("a", "dml", T.mli[:, :], T.ml[:, :], [], [v("mli")], 12)
    dma("s", "du_", T.ut[:, :], T.u[:, :], [], [v("ut")], 128)
    later = [dma("s", "dx%d" % k, T.x0[:, 4 * a:4 * e], T.x[:, 4 * a:4 * e], [], [v("x0", 4 * a, 4 * e)], e - a) for k, (a, e) in enumerate(RUNS)][-1:]
    for sem, out, in_, name, kib in (("dwc", T.wq[:, :].bitcast(dt.uint8), T.wc, "wq", 256), ("dws", T.ws_[:, :], T.ws, "ws_", 64), ("dv", T.vt[:, :], T.v, "vt", 128)):
        dma("s", sem, out, in_[:, :], [], [v(name)], kib, later)

    def iota(out, pattern, base, cm=0):
        kw = {} if SCRATCH[out[0]][2] == "int32" else {"allow_small_or_imprecise_dtypes": True}
        op("p", [out], [], {"p": (0.13 * FIX + 2 * size(out) * CYC, P.iota, (out, pattern, base, cm), kw)})

    def select(out, a, pattern, o, base, cm):
        op("p", [out], [a], {"p": (0.17 * FIX + 2 * size(out) * CYC, P.affine_select, (out, a, pattern, o, 0.0, base, cm), {})})

    iota(v("pi", 0, 1), [[1, 1]], 0, 1)
    iota(v("j16"), [[1, 16]], 0)
    iota(v("c24i"), [[16, 24]], 0)
    iota(v("iot"), [[1, C]], -H)
    loads = len(calls)
    iota(v("u8i"), [[16, 8]], 0)
    fill(v("unit", 0, 516), 1.0)

    place, block = v("qi", 0, 1), v("q32", 0, 1)
    ts(place, v("pi", 0, 1), 15, OP.bitwise_and)
    ts(col(5), place, 0, OP.add)
    ts(col(4), place, 1, OP.add)
    ts(col(6), place, 15, OP.is_lt, 1024.0, OP.mult)
    ts(col(0), col(6), float(H), OP.add)
    ts(col(1), col(6), 512.0, OP.mult)
    ts(col(2), col(6), 512.0, OP.mult, -447.0, OP.add)
    ts(col(3), col(6), 512.0, OP.mult, 767.5 - SIDE, OP.add)
    fill(col(7), 2.0 ** -100)
    ts(col(8), col(0), 2.0, OP.mult, 1.0, OP.add)
    ts(col(9), place, 8, OP.is_lt, 1.0, OP.add)
    ts(col(13), place, 8, OP.is_ge, -2.0 ** 90, OP.mult)
    ts(col(10), place, 8, OP.is_ge, 1.0, OP.mult)
    ts(col(14), place, 8, OP.is_ge, 2.0 ** -100, OP.mult)
    ts(block, v("pi", 0, 1), 31, OP.bitwise_and)
    ts(col(11), block, 16, OP.is_lt, 2.0 ** 20, OP.mult)
    ts(col(12), block, 16, OP.is_ge, 512.0 / U - 2.0 ** -4, OP.mult)
    for k, (a, w, ns) in enumerate(TABLES):
        dma("s", "did%d" % k, T.pw2[:, a:a + C], T.iot[:, :], [v("iot")], [v("pw2", a, a + C)], 96)
    ts(run("k1", 0, 256), "j16", col(5), OP.is_equal, 2048.0, OP.mult)
    ts(run("k2", 0, 256), "j16", col(4), OP.is_equal, -1024.0, OP.mult)
    tt(v("kseed", 0, 16), run("k1", 0, 256), OP.add, run("k2", 0, 256))
    ts("cw", "c24i", col(5), OP.add)
    ts("rl", "c24i", 0.0, OP.mult, col(5), OP.add)
    move("v", "k16", along(v("kseed", 0, 16), v("rl")))
    for n in ("hs", "gs"):
        for a in (0, C + 16):
            move("a", v(n, a, a + 16), v("unit", 0, 16))
    for a in range(C, 7 * 512, 512):
        move("a", v("pw2", a, a + 512 - C), v("unit", 0, 512 - C))
    move("a", v("e0", 3, 96, 4), v("unit", 0, 24), scale=-1.0)
    move("a", v("e0", 0, 96, 4), v("unit", 0, 24), bias=-1.0)
    ts(v("e0", 1, 96, 8), v("e0", 0, 96, 8), col(11), OP.add)
    ts(v("e0", 2, 96, 8), v("e0", 0, 96, 8), 2.0 ** -4, OP.add, col(12), OP.add)
    ts(v("e0", 5, 96, 8), v("e0", 1, 96, 8), -1.0, OP.mult, 2.0 ** 20, OP.add)
    ts(v("e0", 6, 96, 8), v("e0", 2, 96, 8), -1.0, OP.mult, 512.0 / U + 2.0 ** -4, OP.add)
    copy(v("e1", 2, 96, 4), "cw")
    iota(v("c0"), [[0, 24], [2, 3]], 0)
    ts(v("pf", 61, 3 * C + 32, 48), v("c0", 1, 72, 3), col(6), OP.mult)

    copy("uoff", "u8i")
    quant("uq", "ut", 0, 128)
    words = [T.up[:, :].bitcast(dt.uint32), T.uq[:, :].bitcast(dt.uint32).indirect(T.uoff[:, :])]
    op("v", [v("up")], [v("uq"), v("uoff")], {"v": (0.05 * FIX + 128 * GATHER, V.tensor_copy, words, {})})
    move("a", "ups", along(v("us"), v("uoff")))
    quant("vq", "vt", 0, 128)

    copy("pw", "pli")
    copy("qw", "qli")
    copy("muw", "mli")
    gather("qrow", "iot", "qw", HALVES)
    gather(power(1), "qrow", "pw", HALVES)
    gather("prow", "iot", "pw")
    dma("s", "did3", ap(power("p")), T.prow[:, :], [v("prow")], [power("p")], 96)
    tt(v("e1", 3, 96, 4), "pli", OP.add, "cw")
    gather("murow", "iot", "muw")
    fill(v("dl", 0, 2 * C, 2), 0.0)
    tt(v("dl", 1, 2 * C, 2), along(v("murow"), v("pw")), OP.subtract, "prow")
    ts("f3", pick(v("dl", 1, 2 * C, 2)), col(6), OP.add)
    tt("mupf", "f3", OP.add, "pli")
    copy("mupw", "mupf")
    tt("lo_", "mupf", OP.min, "pli")
    tt("hi_", "mupf", OP.max, "pli")
    copy(run("lpw", 0, 2 * C), run("lo_", 0, 2 * C))
    gather("pmr", "prow", "mupw")
    listed(v("pmr"), "pmpw")
    tt("pmc", "pli", OP.subtract, "cw")
    tt("mn", "pli", OP.min, "cw")
    ts("gt", "pmc", 0.0, OP.is_lt, float(C), OP.mult)
    tt("idf", "mn", OP.add, "gt")
    copy("idl", "idf")
    move("a", "k16f", "k16", scale=512.0)
    dma("s", "did4", ap(row("ip", 1)), T.prow[:, :], [v("prow")], [row("ip", 1)], 96)

    def behind_first_writes():
        select(v("et"), v("unit", 0, 516), [[-1, 516]], OP.is_equal, 3, 4)
        for b in range(4):
            pack(v("eq", 128 * b, 128 * b + 128), v("es", 128 * b, 128 * b + 128), v("et", 3 - b, 515 - b))
        select(v("fq", 1, 2 * C, 2), v("prow"), [[0, C]], OP.is_gt, 1, 0)
        iota(v("idc"), [[SIDE, 2], [1024, C]], -1)
        gather("key0", "idc", "idl", bias=float(H))
        move("a", "key1", "key0", bias=-1.0)
        iota(row("ip"), [[1, C]], -H)
        iota(v("m0"), [[0, 72]], 0)
        iota(v("lrow", 0, 16), [[0, 16]], 0)

    def powers(s):
        lists = {n: "l%d" % n if n > 1 else "a%d" % s for n in STEPS}
        runs = WHOLE if s == 1 else HALVES
        listed(power(1), lists[1], runs)
        for n in STEPS[:6]:
            gather(power(2 * n), power(n), lists[n], runs, "aa")
            listed(power(2 * n), lists[2 * n], runs)
        for to, n, by in MORE if s == 1 else ():
            gather(power(to), power(n), lists[by])
        return lists

    def walk(lists, cur, near, pair, spare, last, unit, runs, q):
        for i, n in enumerate(STEPS):
            nxt = last if i == 7 else v(pair[i % 2])
            for a, e in runs:
                if i < 7 and (i or not near):
                    move(q, v(spare, a, e), cut(cur, a, e), bias=-n * unit)
                if i == 6:
                    move(q, v(spare + "2", a, e), cut(cur, a, e), bias=-2 * n * unit)
            for a, e in runs:
                tt(cut(nxt, a, e), along(cur, run(lists[n], a, e)), OP.min, v(spare + "2" if i == 7 else spare if i or not near else near, a, e))
            cur = nxt

    def first_mirror(s, lists):
        for k, (a, e) in enumerate(RUNS):
            one, two = bank("pb", 2 * k + 1, e - a), bank("pb", 2 * k, e - a)
            mm(one, "up", "ups", 0, "tq%d" % (s - 1), a, e)
            mm(two, "up", "ups", 0, "tq%d" % (s - 1), a, e)
            op("a", [v("hm", a, e)], [one, col(10), col(14)], {"a": act(v("hm", a, e), one, AF.Sign, scale=col(10), bias=col(14))})
            ts(v("hf", a, e), two, col(13), OP.is_ge, col(9), OP.mult)
            move("a", v("ssb", a, e), one)
        for a, e in RUNS:
            tt(v("h0", a, e), along(v("hm"), run("pw", a, e)), OP.add, v("hf", a, e))
        walk(lists, v("h0"), None, ("h1", "h0"), "hd", v("hs", 16, 16 + C), U, RUNS, "v")
        gather(v("gs", 16, 16 + C), v("hs", 16, 16 + C), "pw", HALVES)
        for n in ("h", "g"):
            for out, a in ((v("t%s1" % n), v(n + "s", 16, 16 + C)), (v("t%s2" % n), v(n + "s"))):
                op("v", [out], [a], {"v": (pace(out, a), V.transpose, (out, a), {})})
        for o, t, a in ((0, "1", 0), (1, "2", 16)):
            tt(v("e1", o, 96, 4), v("th" + t, a, a + 369, 16), OP.subtract, v("tg" + t, a + 8, a + 377, 16))
        scan(v("eo"), v("e0"), v("e1"), OP.mult, OP.add)
        tt("ei", v("eo", 2, 96, 4), OP.max, v("eo", 3, 96, 4))
        tt("ng", v("eo", 2, 96, 4), OP.is_lt, v("eo", 3, 96, 4))
        ts("d0i", "ei", 8 * 512 - 1, OP.bitwise_and)
        copy("ix", "d0i")
        for k in (1, 2):
            ts("d%di" % k, "ei", 3 * k, OP.logical_shift_right, 7 * 512, OP.bitwise_and)
        ts(run("d1f", 0, 2 * C), run("d1i", 0, 2 * C), 0.75, OP.mult, col(0), OP.add)
        ts("nw", "ng", 3.0 * C, OP.mult)
        tt("d2f", "d2f", OP.add, "nw")
        for k, (a, w, ns) in enumerate(TABLES):
            gather("lv", v("pw2", a, a + w * (len(ns) - 1) + C), "ix", HALVES)
            if k == 2:
                return listed(v("lv"), "m%d" % s, HALVES)
            for a, e in HALVES:
                tt(run("if0", a, e), pick(v("lv", a, e)), OP.add, run("d%df" % (k + 1), a, e))
                copy(run("ix", a, e), run("if0", a, e))

    def later_mirror(s, lists):
        keys = v("kb")
        walk(lists, v("key0"), "key1", ("ka", "kb"), "kd", keys, 1.0, HALVES, "a")
        for a, e in HALVES:
            scan(v("scf", a, e), v("k16f", a, e), cut(keys, a, e), OP.add, OP.min)
        got = v("scf", 15, C, 16)
        ts("kw", got, col(1), OP.add)
        ts("lol", got, col(2), OP.add, 2.0 ** -10, OP.mult)
        ts("el", got, col(3), OP.add, 2.0 ** -9, OP.mult)
        ts("di", "kw", 1023, OP.bitwise_and)
        tt("drow", along(keys, v(lists[1])), OP.subtract, row("idc"))
        op("v", [v("lrow", 1, C + 1)], [v("drow")], {"v": scalars(v("lrow", 1, C + 1), v("drow"), 0.0, OP.max), "a": act(v("lrow", 1, C + 1), v("drow"), AF.Relu)})
        scan(v("sums", 0, 2 * C + 1, 2), v("lrow", 0, C + 1), v("lrow", 0, C + 1), OP.add, OP.add, -float(H))
        scan(v("sums", 1, 2 * C + 1, 2), v("lrow", 1, C + 1), v("lrow", 0, C), OP.add, OP.add, -float(H))
        gather(row("le"), v("sums", 0, 2 * C + 1), "el")
        gather(row("le", 1), "drow", "lol")
        ts("v0", "di", float(SIDE), OP.is_ge, float(C), OP.mult)
        tt("v1", "v0", OP.add, "cw")
        copy("vl", "v1")
        gather("vrow", "ip", "vl")
        ts("sg", "di", -1.0, OP.mult, float(SIDE), OP.add)
        tt("a0", "di", OP.min, "sg")
        lens, lw, pos1 = pick(row("le", 1)), v("m1f", 0, 72, 3), v("m1f", 2, 72, 3)
        ts(lw, lens, col(6), OP.add)
        tt("sp", pick(row("le")), OP.add, "a0")
        ts("spl", "sp", col(0), OP.add)
        copy(along(row("order"), v("spl")), "vrow")
        listed(row("order"), "opl")
        gather(row("order", 1), "prow", "opl")
        tt("w1", "v0", OP.max, lw)
        tt("pos2", "sp", OP.add, "w1")
        tt(pos1, "pos2", OP.subtract, lw)
        ts("p2l", "pos2", col(0), OP.add)
        ts("p1l", pos1, col(0), OP.add)
        for k, (a, e) in enumerate(SENT):
            mm(bank("pb", k, e - a), "up", "ups", 0, "tq%d" % (s - 1), a, e)
            move("a", v("ssb", a, e), bank("pb", k, e - a))
        if s == 2:
            gather("ssp", "ssb", "pw")
            gather(row("laid"), "ssb", "opl")
            gather(row("laid", 1), "ssp", "opl")
        through = v("ssp") if s == 2 else along(v("ssb"), v("pw"))
        op("a", [v("markp")], [through, col(7)], {"a": act(v("markp"), through, AF.Sign, bias=col(7))})
        ts(row("mk"), along(v("ssb"), v("opl")), 0.0, OP.is_ge, 256.0, OP.mult)
        gather(row("mk", 1), "markp", "opl", scale=128.0, bias=128.0)
        for a in (0, C):
            scan(v("sf", a, a + C), row("unit"), v("mk", a, a + C), OP.add, OP.min, 256.0)
            scan(v("sr", a, a + C, -1), row("unit"), v("mk", a, a + C, -1), OP.add, OP.min, 256.0)
        gather(row("fr"), "sf", "p2l")
        gather(row("fr", 1), "sr", "p1l", how="v")
        back, ahead = pick(row("fr")), pick(row("fr", 1))
        tt(v("m1f", 1, 72, 3), ahead, OP.subtract, back)
        tt(v("m0", 1, 72, 3), ahead, OP.is_lt, back)
        tt(v("m0", 2, 72, 3), ahead, OP.is_lt, lens)
        scan(v("mo"), v("m0"), v("m1f"), OP.mult, OP.add)
        ts("tl", v("mo", 2, 72, 3), col(0), OP.add)
        gather("mrow", "order", "tl", HALVES)
        listed(v("mrow"), "m%d" % s, HALVES)

    def conjugate(s):
        gather(row("hh"), "prow", "a%d" % s)
        gather(row("hh", 1), row("hh"), "pmpw")
        stay, swap = pick(row("hh")), pick(row("hh", 1))
        ts(v("pf", 77, 3 * C + 32, 48), stay, 2.0, OP.mult, col(8), OP.add)
        tt(v("c0", 2, 72, 3), swap, OP.subtract, stay)
        runs = HALVES if s < 3 else WHOLE
        gather("smr", *(("laid", "tl") if s == 2 else ("ssb", "m%d" % s)), runs)
        gather("shp", "smr", "hpw", runs)
        for a, e in runs:
            flags = v("fq", 2 * a, 2 * e, 2)
            tt(flags, along(v("smr"), run("lpw", a, e)), OP.is_gt, v("shp", a, e))
            scan(v("pf", 3 * a, 3 * e, 3), v("k16", 0, e - a), flags, OP.add, OP.min)
            scan(v("tau", 2 * a, 2 * e), v("dl", 2 * a, 2 * e), v("fq", 2 * a, 2 * e), OP.mult, OP.add)
            b, f = 3 * a // 16, 3 * e // 16
            scan(v("co", b, f), v("c0", b, f), v("pf", 45 + 16 * b, 30 + 16 * f, 16), OP.mult, OP.add)
            copy(run("uw", a, e), v("co", b + 2, f, 3))
        gather(power(1), "tau", "uw", runs)

    def state(s):
        runs, shared = (LAST, SHARED) if s == 3 else (WHOLE, range(4))
        for k, (a, e) in enumerate(runs):
            for b in range(4):
                tt(v("z", 4 * a + b, 4 * e, 4), along(row("fp", b), run("rm%d" % s, a, e)), OP.add, row("fa", b, a, e))
            quant("zq%d" % s, "z", a, e)
            for b in range(4):
                at = bank("pa" if k % 2 and b not in shared else "pb", b, e - a)
                mm(at, "wq", "ws_", b, "zq%d" % s, a, e)
                move("v" if k else "a", row("rsb", b, a, e), at, scale=0.03125)
        for a, e in runs:
            for b in range(4):
                src = along(row("rsb", b), run("m%d" % s, a, e))
                if b in shared:
                    move("a", row("mg", b, a, e), src)
                    for i, j in ((a, e),) if s == 3 else SENT:
                        tt(v("xn", 4 * i + b, 4 * j, 4), v("pa", 512 * b + i, 512 * b + j), OP.add, row("mg", b, i, j))
                else:
                    tt(v("xn", 4 * a + b, 4 * e, 4), src, OP.add, row("fo", b, a, e))
            for i, j in ((a, e),) if s == 3 else SENT:
                quant("tq%d" % s, "xn", i, j)

    steps = T.tables["STEP"] if "STEP" in T.tables else [1, 2, 3]
    for a, e in RUNS:
        quant("tq0", "x0", a, e)
    for s in (1, 2, 3):
        dst = T.cores[rank ^ steps[s - 1]]
        tq, tp, lq, lp = "tq%d" % (s - 1), "ts%d" % (s - 1), "lq%d" % s, "ls%d" % s
        lists = powers(s)
        if s == 1:
            send(dst, "aa1", v("rpq"), v("pq"))
            copy(run("rp", 0, 2 * C), "rpq")
            gather("drow", "iot", "rq")
            gather("vrow", "drow", "rp")
            listed(v("vrow"), "ra1")
        else:
            send(dst, "aa%d" % s, v("ra%d" % s), v("a%d" % s))
        for k, (a, e) in enumerate(SENT):
            send(dst, "at%d%d" % (k, s), v(lq, a, e), v(tq, a, e))
            if k == 0:
                send(dst, "ap%d" % s, v(lp), v(tp))
        if s == 1:
            behind_first_writes()
        (first_mirror if s == 1 else later_mirror)(s, lists)
        for b in range(4):
            mm(bank("pa", b), "eq", "es", b, tq)
            if s == 3 and b not in SHARED:
                move("a", row("fo", b), bank("pa", b))
        for b in range(4):
            for a, e in SENT:
                mm(bank("pb", b, e - a), "eq", "es", b, lq, a, e)
                move("a", row("fp", b, a, e), bank("pb", b, e - a), scale=0.5)
            gather(row("fa", b), row("fp", b), "ra%d" % s, ALONG, "aa")
        send(dst, "am%d" % s, v("rm%d" % s), v("m%d" % s))
        conjugate(s)
        state(s)
    gather("qr3", power(1), "pw", bias=float(H))
    dma("s", "dqo", T.qo[:, :], T.qr3[0:128:16, :], [v("qr3")], [], 12)
    for k, (a, e) in enumerate(LAST):
        mm(bank("pb", k, e - a), "vq", "vs", 0, "tq3", a, e)
        move("a", v("ysb", a, e), bank("pb", k, e - a))
        dma("a" if e == C else "s", "dy%d" % k, T.y[:, a:e], T.ysb[:, a:e], [v("ysb", a, e)], [], (e - a) / 2)
        dma("s", "doc%d" % k, T.oc[:, 4 * a:4 * e], T.tq3[:, a:e].bitcast(dt.uint8), [v("tq3", a, e)], [], (e - a) / 2)
    for k in range(4):
        dma("as"[k % 2], "dos%d" % k, T.osc[4 * k:4 * k + 4, 0:C], T.ts3[32 * k:32 * k + 4, 0:C], [v("ts3")], [], 2)

    n, deps = len(calls), [c["deps"] for c in calls]
    holds, lates = [c["holds"] for c in calls], [c["lates"] for c in calls]
    users = [[] for _ in calls]
    for i in range(n):
        for d in deps[i]:
            users[d].append(i)

    def gap(d, i, qd, qi, k):
        if qd == qi and d in calls[i]["turns"]:
            return 0.0
        return lates[d][k] + (0.0 if qi in "nd" else SAME[k] if qd == qi else CROSS[k])

    def arrange(ahead, margin, give):
        qs = [c["q"] for c in calls]
        hold = [holds[i][qs[i]][0] for i in range(n)]
        into = [[(d, gap(d, i, qs[d], qs[i], 0), qs[d] != qs[i]) for d in deps[i]] for i in range(n)]
        way, can, end = [0.0] * n, [0.0] * n, [0.0] * n
        for i in reversed(range(n)):
            way[i] = hold[i] + max([gap(i, u, qs[i], qs[u], 0) + way[u] for u in users[i]] + [lates[i][0]])
        free = dict.fromkeys("vatpsnd", 0.0)
        left = [len(d) for d in deps]
        ready = [i for i in range(n) if left[i] == 0]
        order, todo = [], list(range(n))
        while ready:
            near = todo[:300]
            for i in near:
                can[i] = max([free[qs[i]]] + [end[d] + t for d, t, _ in into[i]])
                end[i] = can[i] + hold[i]
            bound = max(can[i] + way[i] for i in near)
            soon = min((i for i in ready if i <= near[-1]), key=lambda i: can[i])
            q, now = qs[soon], can[soon]
            mine = [i for i in near if qs[i] == q and can[i] < now + 1.5]

            def fits(c):
                sure = max([0.0] + [end[d] + t + margin for d, t, other in into[c] if other])
                if sure > now and any(way[u] > way[c] and can[u] < sure + hold[c] for u in mine):
                    return False
                return all(end[c] + way[u] - bound <= give.get(q, 1.0) * (can[u] - can[c]) for u in mine if way[u] > way[c] and can[u] < end[c])

            good = [i for i in ready if i <= near[-1] and qs[i] == q and can[i] <= now + ahead and fits(i)]
            if todo[0] < loads:
                good, q = todo[:1], qs[todo[0]]
            if not good:
                free[q] = now + ahead
                continue
            i = max(good, key=lambda i: way[i])
            free[q] = end[i]
            order.append(i)
            ready.remove(i)
            todo.remove(i)
            for u in users[i]:
                left[u] -= 1
                if left[u] == 0:
                    ready.append(u)
        return max(end), order, qs

    def anneal(order, qs):
        rng, ks = np.random.default_rng(1), range(len(WEIGH))
        hold, into = [[0.0] * n for k in ks], [[None] * n for k in ks]

        def tie(x):
            for k in ks:
                hold[k][x] = holds[x][qs[x]][k]
                for i in [x] + users[x]:
                    into[k][i] = [(d, gap(d, i, qs[d], qs[i], k)) for d in deps[i]]

        def heads(seq, k, end, free):
            h, fin = hold[k], into[k]
            for i in seq:
                q = qs[i]
                t = free[q]
                for d, w in fin[i]:
                    w += end[d]
                    if w > t:
                        t = w
                end[i] = free[q] = t + h[i]
                free["n"] = 0.0
            return end

        for i in range(n):
            tie(i)
        for rnd in range(PASSES):
            heat = HEAT * (1 - rnd / PASSES) + 0.005
            a, b = loads, loads + WIDTH // 2 + int(rng.integers(WIDTH // 2))
            while a < n - WIDTH // 2:
                seg, inside = order[a:b], set(order[a:b])
                ends, frees, exits, nexts = [], [], [], []
                for k in ks:
                    frees.append(dict.fromkeys("vatpsdn", 0.0))
                    ends.append(heads(order[:a], k, [0.0] * n, frees[k]))
                    tail, back = [0.0] * n, dict.fromkeys("vatpsdn", 0.0)
                    for i in reversed(order[b:]):
                        tail[i] = back[qs[i]] = max([back[qs[i]], lates[i][k]] + [tail[u] + gap(i, u, qs[i], qs[u], k) for u in users[i]]) + hold[k][i]
                        back["n"] = 0.0
                    exits.append([(i, {q: max([lates[i][k]] + [tail[u] + gap(i, u, q, qs[u], k) for u in users[i] if u not in inside]) for q in holds[i]})
                                  for i in seg if not users[i] or any(u not in inside for u in users[i])])
                    nexts.append(back)

                def rate(seq, j, most):
                    total, last = [], {qs[i]: i for i in seq[:j] if qs[i] != "n"}
                    for k in ks:
                        if sum(total) > most[k]:
                            return None
                        free, end = dict(frees[k]), ends[k]
                        for q, i in last.items():
                            free[q] = end[i]
                        heads(seq[j:], k, end, free)
                        xs = [end[i] + e[qs[i]] for i, e in exits[k]] + [free[q] + nexts[k][q] for q in "vatpsd"]
                        top = max(xs)
                        total.append(WEIGH[k] * (top + SOFT * math.log(sum([math.exp((x - top) / SOFT) for x in xs if x > top - 4 * SOFT]))))
                    return total

                parts = rate(seg, 0, [1e9 for k in ks])
                best = (sum(parts), seg, [qs[i] for i in seg])
                for r0, r1, r2, r3, r4 in rng.random((TRIES, 5)).tolist():
                    j = int(r0 * len(seg))
                    x = seg[j]
                    q, up = qs[x], r4 < 0.5
                    if len(holds[x]) > 1 and r1 < 0.25:
                        qs[x] = "a" if q == "v" else "v"
                        tie(x)
                        new, i = seg, j
                    elif r1 > 1 - DRAG:
                        i = max(0, j - 2 - int(r2 * 30)) if up else min(len(seg) - 1, j + 2 + int(r2 * 30))
                        part, bound = seg[i:j + 1][::-1] if up else seg[j:i + 1], {x}
                        for y in part:
                            if y in bound:
                                bound.update(deps[y] if up else users[y])
                        part = [y for y in part if y not in bound] + [y for y in part if y in bound]
                        new = seg[:i] + part[::-1] + seg[j + 1:] if up else seg[:j] + part + seg[i + 1:]
                    else:
                        step, stop, spots = -1 if up else 1, deps[x] if up else users[x], []
                        i = j + step
                        while 0 <= i < len(seg) and seg[i] not in stop:
                            if qs[seg[i]] == q:
                                spots.append(i)
                            i += step
                        if not spots or q == "n":
                            continue
                        i = spots[int(r2 * r2 * len(spots))]
                        new = seg[:j] + seg[j + 1:]
                        new.insert(i, x)
                    j = min(i, j)
                    keep = [[end[i] for i in new[j:]] for end in ends]
                    more = -heat * math.log(r3 + 1e-12)
                    score = rate(new, j, [sum(parts[:k]) + more + 0.15 for k in ks])
                    if score and sum(score) < sum(parts) + more:
                        parts, seg = score, sorted(new, key=lambda i: ends[0][i] - hold[0][i])
                        if sum(parts) < best[0]:
                            best = (sum(parts), seg, [qs[i] for i in seg])
                        continue
                    for end, was in zip(ends, keep):
                        for i, e in zip(new[j:], was):
                            end[i] = e
                    if qs[x] != q:
                        qs[x] = q
                        tie(x)
                order[a:b] = best[1]
                for i, q in zip(best[1], best[2]):
                    if qs[i] != q:
                        qs[i] = q
                        tie(i)
                a, b = b - WIDTH // 2, b + WIDTH // 2
            end = heads(order, 0, [0.0] * n, dict.fromkeys("vatpsdn", 0.0))
            order[loads:] = sorted(order[loads:], key=lambda i: end[i] - hold[0][i])
        return order, qs

    if not ORDER:
        ORDER.extend(anneal(*min(arrange(*rule) for rule in RULES)[1:]))

    know = {q: {} for q in queue}
    order, qs = ORDER
    for k, i in enumerate(order):
        c, q = calls[i], qs[i]
        c["end"] = k
        if q in "nd":
            c["tok"], c["then"] = c["emit"](q), {}
            continue
        need = {}
        for d in deps[i]:
            tok = calls[d]["tok"]
            if tok and not (qs[d] == q and d in c["turns"]) and need.get(tok[0], (0,))[0] < tok[1]:
                need[tok[0]] = (tok[1], d)
        for sem in sorted(need, key=lambda k: -calls[need[k][1]]["end"]):
            m, d = need[sem]
            if know[q].get(sem, 0) < m:
                queue[q].wait_ge(T.sem[sem], m)
                know[q][sem] = m
                for x, y in calls[d]["then"].items():
                    know[q][x] = max(know[q].get(x, 0), y)
        c["then"] = dict(know[q])
        c["tok"] = c["emit"](q)
    for sem in sorted(count):
        if know["p"].get(sem, 0) < count[sem]:
            g.wait_ge(T.sem[sem], count[sem])
    g.wait_ge(T.sem.ls, sent[0])
